import numpy as np
import ml_dtypes


def mxq(x, axis, fmt="e4m3"):
    dtype, down = {"e4m3": (ml_dtypes.float8_e4m3fn, 7), "e5m2": (ml_dtypes.float8_e5m2, 14)}[fmt]
    v = np.moveaxis(np.asarray(x, np.float32).astype(ml_dtypes.bfloat16).astype(np.float64), axis, -1)
    blocks = v.reshape(v.shape[:-1] + (-1, 32))
    amax = np.abs(blocks).max(-1, keepdims=True)
    byte = np.maximum(np.where(amax > 0, np.frexp(amax)[1] - 1 + 127, 0) - down, 1)
    scale = np.exp2(byte - 127.0)
    codes = (blocks / scale).astype(np.float32).astype(dtype).astype(np.float64)
    return np.moveaxis((codes * scale).reshape(v.shape), -1, axis)


WIDE = False


def mx_kscale(k):
    if not WIDE:
        return np.ones(k)
    levels = np.array([10, -10, 5, -5, 0])
    if k % 512:
        return np.exp2(np.random.permutation(np.resize(levels, k // 32))).repeat(32)
    a = np.empty((k // 512, 16))
    for p in range(k // 512):
        a[p, :8] = np.random.permutation(np.resize(levels, 8))
        for g in range(8):
            far = levels[np.abs(levels - a[p, g]) >= 10]
            a[p, g + 8] = far[np.random.randint(len(far))]
    return np.exp2(a.ravel()).repeat(32)


def f64(x):
    return np.asarray(x).astype(np.float64)


def striped(idx):
    return np.tile(idx.reshape(-1, 16).T, (8, 1)).astype(np.uint16)


def unstriped(offs):
    return offs[:16].T.reshape(-1).astype(np.int64)


def pack_weight(w):
    k, n = w.shape
    w = f64(np.asarray(w, np.float32).astype(ml_dtypes.bfloat16)).reshape(k // 32, 32, n)
    amax = np.abs(w).max(1)
    byte = np.clip(np.where(amax > 0, np.frexp(amax)[1] - 1 + 127 - 7, 1), 1, 254)
    scaled = (w * np.exp2(127.0 - byte)[:, None, :]).reshape(k, n).astype(np.float32)
    words = np.ascontiguousarray(scaled.reshape(k // 512, 128, 4, n).transpose(0, 1, 3, 2)).astype(ml_dtypes.float8_e4m3fn).view(np.uint8)
    return words, np.ascontiguousarray(byte.astype(np.uint8).reshape(k // 512, 16, n))


def unpack_weight(words, scales):
    g, p, n, _ = words.shape
    vals = np.ascontiguousarray(words).view(ml_dtypes.float8_e4m3fn).astype(np.float64) * np.repeat(np.exp2(scales.astype(np.float64) - 127.0), 8, axis=1)[..., None]
    return vals.transpose(0, 1, 3, 2).reshape(g * 512, n)


K, T, E, C, N = 2560, 640, 10, 128, 128


def by_expert(wq, xq):
    return np.concatenate([wq[e].T @ xq[:, e * C:(e + 1) * C] for e in range(E)], axis=1)


def setup_inputs():
    n = np.random.standard_normal
    s = mx_kscale(K)[:, None]
    first = np.random.permutation(np.repeat(np.arange(E), T // E))
    second = (first + 1 + np.random.permutation(np.repeat(np.arange(E - 1), -(-T // (E - 1)))[:T])) % E
    while np.bincount(second, minlength=E).max() != T // E:
        load = np.bincount(second, minlength=E); hi, lo = int(load.argmax()), int(load.argmin())
        t = np.flatnonzero((second == hi) & (first != lo))[0]; second[t] = lo
    slot_token = np.empty(E * C, np.int64); pos = np.empty((2, T), np.int64); fill = np.zeros(E, np.int64)
    place = np.stack([np.random.permutation(C) for _ in range(E)])
    for r, deal in enumerate((first, second)):
        for t in np.random.permutation(T):
            e = deal[t]; j = e * C + place[e, fill[e]]; fill[e] += 1; slot_token[j] = t; pos[r, t] = j
    g = np.random.uniform(0.2, 0.8, T)
    packed = [pack_weight(m) for m in n((E, K, N)) / np.sqrt(K) / s[None]]
    w_slot = np.empty(E * C); w_slot[pos[0]] = g; w_slot[pos[1]] = 1.0 - g
    return {
        "xT": (n((K, T)) * s).astype(np.float32),
        "w_words": np.stack([m[0] for m in packed]),
        "w_scales": np.stack([m[1] for m in packed]),
        "b": (0.3 * n((N, E))).astype(np.float32),
        "gate": np.tile(w_slot, (K, 1)).astype(np.float32),
        "offs": striped(slot_token),
        "pos1": striped(pos[0]),
        "pos2": striped(pos[1]),
    }


def reference(xT, w_words, w_scales, b, gate, offs, pos1, pos2):
    idx = unstriped(offs)
    w = np.stack([unpack_weight(w_words[e], w_scales[e]) for e in range(E)])
    xq = mxq(f64(gate) * f64(xT)[:, idx], 0, "e4m3")
    y = by_expert(w, xq)
    y = y + np.repeat(f64(b), C, axis=1)
    return y[:, unstriped(pos1)] + y[:, unstriped(pos2)]

@@ -1,0 +1,125 @@
+from contextlib import ExitStack
+
+import concourse.mybir as mybir
+
+K, T, E, C, N = 2560, 640, 10, 128, 128
+S = E * C
+FLOPS = 2 * K * S * N
+BYTES = K * T * 4 + E * K * N + E * (K // 32) * N + N * E * 4 + S * 4 + N * T * 4
+
+F32 = mybir.dt.float32
+BF16 = mybir.dt.bfloat16
+I32 = mybir.dt.int32
+U32 = mybir.dt.uint32
+U16 = mybir.dt.uint16
+U8 = mybir.dt.uint8
+FP8X4 = mybir.dt.float8_e4m3fn_x4
+MULT = mybir.AluOpType.mult
+ADD = mybir.AluOpType.add
+IDENTITY = mybir.ActivationFunctionType.Identity
+
+P = 128
+PACK = 4
+K_PASS = P * PACK
+PASSES = K // K_PASS
+PER_COL = 16
+CHUNKS = ((0, 4), (4, 4), (8, 2))
+HALVES = ((0, 320), (320, 320))
+
+
+def tile_moe_pre_lin_bias_kernel(tc, xT, w_words, w_scales, b, gate, offs, pos1, pos2, out):
+    nc = tc.nc
+    with ExitStack() as ctx:
+        keep = ctx.enter_context(tc.tile_pool(name="keep", bufs=1))
+        ring = ctx.enter_context(tc.tile_pool(name="ring", bufs=3))
+        psum = ctx.enter_context(tc.psum_pool(name="psum", bufs=8))
+
+        offs_sb = keep.tile([P, S // PER_COL], U16, name="offs_sb")
+        pos1_sb = keep.tile([P, T // PER_COL], U16, name="pos1_sb")
+        pos2_sb = keep.tile([P, T // PER_COL], U16, name="pos2_sb")
+        w_sc = keep.tile([P, E * PASSES * N], U8, name="w_sc", align_bytes=64)
+        nc.vector.memset(w_sc[:].bitcast(I32), 0)
+
+        nc.sync.dma_start(offs_sb[:], offs)
+        x_rows = xT.rearrange("(a p t) c -> a t p c", p=P, t=PACK)
+        planes = {}
+        gates = []
+
+        def load_plane(a, t):
+            planes[a, t] = keep.tile([P, T], F32, name=f"x_{a}_{t}")
+            nc.sync.dma_start(planes[a, t][:], x_rows[a, t])
+
+        def load_gate(e0, ne):
+            g = keep.tile([P, ne * C], F32, name=f"gate_{e0}")
+            nc.sync.dma_start(g[:], gate[0:P, e0 * C : (e0 + ne) * C])
+            gates.append(g)
+
+        load_plane(0, 0)
+        load_gate(*CHUNKS[0])
+        for i in range(1, PASSES * PACK):
+            load_plane(i // PACK, i % PACK)
+        for ch in CHUNKS[1:]:
+            load_gate(*ch)
+
+        sc_rows = w_scales.rearrange("e a q n -> q (e a) n").bitcast(I32)
+        for q in range(4):
+            nc.sync.dma_start(
+                w_sc[32 * q : 32 * q + 4, :].bitcast(I32).rearrange("p (i n) -> p i n", n=N // 4),
+                sc_rows[4 * q : 4 * q + 4],
+            )
+        w_codes = []
+        for e0, ne in CHUNKS:
+            w = keep.tile([P, ne * PASSES, N * PACK], U8, name=f"w_{e0}", align_bytes=64)
+            nc.sync.dma_start(
+                w[:].bitcast(I32),
+                w_words[e0 : e0 + ne].rearrange("e a p n r -> p (e a) (n r)").bitcast(I32),
+            )
+            w_codes.append(w)
+        bias = keep.tile([P, E], F32, name="bias")
+        nc.sync.dma_start(bias[:], b)
+        nc.sync.dma_start(pos1_sb[:], pos1)
+        nc.sync.dma_start(pos2_sb[:], pos2)
+
+        y = keep.tile([P, S], F32, name="y")
+
+        for ci, (e0, ne) in enumerate(CHUNKS):
+            width = ne * C
+            chunk_offs = offs_sb[:, e0 * C // PER_COL : (e0 + ne) * C // PER_COL]
+            acc = [psum.tile([P, C], F32, name="acc") for e in range(ne)]
+            for a in range(PASSES):
+                gated = ring.tile([P, PACK, width], F32, name="gated")
+                for t in range(PACK):
+                    nc.vector.tensor_tensor(gated[:, t, :], planes[a, t][:].indirect(chunk_offs), gates[ci][:], MULT)
+                woven = ring.tile([P, width, PACK], BF16, name="woven", align_bytes=64)
+                nc.scalar.copy(woven[:], gated[:].rearrange("p t s -> p s t"))
+                codes = keep.tile([P, width], U32, name=f"codes_{ci}_{a}", align_bytes=64)
+                scales = keep.tile([P, width], U8, name=f"scales_{ci}_{a}", align_bytes=64)
+                nc.vector.quantize_mx(
+                    out=codes[:].bitcast(FP8X4),
+                    scales=scales[:],
+                    in_=woven[:].rearrange("p s t -> p (s t)"),
+                )
+                for j in range(ne):
+                    i = (e0 + j) * PASSES + a
+                    nc.tensor.matmul_mx(
+                        out=acc[j][:],
+                        lhsT=w_codes[ci][:, j * PASSES + a, :].bitcast(FP8X4),
+                        lhsT_scale=w_sc[:, i * N : (i + 1) * N],
+                        rhs=codes[:, j * C : (j + 1) * C].bitcast(FP8X4),
+                        rhs_scale=scales[:, j * C : (j + 1) * C],
+                        start=(a == 0),
+                        stop=(a == PASSES - 1),
+                    )
+            for j in range(ne):
+                e = e0 + j
+                nc.scalar.activation(y[:, e * C : (e + 1) * C], acc[j][:], IDENTITY, bias=bias[:, e : e + 1])
+
+        firsts = []
+        for t0, nt in HALVES:
+            first = keep.tile([P, nt], F32, name=f"first_{t0}")
+            nc.vector.tensor_copy(first[:], y[:].indirect(pos1_sb[:, t0 // PER_COL : (t0 + nt) // PER_COL]))
+            firsts.append(first)
+        for (t0, nt), first in zip(HALVES, firsts):
+            total = keep.tile([P, nt], F32, name=f"total_{t0}")
+            nc.vector.tensor_tensor(total[:], y[:].indirect(pos2_sb[:, t0 // PER_COL : (t0 + nt) // PER_COL]), first[:], ADD)
+            nc.sync.dma_start(out[:, t0 : t0 + nt], total[:])

@@ -23,96 +23,151 @@ PACK = 4
 K_PASS = P * PACK
 PASSES = K // K_PASS
 PER_COL = 16
-CHUNKS = ((0, 4), (4, 4), (8, 2))
-HALVES = ((0, 320), (320, 320))
+WINDOW = S + 8
+WINDOWS = 12
+BANKS = 8
+LAG = 2
+GATE_PIECES = ((0, 2), (2, 4), (6, 4))
+STEPS = ((0, 0, 10), (1, 0, 10), (2, 0, 10), (3, 0, 6), (4, 0, 6), (3, 6, 4), (4, 6, 2), (4, 8, 2))
+HALVES = ((0, 448), (448, 192))
+
+
+def power_of_two_runs(e0, ne):
+    runs = []
+    while ne > 0:
+        n = max(m for m in (8, 4, 2, 1) if m <= ne)
+        runs.append((e0, n))
+        e0, ne = e0 + n, ne - n
+    return runs
 
 
 def tile_moe_pre_lin_bias_kernel(tc, xT, w_words, w_scales, b, gate, offs, pos1, pos2, out):
     nc = tc.nc
     with ExitStack() as ctx:
         keep = ctx.enter_context(tc.tile_pool(name="keep", bufs=1))
-        ring = ctx.enter_context(tc.tile_pool(name="ring", bufs=3))
-        psum = ctx.enter_context(tc.psum_pool(name="psum", bufs=8))
+        ring = ctx.enter_context(tc.tile_pool(name="ring", bufs=2))
+        psum = ctx.enter_context(tc.psum_pool(name="psum", bufs=BANKS))
 
         offs_sb = keep.tile([P, S // PER_COL], U16, name="offs_sb")
         pos1_sb = keep.tile([P, T // PER_COL], U16, name="pos1_sb")
         pos2_sb = keep.tile([P, T // PER_COL], U16, name="pos2_sb")
         w_sc = keep.tile([P, E * PASSES * N], U8, name="w_sc", align_bytes=64)
-        nc.vector.memset(w_sc[:].bitcast(I32), 0)
+        windows = [keep.tile([P, WINDOW], F32, name=f"window_{i}") for i in range(WINDOWS)]
+        nc.gpsimd.memset(w_sc[:].bitcast(I32), 0)
 
-        nc.sync.dma_start(offs_sb[:], offs)
         x_rows = xT.rearrange("(a p t) c -> a t p c", p=P, t=PACK)
-        planes = {}
-        gates = []
+        gate_sb = keep.tile([P, S], F32, name="gate_sb")
 
-        def load_plane(a, t):
-            planes[a, t] = keep.tile([P, T], F32, name=f"x_{a}_{t}")
-            nc.sync.dma_start(planes[a, t][:], x_rows[a, t])
+        def load_plane(i):
+            nc.sync.dma_start(windows[i % WINDOWS][:, :T], x_rows[i // PACK, i % PACK])
 
         def load_gate(e0, ne):
-            g = keep.tile([P, ne * C], F32, name=f"gate_{e0}")
-            nc.sync.dma_start(g[:], gate[0:P, e0 * C : (e0 + ne) * C])
-            gates.append(g)
+            nc.sync.dma_start(gate_sb[:, e0 * C : (e0 + ne) * C], gate[0:P, e0 * C : (e0 + ne) * C])
 
-        load_plane(0, 0)
-        load_gate(*CHUNKS[0])
-        for i in range(1, PASSES * PACK):
-            load_plane(i // PACK, i % PACK)
-        for ch in CHUNKS[1:]:
-            load_gate(*ch)
+        nc.sync.dma_start(offs_sb[:], offs)
+        load_gate(*GATE_PIECES[0])
+        load_plane(0)
+        for piece in GATE_PIECES[1:]:
+            load_gate(*piece)
+        for i in range(1, WINDOWS):
+            load_plane(i)
 
-        sc_rows = w_scales.rearrange("e a q n -> q (e a) n").bitcast(I32)
-        for q in range(4):
-            nc.sync.dma_start(
-                w_sc[32 * q : 32 * q + 4, :].bitcast(I32).rearrange("p (i n) -> p i n", n=N // 4),
-                sc_rows[4 * q : 4 * q + 4],
-            )
-        w_codes = []
-        for e0, ne in CHUNKS:
-            w = keep.tile([P, ne * PASSES, N * PACK], U8, name=f"w_{e0}", align_bytes=64)
-            nc.sync.dma_start(
-                w[:].bitcast(I32),
-                w_words[e0 : e0 + ne].rearrange("e a p n r -> p (e a) (n r)").bitcast(I32),
-            )
-            w_codes.append(w)
         bias = keep.tile([P, E], F32, name="bias")
-        nc.sync.dma_start(bias[:], b)
-        nc.sync.dma_start(pos1_sb[:], pos1)
-        nc.sync.dma_start(pos2_sb[:], pos2)
+
+        def load_small():
+            sc_rows = w_scales.rearrange("e a q n -> q (e a) n").bitcast(I32)
+            for q in range(4):
+                nc.sync.dma_start(
+                    w_sc[32 * q : 32 * q + 4, :].bitcast(I32).rearrange("p (i n) -> p i n", n=N // 4),
+                    sc_rows[4 * q : 4 * q + 4],
+                )
+            nc.sync.dma_start(bias[:], b)
+            nc.sync.dma_start(pos1_sb[:], pos1)
+            nc.sync.dma_start(pos2_sb[:], pos2)
+
+        w_codes = {}
+
+        def load_weights(a):
+            w_codes[a] = keep.tile([P, E, N * PACK], U8, name=f"w_{a}", align_bytes=64)
+            nc.sync.dma_start(
+                w_codes[a][:].bitcast(I32),
+                w_words[:, a].rearrange("e p n r -> p e (n r)").bitcast(I32),
+            )
 
         y = keep.tile([P, S], F32, name="y")
+        acc = {}
+        x_codes = {}
 
-        for ci, (e0, ne) in enumerate(CHUNKS):
-            width = ne * C
-            chunk_offs = offs_sb[:, e0 * C // PER_COL : (e0 + ne) * C // PER_COL]
-            acc = [psum.tile([P, C], F32, name="acc") for e in range(ne)]
-            for a in range(PASSES):
-                gated = ring.tile([P, PACK, width], F32, name="gated")
-                for t in range(PACK):
-                    nc.vector.tensor_tensor(gated[:, t, :], planes[a, t][:].indirect(chunk_offs), gates[ci][:], MULT)
-                woven = ring.tile([P, width, PACK], BF16, name="woven", align_bytes=64)
-                nc.scalar.copy(woven[:], gated[:].rearrange("p t s -> p s t"))
-                codes = keep.tile([P, width], U32, name=f"codes_{ci}_{a}", align_bytes=64)
-                scales = keep.tile([P, width], U8, name=f"scales_{ci}_{a}", align_bytes=64)
+        def gather(dst, i, e0, ne):
+            cols = slice(e0 * C // PER_COL, (e0 + ne) * C // PER_COL)
+            nc.vector.tensor_tensor(dst, windows[i % WINDOWS][:].indirect(offs_sb[:, cols]), gate_sb[:, e0 * C : (e0 + ne) * C], MULT)
+
+        def quantise(weave, a, gated, e0, ne):
+            woven = ring.tile([P, ne * C, PACK], BF16, name="woven", bufs=4, align_bytes=64)
+            weave(woven[:].rearrange("p (c i) t -> p c t i", i=4), gated.rearrange("p t (c i) -> p c t i", i=4))
+            for r0, rn in power_of_two_runs(e0, ne):
+                codes = keep.tile([P, rn * C], U32, name=f"codes_{a}_{r0}", align_bytes=64)
+                scales = keep.tile([P, rn * C], U8, name=f"scales_{a}_{r0}", align_bytes=64)
                 nc.vector.quantize_mx(
                     out=codes[:].bitcast(FP8X4),
                     scales=scales[:],
-                    in_=woven[:].rearrange("p s t -> p (s t)"),
+                    in_=woven[:, (r0 - e0) * C : (r0 - e0 + rn) * C, :].rearrange("p s t -> p (s t)"),
                 )
-                for j in range(ne):
-                    i = (e0 + j) * PASSES + a
-                    nc.tensor.matmul_mx(
-                        out=acc[j][:],
-                        lhsT=w_codes[ci][:, j * PASSES + a, :].bitcast(FP8X4),
-                        lhsT_scale=w_sc[:, i * N : (i + 1) * N],
-                        rhs=codes[:, j * C : (j + 1) * C].bitcast(FP8X4),
-                        rhs_scale=scales[:, j * C : (j + 1) * C],
-                        start=(a == 0),
-                        stop=(a == PASSES - 1),
-                    )
-            for j in range(ne):
-                e = e0 + j
-                nc.scalar.activation(y[:, e * C : (e + 1) * C], acc[j][:], IDENTITY, bias=bias[:, e : e + 1])
+                for j in range(rn):
+                    x_codes[a, r0 + j] = (codes[:, j * C : (j + 1) * C], scales[:, j * C : (j + 1) * C])
+
+        def multiply(a, e):
+            if a == 0:
+                acc[e] = psum.tile([P, C], F32, name="acc")
+            i = e * PASSES + a
+            codes, scales = x_codes[a, e]
+            nc.tensor.matmul_mx(
+                out=acc[e][:],
+                lhsT=w_codes[a][:, e, :].bitcast(FP8X4),
+                lhsT_scale=w_sc[:, i * N : (i + 1) * N],
+                rhs=codes.bitcast(FP8X4),
+                rhs_scale=scales,
+                start=(a == 0),
+                stop=(a == PASSES - 1),
+            )
+            if a == PASSES - 1 and e < E - 1:
+                nc.scalar.activation(y[:, e * C : (e + 1) * C], acc[e][:], IDENTITY, bias=bias[:, e : e + 1])
+            elif a == PASSES - 1:
+                nc.vector.tensor_scalar_add(y[:, e * C : (e + 1) * C], acc[e][:], bias[:, e : e + 1])
+
+        def products(n):
+            a, e0, ne = STEPS[n]
+            if n == 0:
+                load_small()
+            if e0 == 0:
+                load_weights(a)
+            first_close = min(m for m, step in enumerate(STEPS) if step[0] == PASSES - 1)
+            for e in range(e0, e0 + ne):
+                if e < BANKS or n > first_close:
+                    multiply(a, e)
+            if n == first_close:
+                for e in range(BANKS, E):
+                    for early, s0, sn in STEPS[:n]:
+                        if s0 <= e < s0 + sn:
+                            multiply(early, e)
+
+        for n, (a, e0, ne) in enumerate(STEPS):
+            gated = ring.tile([P, PACK, ne * C], F32, name="gated", align_bytes=64)
+            for t in range(PACK):
+                i = a * PACK + t
+                for g0, gn in GATE_PIECES if i == 0 else ((e0, ne),):
+                    gather(gated[:, t, (g0 - e0) * C : (g0 - e0 + gn) * C], i, g0, gn)
+                if e0 + ne == E and i + WINDOWS < PASSES * PACK:
+                    load_plane(i + WINDOWS)
+            if n < len(STEPS) - 1:
+                quantise(nc.scalar.copy, a, gated[:], e0, ne)
+            else:
+                quantise(nc.scalar.copy, a, gated[:, :, :C], e0, 1)
+                quantise(nc.vector.tensor_copy, a, gated[:, :, C:], e0 + 1, 1)
+            if n >= LAG:
+                products(n - LAG)
+        for n in range(len(STEPS) - LAG, len(STEPS)):
+            products(n)
 
         firsts = []
         for t0, nt in HALVES:

@@ -5,7 +5,7 @@ import concourse.mybir as mybir
 K, T, E, C, N = 2560, 640, 10, 128, 128
 S = E * C
 FLOPS = 2 * K * S * N
-BYTES = K * T * 4 + E * K * N + E * (K // 32) * N + N * E * 4 + S * 4 + N * T * 4
+BYTES = K * T * 4 + E * K * N + E * (K // 32) * N + N * E * 4 + S * 4 + 128 * (S + 2 * T) // 8 + N * T * 4
 
 F32 = mybir.dt.float32
 BF16 = mybir.dt.bfloat16
@@ -20,49 +20,65 @@ IDENTITY = mybir.ActivationFunctionType.Identity
 
 P = 128
 PACK = 4
-K_PASS = P * PACK
-PASSES = K // K_PASS
-PER_COL = 16
-WINDOW = S + 8
-WINDOWS = 12
+PASSES = K // (P * PACK)
+PLANES = PASSES * PACK
+LAST_PASS = PASSES - 1
+PER_COLUMN = 16
+QUADRANT = 32
+LINE = 4
 BANKS = 8
-LAG = 2
-GATE_PIECES = ((0, 2), (2, 4), (6, 4))
+
+WINDOW_COLUMNS = S + 8
+WINDOWS = 12
+
 STEPS = ((0, 0, 10), (1, 0, 10), (2, 0, 10), (3, 0, 6), (4, 0, 6), (3, 6, 4), (4, 6, 2), (4, 8, 2))
-HALVES = ((0, 448), (448, 192))
+FIRST_CLOSING_STEP = min(n for n, step in enumerate(STEPS) if step[0] == LAST_PASS)
+LAG = 2
+GATED_BUFS = 2
+WOVEN_BUFS = 4
+GATE_PIECES = ((0, 2), (2, 4), (6, 4))
+TOKEN_RUNS = ((0, 448), (448, 192))
 
 
-def power_of_two_runs(e0, ne):
+def power_of_two_runs(first, count):
     runs = []
-    while ne > 0:
-        n = max(m for m in (8, 4, 2, 1) if m <= ne)
-        runs.append((e0, n))
-        e0, ne = e0 + n, ne - n
+    while count > 0:
+        size = max(m for m in (8, 4, 2, 1) if m <= count)
+        runs.append((first, size))
+        first, count = first + size, count - size
     return runs
+
+
+def slots(first, count):
+    return slice(first * C, (first + count) * C)
+
+
+def list_columns(first_entry, count):
+    return slice(first_entry // PER_COLUMN, (first_entry + count) // PER_COLUMN)
 
 
 def tile_moe_pre_lin_bias_kernel(tc, xT, w_words, w_scales, b, gate, offs, pos1, pos2, out):
     nc = tc.nc
     with ExitStack() as ctx:
         keep = ctx.enter_context(tc.tile_pool(name="keep", bufs=1))
-        ring = ctx.enter_context(tc.tile_pool(name="ring", bufs=2))
+        ring = ctx.enter_context(tc.tile_pool(name="ring", bufs=GATED_BUFS))
         psum = ctx.enter_context(tc.psum_pool(name="psum", bufs=BANKS))
 
-        offs_sb = keep.tile([P, S // PER_COL], U16, name="offs_sb")
-        pos1_sb = keep.tile([P, T // PER_COL], U16, name="pos1_sb")
-        pos2_sb = keep.tile([P, T // PER_COL], U16, name="pos2_sb")
-        w_sc = keep.tile([P, E * PASSES * N], U8, name="w_sc", align_bytes=64)
-        windows = [keep.tile([P, WINDOW], F32, name=f"window_{i}") for i in range(WINDOWS)]
-        nc.gpsimd.memset(w_sc[:].bitcast(I32), 0)
+        offs_sb = keep.tile([P, S // PER_COLUMN], U16, name="offs_sb")
+        pos1_sb = keep.tile([P, T // PER_COLUMN], U16, name="pos1_sb")
+        pos2_sb = keep.tile([P, T // PER_COLUMN], U16, name="pos2_sb")
+        w_scale_sb = keep.tile([P, E * PASSES * N], U8, name="w_scale_sb", align_bytes=64)
+        windows = [keep.tile([P, WINDOW_COLUMNS], F32, name=f"window_{i}") for i in range(WINDOWS)]
+        nc.gpsimd.memset(w_scale_sb[:].bitcast(I32), 0)
 
-        x_rows = xT.rearrange("(a p t) c -> a t p c", p=P, t=PACK)
+        x_planes = xT.rearrange("(a p t) c -> a t p c", p=P, t=PACK)
         gate_sb = keep.tile([P, S], F32, name="gate_sb")
 
         def load_plane(i):
-            nc.sync.dma_start(windows[i % WINDOWS][:, :T], x_rows[i // PACK, i % PACK])
+            nc.sync.dma_start(windows[i % WINDOWS][:, :T], x_planes[i // PACK, i % PACK])
 
-        def load_gate(e0, ne):
-            nc.sync.dma_start(gate_sb[:, e0 * C : (e0 + ne) * C], gate[0:P, e0 * C : (e0 + ne) * C])
+        def load_gate(first, count):
+            nc.sync.dma_start(gate_sb[:, slots(first, count)], gate[0:P, slots(first, count)])
 
         nc.sync.dma_start(offs_sb[:], offs)
         load_gate(*GATE_PIECES[0])
@@ -74,12 +90,12 @@ def tile_moe_pre_lin_bias_kernel(tc, xT, w_words, w_scales, b, gate, offs, pos1,
 
         bias = keep.tile([P, E], F32, name="bias")
 
-        def load_small():
-            sc_rows = w_scales.rearrange("e a q n -> q (e a) n").bitcast(I32)
-            for q in range(4):
+        def load_scales_bias_positions():
+            rows = w_scales.rearrange("e a q n -> q (e a) n").bitcast(I32)
+            for quadrant in range(P // QUADRANT):
                 nc.sync.dma_start(
-                    w_sc[32 * q : 32 * q + 4, :].bitcast(I32).rearrange("p (i n) -> p i n", n=N // 4),
-                    sc_rows[4 * q : 4 * q + 4],
+                    w_scale_sb[QUADRANT * quadrant : QUADRANT * quadrant + 4, :].bitcast(I32).rearrange("p (i n) -> p i n", n=N // 4),
+                    rows[4 * quadrant : 4 * quadrant + 4],
                 )
             nc.sync.dma_start(bias[:], b)
             nc.sync.dma_start(pos1_sb[:], pos1)
@@ -96,85 +112,84 @@ def tile_moe_pre_lin_bias_kernel(tc, xT, w_words, w_scales, b, gate, offs, pos1,
 
         y = keep.tile([P, S], F32, name="y")
         acc = {}
-        x_codes = {}
+        x_mx = {}
 
-        def gather(dst, i, e0, ne):
-            cols = slice(e0 * C // PER_COL, (e0 + ne) * C // PER_COL)
-            nc.vector.tensor_tensor(dst, windows[i % WINDOWS][:].indirect(offs_sb[:, cols]), gate_sb[:, e0 * C : (e0 + ne) * C], MULT)
+        def gather_times_gate(dst, i, first, count):
+            window = windows[i % WINDOWS][:].indirect(offs_sb[:, list_columns(first * C, count * C)])
+            nc.vector.tensor_tensor(dst, window, gate_sb[:, slots(first, count)], MULT)
 
-        def quantise(weave, a, gated, e0, ne):
-            woven = ring.tile([P, ne * C, PACK], BF16, name="woven", bufs=4, align_bytes=64)
-            weave(woven[:].rearrange("p (c i) t -> p c t i", i=4), gated.rearrange("p t (c i) -> p c t i", i=4))
-            for r0, rn in power_of_two_runs(e0, ne):
-                codes = keep.tile([P, rn * C], U32, name=f"codes_{a}_{r0}", align_bytes=64)
-                scales = keep.tile([P, rn * C], U8, name=f"scales_{a}_{r0}", align_bytes=64)
+        def weave_and_quantise(copy, a, gated, first, count):
+            woven = ring.tile([P, count * C, PACK], BF16, name="woven", bufs=WOVEN_BUFS, align_bytes=64)
+            copy(woven[:], gated.rearrange("p t s -> p s t"))
+            for run_first, size in power_of_two_runs(first, count):
+                codes = keep.tile([P, size * C], U32, name=f"codes_{a}_{run_first}", align_bytes=64)
+                scales = keep.tile([P, size * C], U8, name=f"scales_{a}_{run_first}", align_bytes=64)
                 nc.vector.quantize_mx(
                     out=codes[:].bitcast(FP8X4),
                     scales=scales[:],
-                    in_=woven[:, (r0 - e0) * C : (r0 - e0 + rn) * C, :].rearrange("p s t -> p (s t)"),
+                    in_=woven[:, slots(run_first - first, size), :].rearrange("p s t -> p (s t)"),
                 )
-                for j in range(rn):
-                    x_codes[a, r0 + j] = (codes[:, j * C : (j + 1) * C], scales[:, j * C : (j + 1) * C])
+                for j in range(size):
+                    x_mx[a, run_first + j] = (codes[:, slots(j, 1)], scales[:, slots(j, 1)])
 
         def multiply(a, e):
             if a == 0:
                 acc[e] = psum.tile([P, C], F32, name="acc")
-            i = e * PASSES + a
-            codes, scales = x_codes[a, e]
+            codes, scales = x_mx[a, e]
+            scale_column = (e * PASSES + a) * N
             nc.tensor.matmul_mx(
                 out=acc[e][:],
                 lhsT=w_codes[a][:, e, :].bitcast(FP8X4),
-                lhsT_scale=w_sc[:, i * N : (i + 1) * N],
+                lhsT_scale=w_scale_sb[:, scale_column : scale_column + N],
                 rhs=codes.bitcast(FP8X4),
                 rhs_scale=scales,
                 start=(a == 0),
-                stop=(a == PASSES - 1),
+                stop=(a == LAST_PASS),
             )
-            if a == PASSES - 1 and e < E - 1:
-                nc.scalar.activation(y[:, e * C : (e + 1) * C], acc[e][:], IDENTITY, bias=bias[:, e : e + 1])
-            elif a == PASSES - 1:
-                nc.vector.tensor_scalar_add(y[:, e * C : (e + 1) * C], acc[e][:], bias[:, e : e + 1])
+            if a == LAST_PASS and e < E - 1:
+                nc.scalar.activation(y[:, slots(e, 1)], acc[e][:], IDENTITY, bias=bias[:, e : e + 1])
+            elif a == LAST_PASS:
+                nc.vector.tensor_scalar_add(y[:, slots(e, 1)], acc[e][:], bias[:, e : e + 1])
 
         def products(n):
-            a, e0, ne = STEPS[n]
+            a, first, count = STEPS[n]
             if n == 0:
-                load_small()
-            if e0 == 0:
+                load_scales_bias_positions()
+            if first == 0:
                 load_weights(a)
-            first_close = min(m for m, step in enumerate(STEPS) if step[0] == PASSES - 1)
-            for e in range(e0, e0 + ne):
-                if e < BANKS or n > first_close:
+            for e in range(first, first + count):
+                if e < BANKS or n > FIRST_CLOSING_STEP:
                     multiply(a, e)
-            if n == first_close:
+            if n == FIRST_CLOSING_STEP:
                 for e in range(BANKS, E):
-                    for early, s0, sn in STEPS[:n]:
-                        if s0 <= e < s0 + sn:
-                            multiply(early, e)
+                    for missed, missed_first, missed_count in STEPS[:n]:
+                        if missed_first <= e < missed_first + missed_count:
+                            multiply(missed, e)
 
-        for n, (a, e0, ne) in enumerate(STEPS):
-            gated = ring.tile([P, PACK, ne * C], F32, name="gated", align_bytes=64)
+        for n, (a, first, count) in enumerate(STEPS):
+            gated = ring.tile([P, PACK, count * C], F32, name="gated", align_bytes=64)
             for t in range(PACK):
                 i = a * PACK + t
-                for g0, gn in GATE_PIECES if i == 0 else ((e0, ne),):
-                    gather(gated[:, t, (g0 - e0) * C : (g0 - e0 + gn) * C], i, g0, gn)
-                if e0 + ne == E and i + WINDOWS < PASSES * PACK:
+                for piece_first, piece_count in GATE_PIECES if i == 0 else ((first, count),):
+                    gather_times_gate(gated[:, t, slots(piece_first - first, piece_count)], i, piece_first, piece_count)
+                if first + count == E and i + WINDOWS < PLANES:
                     load_plane(i + WINDOWS)
             if n < len(STEPS) - 1:
-                quantise(nc.scalar.copy, a, gated[:], e0, ne)
+                weave_and_quantise(nc.scalar.copy, a, gated[:], first, count)
             else:
-                quantise(nc.scalar.copy, a, gated[:, :, :C], e0, 1)
-                quantise(nc.vector.tensor_copy, a, gated[:, :, C:], e0 + 1, 1)
+                weave_and_quantise(nc.scalar.copy, a, gated[:, :, :C], first, 1)
+                weave_and_quantise(nc.vector.tensor_copy, a, gated[:, :, C:], first + 1, 1)
             if n >= LAG:
                 products(n - LAG)
         for n in range(len(STEPS) - LAG, len(STEPS)):
             products(n)
 
-        firsts = []
-        for t0, nt in HALVES:
-            first = keep.tile([P, nt], F32, name=f"first_{t0}")
-            nc.vector.tensor_copy(first[:], y[:].indirect(pos1_sb[:, t0 // PER_COL : (t0 + nt) // PER_COL]))
-            firsts.append(first)
-        for (t0, nt), first in zip(HALVES, firsts):
-            total = keep.tile([P, nt], F32, name=f"total_{t0}")
-            nc.vector.tensor_tensor(total[:], y[:].indirect(pos2_sb[:, t0 // PER_COL : (t0 + nt) // PER_COL]), first[:], ADD)
-            nc.sync.dma_start(out[:, t0 : t0 + nt], total[:])
+        picked = []
+        for t0, count in TOKEN_RUNS:
+            y_p1 = keep.tile([P, count], F32, name=f"y_p1_{t0}")
+            nc.vector.tensor_copy(y_p1[:], y[:].indirect(pos1_sb[:, list_columns(t0, count)]))
+            picked.append(y_p1)
+        for (t0, count), y_p1 in zip(TOKEN_RUNS, picked):
+            total = keep.tile([P, count], F32, name=f"total_{t0}")
+            nc.vector.tensor_tensor(total[:], y[:].indirect(pos2_sb[:, list_columns(t0, count)]), y_p1[:], ADD)
+            nc.sync.dma_start(out[:, t0 : t0 + count], total[:])

@@ -34,8 +34,8 @@ WINDOWS = 12
 STEPS = ((0, 0, 10), (1, 0, 10), (2, 0, 10), (3, 0, 6), (4, 0, 6), (3, 6, 4), (4, 6, 2), (4, 8, 2))
 FIRST_CLOSING_STEP = min(n for n, step in enumerate(STEPS) if step[0] == LAST_PASS)
 LAG = 2
-GATED_BUFS = 2
-WOVEN_BUFS = 4
+GATED_BUFS = 3
+WOVEN_BUFS = 3
 GATE_PIECES = ((0, 2), (2, 4), (6, 4))
 TOKEN_RUNS = ((0, 448), (448, 192))
 
@@ -120,7 +120,7 @@ def tile_moe_pre_lin_bias_kernel(tc, xT, w_words, w_scales, b, gate, offs, pos1,
 
         def weave_and_quantise(copy, a, gated, first, count):
             woven = ring.tile([P, count * C, PACK], BF16, name="woven", bufs=WOVEN_BUFS, align_bytes=64)
-            copy(woven[:], gated.rearrange("p t s -> p s t"))
+            copy(woven[:].rearrange("p (c i) t -> p c t i", i=LINE), gated.rearrange("p t (c i) -> p c t i", i=LINE))
             for run_first, size in power_of_two_runs(first, count):
                 codes = keep.tile([P, size * C], U32, name=f"codes_{a}_{run_first}", align_bytes=64)
                 scales = keep.tile([P, size * C], U8, name=f"scales_{a}_{run_first}", align_bytes=64)

@@ -17,6 +17,7 @@ FP8X4 = mybir.dt.float8_e4m3fn_x4
 MULT = mybir.AluOpType.mult
 ADD = mybir.AluOpType.add
 IDENTITY = mybir.ActivationFunctionType.Identity
+COPY = mybir.ActivationFunctionType.Copy
 
 P = 128
 PACK = 4
@@ -25,28 +26,16 @@ PLANES = PASSES * PACK
 LAST_PASS = PASSES - 1
 PER_COLUMN = 16
 QUADRANT = 32
-LINE = 4
-BANKS = 8
+RUN = 2
 
-WINDOW_COLUMNS = S + 8
-WINDOWS = 12
-
-STEPS = ((0, 0, 10), (1, 0, 10), (2, 0, 10), (3, 0, 6), (4, 0, 6), (3, 6, 4), (4, 6, 2), (4, 8, 2))
-FIRST_CLOSING_STEP = min(n for n, step in enumerate(STEPS) if step[0] == LAST_PASS)
-LAG = 2
-GATED_BUFS = 3
-WOVEN_BUFS = 3
-GATE_PIECES = ((0, 2), (2, 4), (6, 4))
-TOKEN_RUNS = ((0, 448), (448, 192))
-
-
-def power_of_two_runs(first, count):
-    runs = []
-    while count > 0:
-        size = max(m for m in (8, 4, 2, 1) if m <= count)
-        runs.append((first, size))
-        first, count = first + size, count - size
-    return runs
+FED = 8
+OWN = E - FED
+WINDOW_COLUMNS = FED * C + 8
+CHUNKS = ((0, 0, 8), (1, 0, 8), (2, 0, 8), (3, 0, 4), (3, 4, 4), (4, 0, 4), (4, 4, 2), (4, 6, 1), (4, 7, 1))
+LEAD = 3
+RAW_BUFS = 3
+TOKEN_RUN = 160
+BANK_OF = (0, 0, 1, 1, 2, 3, 4, 5, 6, 6)
 
 
 def slots(first, count):
@@ -61,135 +50,129 @@ def tile_moe_pre_lin_bias_kernel(tc, xT, w_words, w_scales, b, gate, offs, pos1,
     nc = tc.nc
     with ExitStack() as ctx:
         keep = ctx.enter_context(tc.tile_pool(name="keep", bufs=1))
-        ring = ctx.enter_context(tc.tile_pool(name="ring", bufs=GATED_BUFS))
-        psum = ctx.enter_context(tc.psum_pool(name="psum", bufs=BANKS))
+        psum = ctx.enter_context(tc.psum_pool(name="psum", bufs=1))
 
         offs_sb = keep.tile([P, S // PER_COLUMN], U16, name="offs_sb")
         pos1_sb = keep.tile([P, T // PER_COLUMN], U16, name="pos1_sb")
         pos2_sb = keep.tile([P, T // PER_COLUMN], U16, name="pos2_sb")
         w_scale_sb = keep.tile([P, E * PASSES * N], U8, name="w_scale_sb", align_bytes=64)
-        windows = [keep.tile([P, WINDOW_COLUMNS], F32, name=f"window_{i}") for i in range(WINDOWS)]
+        windows = [keep.tile([P, WINDOW_COLUMNS], F32, name=f"window_{i}") for i in range(PLANES)]
         nc.gpsimd.memset(w_scale_sb[:].bitcast(I32), 0)
 
         x_planes = xT.rearrange("(a p t) c -> a t p c", p=P, t=PACK)
-        gate_sb = keep.tile([P, S], F32, name="gate_sb")
+        gate_own = keep.tile([P, OWN * C], F32, name="gate_own")
+        gate_fed = keep.tile([P, FED * C], F32, name="gate_fed")
 
         def load_plane(i):
-            nc.sync.dma_start(windows[i % WINDOWS][:, :T], x_planes[i // PACK, i % PACK])
-
-        def load_gate(first, count):
-            nc.sync.dma_start(gate_sb[:, slots(first, count)], gate[0:P, slots(first, count)])
+            nc.sync.dma_start(windows[i][:, :T], x_planes[i // PACK, i % PACK])
 
         nc.sync.dma_start(offs_sb[:], offs)
-        load_gate(*GATE_PIECES[0])
         load_plane(0)
-        for piece in GATE_PIECES[1:]:
-            load_gate(*piece)
-        for i in range(1, WINDOWS):
+        nc.sync.dma_start(gate_own[:], gate[0:P, slots(FED, OWN)])
+        for i in range(1, LEAD * PACK):
+            load_plane(i)
+        nc.sync.dma_start(gate_fed[:], gate[0:P, slots(0, FED)])
+        for i in range(LEAD * PACK, PLANES):
             load_plane(i)
 
         bias = keep.tile([P, E], F32, name="bias")
-
-        def load_scales_bias_positions():
-            rows = w_scales.rearrange("e a q n -> q (e a) n").bitcast(I32)
-            for quadrant in range(P // QUADRANT):
-                nc.sync.dma_start(
-                    w_scale_sb[QUADRANT * quadrant : QUADRANT * quadrant + 4, :].bitcast(I32).rearrange("p (i n) -> p i n", n=N // 4),
-                    rows[4 * quadrant : 4 * quadrant + 4],
-                )
-            nc.sync.dma_start(bias[:], b)
-            nc.sync.dma_start(pos1_sb[:], pos1)
-            nc.sync.dma_start(pos2_sb[:], pos2)
-
-        w_codes = {}
-
-        def load_weights(a):
-            w_codes[a] = keep.tile([P, E, N * PACK], U8, name=f"w_{a}", align_bytes=64)
+        rows = w_scales.rearrange("e a q n -> q (e a) n").bitcast(I32)
+        for quadrant in range(P // QUADRANT):
             nc.sync.dma_start(
-                w_codes[a][:].bitcast(I32),
-                w_words[:, a].rearrange("e p n r -> p e (n r)").bitcast(I32),
+                w_scale_sb[QUADRANT * quadrant : QUADRANT * quadrant + 4, :].bitcast(I32).rearrange("p (i n) -> p i n", n=N // 4),
+                rows[4 * quadrant : 4 * quadrant + 4],
             )
+        nc.sync.dma_start(bias[:], b)
+        nc.sync.dma_start(pos1_sb[:], pos1)
+        nc.sync.dma_start(pos2_sb[:], pos2)
+        w_codes = []
+        for a in range(PASSES):
+            w_a = keep.tile([P, E, N * PACK], U8, name=f"w_{a}", align_bytes=64)
+            nc.sync.dma_start(w_a[:].bitcast(I32), w_words[:, a].rearrange("e p n r -> p e (n r)").bitcast(I32))
+            w_codes.append(w_a)
 
         y = keep.tile([P, S], F32, name="y")
-        acc = {}
-        x_mx = {}
+        banks = [psum.tile([P, BANK_OF.count(i) * C], F32, name=f"bank_{i}") for i in range(max(BANK_OF) + 1)]
+        raw = [keep.tile([P, PACK * FED * C], F32, name=f"raw_{i}", align_bytes=64) for i in range(RAW_BUFS)]
+        gated = [keep.tile([P, PACK * OWN * C], F32, name=f"gated_{i}", align_bytes=64) for i in range(2)]
+        woven = [keep.tile([P, PACK * FED * C], BF16, name=f"woven_{i}", align_bytes=64) for i in range(2)]
 
-        def gather_times_gate(dst, i, first, count):
-            window = windows[i % WINDOWS][:].indirect(offs_sb[:, list_columns(first * C, count * C)])
-            nc.vector.tensor_tensor(dst, window, gate_sb[:, slots(first, count)], MULT)
+        def window(a, t, first, count):
+            return windows[a * PACK + t][:].indirect(offs_sb[:, list_columns(first * C, count * C)])
 
-        def weave_and_quantise(copy, a, gated, first, count):
-            woven = ring.tile([P, count * C, PACK], BF16, name="woven", bufs=WOVEN_BUFS, align_bytes=64)
-            copy(woven[:].rearrange("p (c i) t -> p c t i", i=LINE), gated.rearrange("p t (c i) -> p c t i", i=LINE))
-            for run_first, size in power_of_two_runs(first, count):
-                codes = keep.tile([P, size * C], U32, name=f"codes_{a}_{run_first}", align_bytes=64)
-                scales = keep.tile([P, size * C], U8, name=f"scales_{a}_{run_first}", align_bytes=64)
-                nc.vector.quantize_mx(
-                    out=codes[:].bitcast(FP8X4),
-                    scales=scales[:],
-                    in_=woven[:, slots(run_first - first, size), :].rearrange("p s t -> p (s t)"),
+        def by_plane(flat):
+            return flat.rearrange("p (t c i) -> p c t i", t=PACK, i=RUN)
+
+        def by_slot(flat):
+            return flat.rearrange("p (c i t) -> p c t i", t=PACK, i=RUN)
+
+        def quantise_and_multiply(a, first, count, rounded):
+            codes = keep.tile([P, count * C], U32, name=f"codes_{a}_{first}", align_bytes=64)
+            scales = keep.tile([P, count * C], U8, name=f"scales_{a}_{first}", align_bytes=64)
+            nc.vector.quantize_mx(out=codes[:].bitcast(FP8X4), scales=scales[:], in_=rounded)
+            for j in range(count):
+                e = first + j
+                place = e - BANK_OF.index(BANK_OF[e])
+                closes = place == BANK_OF.count(BANK_OF[e]) - 1
+                scale_column = (e * PASSES + a) * N
+                nc.tensor.matmul_mx(
+                    out=banks[BANK_OF[e]][:, slots(place, 1)],
+                    lhsT=w_codes[a][:, e, :].bitcast(FP8X4),
+                    lhsT_scale=w_scale_sb[:, scale_column : scale_column + N],
+                    rhs=codes[:, slots(j, 1)].bitcast(FP8X4),
+                    rhs_scale=scales[:, slots(j, 1)],
+                    start=(a == 0 and place == 0),
+                    stop=(a == LAST_PASS and closes),
                 )
-                for j in range(size):
-                    x_mx[a, run_first + j] = (codes[:, slots(j, 1)], scales[:, slots(j, 1)])
+            if a == LAST_PASS:
+                for e in range(first, first + count):
+                    sums = banks[BANK_OF[e]][:, slots(e - BANK_OF.index(BANK_OF[e]), 1)]
+                    if e == FED - 1:
+                        nc.vector.tensor_scalar_add(y[:, slots(e, 1)], sums, bias[:, e : e + 1])
+                    else:
+                        nc.scalar.activation(y[:, slots(e, 1)], sums, IDENTITY, bias=bias[:, e : e + 1])
 
-        def multiply(a, e):
-            if a == 0:
-                acc[e] = psum.tile([P, C], F32, name="acc")
-            codes, scales = x_mx[a, e]
-            scale_column = (e * PASSES + a) * N
-            nc.tensor.matmul_mx(
-                out=acc[e][:],
-                lhsT=w_codes[a][:, e, :].bitcast(FP8X4),
-                lhsT_scale=w_scale_sb[:, scale_column : scale_column + N],
-                rhs=codes.bitcast(FP8X4),
-                rhs_scale=scales,
-                start=(a == 0),
-                stop=(a == LAST_PASS),
-            )
-            if a == LAST_PASS and e < E - 1:
-                nc.scalar.activation(y[:, slots(e, 1)], acc[e][:], IDENTITY, bias=bias[:, e : e + 1])
-            elif a == LAST_PASS:
-                nc.vector.tensor_scalar_add(y[:, slots(e, 1)], acc[e][:], bias[:, e : e + 1])
-
-        def products(n):
-            a, first, count = STEPS[n]
-            if n == 0:
-                load_scales_bias_positions()
-            if first == 0:
-                load_weights(a)
-            for e in range(first, first + count):
-                if e < BANKS or n > FIRST_CLOSING_STEP:
-                    multiply(a, e)
-            if n == FIRST_CLOSING_STEP:
-                for e in range(BANKS, E):
-                    for missed, missed_first, missed_count in STEPS[:n]:
-                        if missed_first <= e < missed_first + missed_count:
-                            multiply(missed, e)
-
-        for n, (a, first, count) in enumerate(STEPS):
-            gated = ring.tile([P, PACK, count * C], F32, name="gated", align_bytes=64)
+        def own_step(a, rounded):
+            values = gated[a % 2]
             for t in range(PACK):
-                i = a * PACK + t
-                for piece_first, piece_count in GATE_PIECES if i == 0 else ((first, count),):
-                    gather_times_gate(gated[:, t, slots(piece_first - first, piece_count)], i, piece_first, piece_count)
-                if first + count == E and i + WINDOWS < PLANES:
-                    load_plane(i + WINDOWS)
-            if n < len(STEPS) - 1:
-                weave_and_quantise(nc.scalar.copy, a, gated[:], first, count)
-            else:
-                weave_and_quantise(nc.scalar.copy, a, gated[:, :, :C], first, 1)
-                weave_and_quantise(nc.vector.tensor_copy, a, gated[:, :, C:], first + 1, 1)
-            if n >= LAG:
-                products(n - LAG)
-        for n in range(len(STEPS) - LAG, len(STEPS)):
-            products(n)
+                nc.vector.tensor_tensor(values[:, slots(t * OWN, OWN)], window(a, t, FED, OWN), gate_own[:], MULT)
+            rounded = rounded[:, : PACK * OWN * C]
+            nc.vector.tensor_copy(by_slot(rounded), by_plane(values[:]))
+            quantise_and_multiply(a, FED, OWN, rounded)
 
-        picked = []
-        for t0, count in TOKEN_RUNS:
-            y_p1 = keep.tile([P, count], F32, name=f"y_p1_{t0}")
-            nc.vector.tensor_copy(y_p1[:], y[:].indirect(pos1_sb[:, list_columns(t0, count)]))
-            picked.append(y_p1)
-        for (t0, count), y_p1 in zip(TOKEN_RUNS, picked):
-            total = keep.tile([P, count], F32, name=f"total_{t0}")
-            nc.vector.tensor_tensor(total[:], y[:].indirect(pos2_sb[:, list_columns(t0, count)]), y_p1[:], ADD)
-            nc.sync.dma_start(out[:, t0 : t0 + count], total[:])
+        def chunk_values(a, first, count):
+            return raw[a % RAW_BUFS][:, slots(PACK * first, PACK * count)]
+
+        def gather_chunk(a, first, count):
+            values = chunk_values(a, first, count)
+            for t in range(PACK):
+                nc.scalar.activation(values[:, slots(t * count, count)], window(a, t, first, count), COPY)
+
+        def fed_step(a, first, count, rounded):
+            rounded = rounded[:, : PACK * count * C]
+            pairs = count * C // RUN
+            weight = gate_fed[:, slots(first, count)].rearrange("p (c i) -> p c i", i=RUN).unsqueeze(2).to_broadcast([P, pairs, PACK, RUN])
+            nc.vector.tensor_tensor(by_slot(rounded), by_plane(chunk_values(a, first, count)), weight, MULT)
+            quantise_and_multiply(a, first, count, rounded)
+
+        steps = [("own", a) for a in range(LEAD)]
+        for n in range(len(CHUNKS)):
+            steps.append(("fed", n))
+            if LEAD + n < PASSES:
+                steps.append(("own", LEAD + n))
+        for place, (kind, n) in enumerate(steps):
+            if kind == "own":
+                own_step(n, woven[place % 2])
+            else:
+                gather_chunk(*CHUNKS[n])
+                fed_step(*CHUNKS[n], woven[place % 2])
+
+        picked = keep.tile([P, T], F32, name="picked")
+        total = keep.tile([P, T], F32, name="total")
+        for t0 in range(0, T, TOKEN_RUN):
+            run = slice(t0, t0 + TOKEN_RUN)
+            nc.scalar.activation(picked[:, run], y[:].indirect(pos1_sb[:, list_columns(t0, TOKEN_RUN)]), COPY)
+            nc.vector.tensor_tensor(total[:, run], y[:].indirect(pos2_sb[:, list_columns(t0, TOKEN_RUN)]), picked[:, run], ADD)
+            if t0 == 2 * TOKEN_RUN:
+                nc.sync.dma_start(out[:, : 3 * TOKEN_RUN], total[:, : 3 * TOKEN_RUN])
+        nc.sync.dma_start(out[:, 3 * TOKEN_RUN :], total[:, 3 * TOKEN_RUN :])

@@ -28,14 +28,30 @@ PER_COLUMN = 16
 QUADRANT = 32
 RUN = 2
 
-FED = 8
-OWN = E - FED
-WINDOW_COLUMNS = FED * C + 8
-CHUNKS = ((0, 0, 8), (1, 0, 8), (2, 0, 8), (3, 0, 4), (3, 4, 4), (4, 0, 4), (4, 4, 2), (4, 6, 1), (4, 7, 1))
-LEAD = 3
-RAW_BUFS = 3
+OWN = 6
+OWN_PASSES = 2
+CHUNKS = ((0, 6, 4), (1, 6, 4), (2, 0, 5), (2, 5, 5), (3, 0, 5), (3, 5, 5), (4, 0, 4), (4, 4, 3), (4, 7, 2), (4, 9, 1))
+WIDEST = max(count for a, first, count in CHUNKS)
+RAW_BUFS = 4
+WOVEN_BUFS = 3
+GATE_PIECES = ((0, 2), (2, 4), (6, 4))
 TOKEN_RUN = 160
-BANK_OF = (0, 0, 1, 1, 2, 3, 4, 5, 6, 6)
+BANK_OF = (0, 0, 1, 1, 2, 3, 4, 5, 6, 7)
+QUANTISE_RUNS = (8, 4, 3, 2, 1)
+
+
+def quantise_runs(first, count):
+    runs = []
+    while count > 0:
+        size = max(m for m in QUANTISE_RUNS if m <= count)
+        runs.append((first, size))
+        first, count = first + size, count - size
+    return runs
+
+
+def window_columns(a):
+    widest = max([count for b, first, count in CHUNKS if b == a] + [OWN if a < OWN_PASSES else 0])
+    return max(T, widest * C + 8)
 
 
 def slots(first, count):
@@ -56,23 +72,26 @@ def tile_moe_pre_lin_bias_kernel(tc, xT, w_words, w_scales, b, gate, offs, pos1,
         pos1_sb = keep.tile([P, T // PER_COLUMN], U16, name="pos1_sb")
         pos2_sb = keep.tile([P, T // PER_COLUMN], U16, name="pos2_sb")
         w_scale_sb = keep.tile([P, E * PASSES * N], U8, name="w_scale_sb", align_bytes=64)
-        windows = [keep.tile([P, WINDOW_COLUMNS], F32, name=f"window_{i}") for i in range(PLANES)]
+        windows = [keep.tile([P, window_columns(i // PACK)], F32, name=f"window_{i}") for i in range(PLANES)]
         nc.gpsimd.memset(w_scale_sb[:].bitcast(I32), 0)
 
         x_planes = xT.rearrange("(a p t) c -> a t p c", p=P, t=PACK)
-        gate_own = keep.tile([P, OWN * C], F32, name="gate_own")
-        gate_fed = keep.tile([P, FED * C], F32, name="gate_fed")
+        gate_sb = keep.tile([P, S], F32, name="gate_sb")
 
         def load_plane(i):
             nc.sync.dma_start(windows[i][:, :T], x_planes[i // PACK, i % PACK])
 
+        def load_gate(first, count):
+            nc.sync.dma_start(gate_sb[:, slots(first, count)], gate[0:P, slots(first, count)])
+
         nc.sync.dma_start(offs_sb[:], offs)
         load_plane(0)
-        nc.sync.dma_start(gate_own[:], gate[0:P, slots(FED, OWN)])
-        for i in range(1, LEAD * PACK):
+        load_gate(*GATE_PIECES[0])
+        load_gate(*GATE_PIECES[1])
+        for i in range(1, PACK):
             load_plane(i)
-        nc.sync.dma_start(gate_fed[:], gate[0:P, slots(0, FED)])
-        for i in range(LEAD * PACK, PLANES):
+        load_gate(*GATE_PIECES[2])
+        for i in range(PACK, PLANES):
             load_plane(i)
 
         bias = keep.tile([P, E], F32, name="bias")
@@ -93,9 +112,9 @@ def tile_moe_pre_lin_bias_kernel(tc, xT, w_words, w_scales, b, gate, offs, pos1,
 
         y = keep.tile([P, S], F32, name="y")
         banks = [psum.tile([P, BANK_OF.count(i) * C], F32, name=f"bank_{i}") for i in range(max(BANK_OF) + 1)]
-        raw = [keep.tile([P, PACK * FED * C], F32, name=f"raw_{i}", align_bytes=64) for i in range(RAW_BUFS)]
-        gated = [keep.tile([P, PACK * OWN * C], F32, name=f"gated_{i}", align_bytes=64) for i in range(2)]
-        woven = [keep.tile([P, PACK * FED * C], BF16, name=f"woven_{i}", align_bytes=64) for i in range(2)]
+        raw = [keep.tile([P, PACK * WIDEST * C], F32, name=f"raw_{i}", align_bytes=64) for i in range(RAW_BUFS)]
+        gated = [keep.tile([P, PACK * OWN * C], F32, name=f"gated_{i}", align_bytes=64) for i in range(OWN_PASSES)]
+        woven = [keep.tile([P, PACK * max(OWN, WIDEST) * C], BF16, name=f"woven_{i}", align_bytes=64) for i in range(WOVEN_BUFS)]
 
         def window(a, t, first, count):
             return windows[a * PACK + t][:].indirect(offs_sb[:, list_columns(first * C, count * C)])
@@ -107,65 +126,70 @@ def tile_moe_pre_lin_bias_kernel(tc, xT, w_words, w_scales, b, gate, offs, pos1,
             return flat.rearrange("p (c i t) -> p c t i", t=PACK, i=RUN)
 
         def quantise_and_multiply(a, first, count, rounded):
-            codes = keep.tile([P, count * C], U32, name=f"codes_{a}_{first}", align_bytes=64)
-            scales = keep.tile([P, count * C], U8, name=f"scales_{a}_{first}", align_bytes=64)
-            nc.vector.quantize_mx(out=codes[:].bitcast(FP8X4), scales=scales[:], in_=rounded)
-            for j in range(count):
-                e = first + j
-                place = e - BANK_OF.index(BANK_OF[e])
-                closes = place == BANK_OF.count(BANK_OF[e]) - 1
-                scale_column = (e * PASSES + a) * N
-                nc.tensor.matmul_mx(
-                    out=banks[BANK_OF[e]][:, slots(place, 1)],
-                    lhsT=w_codes[a][:, e, :].bitcast(FP8X4),
-                    lhsT_scale=w_scale_sb[:, scale_column : scale_column + N],
-                    rhs=codes[:, slots(j, 1)].bitcast(FP8X4),
-                    rhs_scale=scales[:, slots(j, 1)],
-                    start=(a == 0 and place == 0),
-                    stop=(a == LAST_PASS and closes),
-                )
+            for run_first, size in quantise_runs(first, count):
+                codes = keep.tile([P, size * C], U32, name=f"codes_{a}_{run_first}", align_bytes=64)
+                scales = keep.tile([P, size * C], U8, name=f"scales_{a}_{run_first}", align_bytes=64)
+                nc.vector.quantize_mx(out=codes[:].bitcast(FP8X4), scales=scales[:], in_=rounded[:, slots(PACK * (run_first - first), PACK * size)])
+                for j in range(size):
+                    e = run_first + j
+                    place = e - BANK_OF.index(BANK_OF[e])
+                    closes = place == BANK_OF.count(BANK_OF[e]) - 1
+                    scale_column = (e * PASSES + a) * N
+                    nc.tensor.matmul_mx(
+                        out=banks[BANK_OF[e]][:, slots(place, 1)],
+                        lhsT=w_codes[a][:, e, :].bitcast(FP8X4),
+                        lhsT_scale=w_scale_sb[:, scale_column : scale_column + N],
+                        rhs=codes[:, slots(j, 1)].bitcast(FP8X4),
+                        rhs_scale=scales[:, slots(j, 1)],
+                        start=(a == 0 and place == 0),
+                        stop=(a == LAST_PASS and closes),
+                    )
             if a == LAST_PASS:
                 for e in range(first, first + count):
                     sums = banks[BANK_OF[e]][:, slots(e - BANK_OF.index(BANK_OF[e]), 1)]
-                    if e == FED - 1:
+                    if e == E - 1:
                         nc.vector.tensor_scalar_add(y[:, slots(e, 1)], sums, bias[:, e : e + 1])
                     else:
                         nc.scalar.activation(y[:, slots(e, 1)], sums, IDENTITY, bias=bias[:, e : e + 1])
 
-        def own_step(a, rounded):
-            values = gated[a % 2]
+        def gather_own(a):
             for t in range(PACK):
-                nc.vector.tensor_tensor(values[:, slots(t * OWN, OWN)], window(a, t, FED, OWN), gate_own[:], MULT)
-            rounded = rounded[:, : PACK * OWN * C]
-            nc.vector.tensor_copy(by_slot(rounded), by_plane(values[:]))
-            quantise_and_multiply(a, FED, OWN, rounded)
+                for first, count in GATE_PIECES[:2] if a == 0 and t == 0 else ((0, OWN),):
+                    nc.vector.tensor_tensor(gated[a][:, slots(t * OWN + first, count)], window(a, t, first, count), gate_sb[:, slots(first, count)], MULT)
 
-        def chunk_values(a, first, count):
-            return raw[a % RAW_BUFS][:, slots(PACK * first, PACK * count)]
-
-        def gather_chunk(a, first, count):
-            values = chunk_values(a, first, count)
+        def gather_chunk(n):
+            a, first, count = CHUNKS[n]
             for t in range(PACK):
-                nc.scalar.activation(values[:, slots(t * count, count)], window(a, t, first, count), COPY)
+                nc.scalar.activation(raw[n % RAW_BUFS][:, slots(t * count, count)], window(a, t, first, count), COPY)
 
-        def fed_step(a, first, count, rounded):
-            rounded = rounded[:, : PACK * count * C]
-            pairs = count * C // RUN
-            weight = gate_fed[:, slots(first, count)].rearrange("p (c i) -> p c i", i=RUN).unsqueeze(2).to_broadcast([P, pairs, PACK, RUN])
-            nc.vector.tensor_tensor(by_slot(rounded), by_plane(chunk_values(a, first, count)), weight, MULT)
-            quantise_and_multiply(a, first, count, rounded)
+        def weave_own(a, rounded):
+            nc.vector.tensor_copy(by_slot(rounded[:, : PACK * OWN * C]), by_plane(gated[a][:]))
 
-        steps = [("own", a) for a in range(LEAD)]
+        def weave_chunk(n, rounded):
+            a, first, count = CHUNKS[n]
+            weight = gate_sb[:, slots(first, count)].rearrange("p (c i) -> p c i", i=RUN).unsqueeze(2).to_broadcast([P, count * C // RUN, PACK, RUN])
+            nc.vector.tensor_tensor(by_slot(rounded[:, : PACK * count * C]), by_plane(raw[n % RAW_BUFS][:, : PACK * count * C]), weight, MULT)
+
+        steps = []
         for n in range(len(CHUNKS)):
-            steps.append(("fed", n))
-            if LEAD + n < PASSES:
-                steps.append(("own", LEAD + n))
+            if n < OWN_PASSES:
+                steps.append(("own", n))
+            steps.append(("chunk", n))
+        waiting = None
         for place, (kind, n) in enumerate(steps):
+            rounded = woven[place % WOVEN_BUFS]
             if kind == "own":
-                own_step(n, woven[place % 2])
+                gather_own(n)
+                if waiting is not None:
+                    quantise_and_multiply(*waiting)
+                weave_own(n, rounded)
+                waiting = (n, 0, OWN, rounded)
             else:
-                gather_chunk(*CHUNKS[n])
-                fed_step(*CHUNKS[n], woven[place % 2])
+                gather_chunk(n)
+                weave_chunk(n, rounded)
+                quantise_and_multiply(*waiting)
+                waiting = CHUNKS[n] + (rounded,)
+        quantise_and_multiply(*waiting)
 
         picked = keep.tile([P, T], F32, name="picked")
         total = keep.tile([P, T], F32, name="total")

@@ -75,6 +75,10 @@ def tile_moe_pre_lin_bias_kernel(tc, xT, w_words, w_scales, b, gate, offs, pos1,
         windows = [keep.tile([P, window_columns(i // PACK)], F32, name=f"window_{i}") for i in range(PLANES)]
         nc.gpsimd.memset(w_scale_sb[:].bitcast(I32), 0)
 
+        warm = keep.tile([P, 2], F32, name="warm")
+        nc.vector.memset(warm[:, 0:1], 0.0)
+        nc.scalar.activation(warm[:, 1:2], warm[:, 0:1], COPY)
+
         x_planes = xT.rearrange("(a p t) c -> a t p c", p=P, t=PACK)
         gate_sb = keep.tile([P, S], F32, name="gate_sb")
 

@@ -1,6 +1,7 @@
 from contextlib import ExitStack
 
 import concourse.mybir as mybir
+from concourse.masks import make_identity
 
 K, T, E, C, N = 2560, 640, 10, 128, 128
 S = E * C
@@ -28,30 +29,15 @@ PER_COLUMN = 16
 QUADRANT = 32
 RUN = 2
 
-OWN = 6
 OWN_PASSES = 2
-CHUNKS = ((0, 6, 4), (1, 6, 4), (2, 0, 5), (2, 5, 5), (3, 0, 5), (3, 5, 5), (4, 0, 4), (4, 4, 3), (4, 7, 2), (4, 9, 1))
-WIDEST = max(count for a, first, count in CHUNKS)
-RAW_BUFS = 4
-WOVEN_BUFS = 3
-GATE_PIECES = ((0, 2), (2, 4), (6, 4))
+OWN_FIRST = 3
+OWN = E - OWN_FIRST
+POOL_FIRST = 7
+PER_BANK = 4
+GATE_BANKS = 2
+GATE_PIECES = ((OWN_FIRST, 2), (OWN_FIRST + 2, OWN - 2), (0, OWN_FIRST))
 TOKEN_RUN = 160
-BANK_OF = (0, 0, 1, 1, 2, 3, 4, 5, 6, 7)
-QUANTISE_RUNS = (8, 4, 3, 2, 1)
-
-
-def quantise_runs(first, count):
-    runs = []
-    while count > 0:
-        size = max(m for m in QUANTISE_RUNS if m <= count)
-        runs.append((first, size))
-        first, count = first + size, count - size
-    return runs
-
-
-def window_columns(a):
-    widest = max([count for b, first, count in CHUNKS if b == a] + [OWN if a < OWN_PASSES else 0])
-    return max(T, widest * C + 8)
+BANK_OF = (0, 0, 0, 0, 1, 1, 2, 3, 4, 4)
 
 
 def slots(first, count):
@@ -72,7 +58,7 @@ def tile_moe_pre_lin_bias_kernel(tc, xT, w_words, w_scales, b, gate, offs, pos1,
         pos1_sb = keep.tile([P, T // PER_COLUMN], U16, name="pos1_sb")
         pos2_sb = keep.tile([P, T // PER_COLUMN], U16, name="pos2_sb")
         w_scale_sb = keep.tile([P, E * PASSES * N], U8, name="w_scale_sb", align_bytes=64)
-        windows = [keep.tile([P, window_columns(i // PACK)], F32, name=f"window_{i}") for i in range(PLANES)]
+        windows = [keep.tile([P, OWN * C + 8 if i < OWN_PASSES * PACK else T], F32, name=f"window_{i}") for i in range(PLANES)]
         nc.gpsimd.memset(w_scale_sb[:].bitcast(I32), 0)
 
         warm = keep.tile([P, 2], F32, name="warm")
@@ -116,84 +102,127 @@ def tile_moe_pre_lin_bias_kernel(tc, xT, w_words, w_scales, b, gate, offs, pos1,
 
         y = keep.tile([P, S], F32, name="y")
         banks = [psum.tile([P, BANK_OF.count(i) * C], F32, name=f"bank_{i}") for i in range(max(BANK_OF) + 1)]
-        raw = [keep.tile([P, PACK * WIDEST * C], F32, name=f"raw_{i}", align_bytes=64) for i in range(RAW_BUFS)]
         gated = [keep.tile([P, PACK * OWN * C], F32, name=f"gated_{i}", align_bytes=64) for i in range(OWN_PASSES)]
-        woven = [keep.tile([P, PACK * max(OWN, WIDEST) * C], BF16, name=f"woven_{i}", align_bytes=64) for i in range(WOVEN_BUFS)]
+        woven = keep.tile([P, PACK * S], BF16, name="woven", align_bytes=64)
+
+        identity = keep.tile([P, P], F32, name="identity")
+        make_identity(nc, identity[:])
+        gate_columns = keep.tile([P, GATE_BANKS * PER_BANK], F32, name="gate_columns")
+        gate_ps = []
+        for i in range(GATE_BANKS):
+            spread = psum.tile([P, PER_BANK * C], F32, name=f"gate_ps_{i}")
+            for j in range(PER_BANK):
+                nc.tensor.transpose(spread[:, slots(j, 1)], gate_sb[:, slots(i * PER_BANK + j, 1)], identity[:])
+            columns = gate_columns[:, i * PER_BANK : (i + 1) * PER_BANK]
+            nc.vector.tensor_copy(columns, spread[:, 0 : PER_BANK * C : C])
+            for j in range(PER_BANK):
+                nc.tensor.transpose(spread[:, slots(j, 1)], columns[:, j : j + 1].to_broadcast([P, P]), identity[:])
+            gate_ps.append(spread)
 
         def window(a, t, first, count):
             return windows[a * PACK + t][:].indirect(offs_sb[:, list_columns(first * C, count * C)])
 
-        def by_plane(flat):
-            return flat.rearrange("p (t c i) -> p c t i", t=PACK, i=RUN)
+        def by_plane(flat, run):
+            return flat.rearrange("p (t c i) -> p c t i", t=PACK, i=run)
 
-        def by_slot(flat):
-            return flat.rearrange("p (c i t) -> p c t i", t=PACK, i=RUN)
-
-        def quantise_and_multiply(a, first, count, rounded):
-            for run_first, size in quantise_runs(first, count):
-                codes = keep.tile([P, size * C], U32, name=f"codes_{a}_{run_first}", align_bytes=64)
-                scales = keep.tile([P, size * C], U8, name=f"scales_{a}_{run_first}", align_bytes=64)
-                nc.vector.quantize_mx(out=codes[:].bitcast(FP8X4), scales=scales[:], in_=rounded[:, slots(PACK * (run_first - first), PACK * size)])
-                for j in range(size):
-                    e = run_first + j
-                    place = e - BANK_OF.index(BANK_OF[e])
-                    closes = place == BANK_OF.count(BANK_OF[e]) - 1
-                    scale_column = (e * PASSES + a) * N
-                    nc.tensor.matmul_mx(
-                        out=banks[BANK_OF[e]][:, slots(place, 1)],
-                        lhsT=w_codes[a][:, e, :].bitcast(FP8X4),
-                        lhsT_scale=w_scale_sb[:, scale_column : scale_column + N],
-                        rhs=codes[:, slots(j, 1)].bitcast(FP8X4),
-                        rhs_scale=scales[:, slots(j, 1)],
-                        start=(a == 0 and place == 0),
-                        stop=(a == LAST_PASS and closes),
-                    )
-            if a == LAST_PASS:
-                for e in range(first, first + count):
-                    sums = banks[BANK_OF[e]][:, slots(e - BANK_OF.index(BANK_OF[e]), 1)]
-                    if e == E - 1:
-                        nc.vector.tensor_scalar_add(y[:, slots(e, 1)], sums, bias[:, e : e + 1])
-                    else:
-                        nc.scalar.activation(y[:, slots(e, 1)], sums, IDENTITY, bias=bias[:, e : e + 1])
+        def by_slot(first, count, run):
+            return woven[:, slots(PACK * first, PACK * count)].rearrange("p (c i t) -> p c t i", t=PACK, i=run)
 
         def gather_own(a):
             for t in range(PACK):
-                for first, count in GATE_PIECES[:2] if a == 0 and t == 0 else ((0, OWN),):
-                    nc.vector.tensor_tensor(gated[a][:, slots(t * OWN + first, count)], window(a, t, first, count), gate_sb[:, slots(first, count)], MULT)
+                for first, count in GATE_PIECES[:2] if a == 0 and t == 0 else ((OWN_FIRST, OWN),):
+                    nc.vector.tensor_tensor(gated[a][:, slots(t * OWN + first - OWN_FIRST, count)], window(a, t, first, count), gate_sb[:, slots(first, count)], MULT)
 
-        def gather_chunk(n):
-            a, first, count = CHUNKS[n]
+        raw = {}
+
+        def gather(a, first, count, room=None):
+            if room is None:
+                room = keep.tile([P, PACK * count * C], F32, name=f"raw_{a}_{first}", align_bytes=64)[:]
+            raw[a, first] = room
             for t in range(PACK):
-                nc.scalar.activation(raw[n % RAW_BUFS][:, slots(t * count, count)], window(a, t, first, count), COPY)
+                nc.scalar.activation(room[:, slots(t * count, count)], window(a, t, first, count), COPY)
 
-        def weave_own(a, rounded):
-            nc.vector.tensor_copy(by_slot(rounded[:, : PACK * OWN * C]), by_plane(gated[a][:]))
+        def weave(engine, a, first, count, weight, run):
+            spread = weight.rearrange("p (c i) -> p c i", i=run).unsqueeze(2).to_broadcast([P, count * C // run, PACK, run])
+            engine.tensor_tensor(by_slot(first, count, run), by_plane(raw[a, first], run), spread, MULT)
 
-        def weave_chunk(n, rounded):
-            a, first, count = CHUNKS[n]
-            weight = gate_sb[:, slots(first, count)].rearrange("p (c i) -> p c i", i=RUN).unsqueeze(2).to_broadcast([P, count * C // RUN, PACK, RUN])
-            nc.vector.tensor_tensor(by_slot(rounded[:, : PACK * count * C]), by_plane(raw[n % RAW_BUFS][:, : PACK * count * C]), weight, MULT)
+        def pool_weave(a, first, count):
+            weave(nc.gpsimd, a, first, count, gate_sb[:, slots(first, count)], 2)
 
-        steps = []
-        for n in range(len(CHUNKS)):
-            if n < OWN_PASSES:
-                steps.append(("own", n))
-            steps.append(("chunk", n))
-        waiting = None
-        for place, (kind, n) in enumerate(steps):
-            rounded = woven[place % WOVEN_BUFS]
-            if kind == "own":
-                gather_own(n)
-                if waiting is not None:
-                    quantise_and_multiply(*waiting)
-                weave_own(n, rounded)
-                waiting = (n, 0, OWN, rounded)
-            else:
-                gather_chunk(n)
-                weave_chunk(n, rounded)
-                quantise_and_multiply(*waiting)
-                waiting = CHUNKS[n] + (rounded,)
-        quantise_and_multiply(*waiting)
+        def vector_weave(a, first, count):
+            weave(nc.vector, a, first, count, gate_ps[first // PER_BANK][:, slots(first % PER_BANK, count)], RUN)
+
+        passes_left = [PASSES * BANK_OF.count(i) for i in range(len(banks))]
+
+        def quantise_and_multiply(a, first, count):
+            codes = keep.tile([P, count * C], U32, name=f"codes_{a}_{first}", align_bytes=64)
+            scales = keep.tile([P, count * C], U8, name=f"scales_{a}_{first}", align_bytes=64)
+            nc.vector.quantize_mx(out=codes[:].bitcast(FP8X4), scales=scales[:], in_=woven[:, slots(PACK * first, PACK * count)])
+            for j in range(count):
+                e = first + j
+                bank = BANK_OF[e]
+                opens = passes_left[bank] == PASSES * BANK_OF.count(bank)
+                passes_left[bank] = passes_left[bank] - 1
+                scale_column = (e * PASSES + a) * N
+                nc.tensor.matmul_mx(
+                    out=banks[bank][:, slots(e - BANK_OF.index(bank), 1)],
+                    lhsT=w_codes[a][:, e, :].bitcast(FP8X4),
+                    lhsT_scale=w_scale_sb[:, scale_column : scale_column + N],
+                    rhs=codes[:, slots(j, 1)].bitcast(FP8X4),
+                    rhs_scale=scales[:, slots(j, 1)],
+                    start=opens,
+                    stop=(passes_left[bank] == 0),
+                )
+
+        def add_bias_on_scalar(first, count):
+            for e in range(first, first + count):
+                sums = banks[BANK_OF[e]][:, slots(e - BANK_OF.index(BANK_OF[e]), 1)]
+                nc.scalar.activation(y[:, slots(e, 1)], sums, IDENTITY, bias=bias[:, e : e + 1])
+
+        def add_bias_on_vector(first, count):
+            nc.vector.tensor_tensor(
+                y[:, slots(first, count)].rearrange("p (e c) -> p e c", c=C),
+                banks[BANK_OF[first]][:].rearrange("p (e c) -> p e c", c=C),
+                bias[:, first : first + count].unsqueeze(2).to_broadcast([P, count, C]),
+                ADD,
+            )
+
+        for a in range(OWN_PASSES):
+            gather_own(a)
+            gather(a, 0, OWN_FIRST)
+            nc.vector.tensor_copy(by_slot(OWN_FIRST, OWN, RUN), by_plane(gated[a][:], RUN))
+            vector_weave(a, 0, OWN_FIRST)
+            quantise_and_multiply(a, 8, 2)
+            quantise_and_multiply(a, 0, 8)
+        for a in range(OWN_PASSES, LAST_PASS):
+            gather(a, POOL_FIRST, E - POOL_FIRST)
+            pool_weave(a, POOL_FIRST, E - POOL_FIRST)
+            for first, count in ((0, PER_BANK), (PER_BANK, POOL_FIRST - PER_BANK)):
+                gather(a, first, count)
+                vector_weave(a, first, count)
+            quantise_and_multiply(a, 0, 8)
+            quantise_and_multiply(a, 8, 2)
+        a = LAST_PASS
+        gather(a, 0, 4, gated[0][:, slots(0, 16)])
+        gather(a, 8, 2, gated[0][:, slots(16, 8)])
+        gather(a, 4, 2, gated[1][:, slots(0, 8)])
+        gather(a, 6, 1, gated[1][:, slots(8, 4)])
+        gather(a, 7, 1, gated[1][:, slots(12, 4)])
+        pool_weave(a, 8, 2)
+        vector_weave(a, 0, 4)
+        vector_weave(a, 4, 2)
+        quantise_and_multiply(a, 0, 4)
+        add_bias_on_scalar(0, 4)
+        quantise_and_multiply(a, 8, 2)
+        add_bias_on_scalar(8, 2)
+        vector_weave(a, 6, 1)
+        quantise_and_multiply(a, 4, 2)
+        vector_weave(a, 7, 1)
+        quantise_and_multiply(a, 6, 1)
+        add_bias_on_scalar(6, 1)
+        quantise_and_multiply(a, 7, 1)
+        add_bias_on_vector(4, 2)
+        add_bias_on_vector(7, 1)
 
         picked = keep.tile([P, T], F32, name="picked")
         total = keep.tile([P, T], F32, name="total")

@@ -29,15 +29,26 @@ PER_COLUMN = 16
 QUADRANT = 32
 RUN = 2
 
-OWN_PASSES = 2
-OWN_FIRST = 3
+OWN_PASSES = 3
+OWN_FIRST = 5
 OWN = E - OWN_FIRST
-POOL_FIRST = 7
+POOL_PASS = OWN_PASSES
+POOL_SECOND = 3
 PER_BANK = 4
 GATE_BANKS = 2
 GATE_PIECES = ((OWN_FIRST, 2), (OWN_FIRST + 2, OWN - 2), (0, OWN_FIRST))
+WINDOW_COLUMNS = T + 8
 TOKEN_RUN = 160
-BANK_OF = (0, 0, 0, 0, 1, 1, 2, 3, 4, 4)
+BANK_OF = (0, 0, 0, 0, 1, 1, 2, 2, 3, 4)
+
+
+def quantise_runs(count):
+    runs, first = [], 0
+    while first < count:
+        size = max(m for m in (8, 4, 3, 2, 1) if m <= count - first)
+        runs.append((first, size))
+        first = first + size
+    return runs
 
 
 def slots(first, count):
@@ -58,7 +69,7 @@ def tile_moe_pre_lin_bias_kernel(tc, xT, w_words, w_scales, b, gate, offs, pos1,
         pos1_sb = keep.tile([P, T // PER_COLUMN], U16, name="pos1_sb")
         pos2_sb = keep.tile([P, T // PER_COLUMN], U16, name="pos2_sb")
         w_scale_sb = keep.tile([P, E * PASSES * N], U8, name="w_scale_sb", align_bytes=64)
-        windows = [keep.tile([P, OWN * C + 8 if i < OWN_PASSES * PACK else T], F32, name=f"window_{i}") for i in range(PLANES)]
+        windows = [keep.tile([P, WINDOW_COLUMNS], F32, name=f"window_{i}") for i in range(PLANES)]
         nc.gpsimd.memset(w_scale_sb[:].bitcast(I32), 0)
 
         warm = keep.tile([P, 2], F32, name="warm")
@@ -78,11 +89,12 @@ def tile_moe_pre_lin_bias_kernel(tc, xT, w_words, w_scales, b, gate, offs, pos1,
         load_plane(0)
         load_gate(*GATE_PIECES[0])
         load_gate(*GATE_PIECES[1])
-        for i in range(1, PACK):
+        for i in range(1, PLANES):
             load_plane(i)
         load_gate(*GATE_PIECES[2])
-        for i in range(PACK, PLANES):
-            load_plane(i)
+        gate_columns = keep.tile([P, GATE_BANKS * PER_BANK], F32, name="gate_columns")
+        with nc.allow_non_contiguous_dma(reason="one gate value a partition"):
+            nc.sync.dma_start(gate_columns[:], gate[0, slots(0, GATE_BANKS * PER_BANK)].rearrange("(e s) -> s e", s=C))
 
         bias = keep.tile([P, E], F32, name="bias")
         rows = w_scales.rearrange("e a q n -> q (e a) n").bitcast(I32)
@@ -102,62 +114,70 @@ def tile_moe_pre_lin_bias_kernel(tc, xT, w_words, w_scales, b, gate, offs, pos1,
 
         y = keep.tile([P, S], F32, name="y")
         banks = [psum.tile([P, BANK_OF.count(i) * C], F32, name=f"bank_{i}") for i in range(max(BANK_OF) + 1)]
-        gated = [keep.tile([P, PACK * OWN * C], F32, name=f"gated_{i}", align_bytes=64) for i in range(OWN_PASSES)]
-        woven = keep.tile([P, PACK * S], BF16, name="woven", align_bytes=64)
+        gated = [keep.tile([P, PACK * OWN * C], F32, name=f"gated_{i}", align_bytes=64) for i in range(2)]
+        woven = [keep.tile([P, PACK * OWN * C], BF16, name=f"woven_{i}", align_bytes=64) for i in range(OWN_PASSES + 1)]
 
         identity = keep.tile([P, P], F32, name="identity")
         make_identity(nc, identity[:])
-        gate_columns = keep.tile([P, GATE_BANKS * PER_BANK], F32, name="gate_columns")
         gate_ps = []
         for i in range(GATE_BANKS):
             spread = psum.tile([P, PER_BANK * C], F32, name=f"gate_ps_{i}")
             for j in range(PER_BANK):
-                nc.tensor.transpose(spread[:, slots(j, 1)], gate_sb[:, slots(i * PER_BANK + j, 1)], identity[:])
-            columns = gate_columns[:, i * PER_BANK : (i + 1) * PER_BANK]
-            nc.vector.tensor_copy(columns, spread[:, 0 : PER_BANK * C : C])
-            for j in range(PER_BANK):
-                nc.tensor.transpose(spread[:, slots(j, 1)], columns[:, j : j + 1].to_broadcast([P, P]), identity[:])
+                e = i * PER_BANK + j
+                nc.tensor.transpose(spread[:, slots(j, 1)], gate_columns[:, e : e + 1].to_broadcast([P, P]), identity[:])
             gate_ps.append(spread)
 
         def window(a, t, first, count):
             return windows[a * PACK + t][:].indirect(offs_sb[:, list_columns(first * C, count * C)])
 
-        def by_plane(flat, run):
-            return flat.rearrange("p (t c i) -> p c t i", t=PACK, i=run)
+        def by_plane(values):
+            return values.rearrange("p t (c i) -> p c t i", i=RUN)
 
-        def by_slot(first, count, run):
-            return woven[:, slots(PACK * first, PACK * count)].rearrange("p (c i t) -> p c t i", t=PACK, i=run)
+        def by_slot(rounded):
+            return rounded.rearrange("p (c i t) -> p c t i", t=PACK, i=RUN)
 
-        def gather_own(a):
-            for t in range(PACK):
+        def room(tile, first, count):
+            return tile[:, slots(PACK * first, PACK * count)]
+
+        def gather_own(a, planes):
+            for t in planes:
                 for first, count in GATE_PIECES[:2] if a == 0 and t == 0 else ((OWN_FIRST, OWN),):
-                    nc.vector.tensor_tensor(gated[a][:, slots(t * OWN + first - OWN_FIRST, count)], window(a, t, first, count), gate_sb[:, slots(first, count)], MULT)
+                    nc.vector.tensor_tensor(gated[a % 2][:, slots(t * OWN + first - OWN_FIRST, count)], window(a, t, first, count), gate_sb[:, slots(first, count)], MULT)
 
-        raw = {}
-
-        def gather(a, first, count, room=None):
-            if room is None:
-                room = keep.tile([P, PACK * count * C], F32, name=f"raw_{a}_{first}", align_bytes=64)[:]
-            raw[a, first] = room
+        def gather(a, first, count, values=None):
+            if values is None:
+                values = keep.tile([P, PACK * count * C], F32, name=f"raw_{a}_{first}", align_bytes=64)[:]
             for t in range(PACK):
-                nc.scalar.activation(room[:, slots(t * count, count)], window(a, t, first, count), COPY)
+                nc.scalar.activation(values[:, slots(t * count, count)], window(a, t, first, count), COPY)
+            return values.rearrange("p (t s) -> p t s", t=PACK)
 
-        def weave(engine, a, first, count, weight, run):
-            spread = weight.rearrange("p (c i) -> p c i", i=run).unsqueeze(2).to_broadcast([P, count * C // run, PACK, run])
-            engine.tensor_tensor(by_slot(first, count, run), by_plane(raw[a, first], run), spread, MULT)
+        def weave(engine, values, weight, rounded):
+            count = weight.shape[1]
+            spread = weight.rearrange("p (c i) -> p c i", i=RUN).unsqueeze(2).to_broadcast([P, count // RUN, PACK, RUN])
+            engine.tensor_tensor(by_slot(rounded), by_plane(values), spread, MULT)
 
-        def pool_weave(a, first, count):
-            weave(nc.gpsimd, a, first, count, gate_sb[:, slots(first, count)], 2)
+        def pool_weave(first, count, values, rounded):
+            weave(nc.gpsimd, values, gate_sb[:, slots(first, count)], rounded)
 
-        def vector_weave(a, first, count):
-            weave(nc.vector, a, first, count, gate_ps[first // PER_BANK][:, slots(first % PER_BANK, count)], RUN)
+        def vector_weave(first, count, values, rounded):
+            if first >= GATE_BANKS * PER_BANK:
+                weave(nc.vector, values, gate_sb[:, slots(first, count)], rounded)
+                return
+            for lo in range(first, first + count):
+                if lo == first or lo % PER_BANK == 0:
+                    size = min(first + count, (lo // PER_BANK + 1) * PER_BANK) - lo
+                    weave(nc.vector, values[:, :, slots(lo - first, size)], gate_ps[lo // PER_BANK][:, slots(lo % PER_BANK, size)], room(rounded, lo - first, size))
 
         passes_left = [PASSES * BANK_OF.count(i) for i in range(len(banks))]
 
-        def quantise_and_multiply(a, first, count):
+        def quantise(a, first, count, rounded):
+            for place, size in quantise_runs(count):
+                quantise_and_multiply(a, first + place, size, room(rounded, place, size))
+
+        def quantise_and_multiply(a, first, count, rounded):
             codes = keep.tile([P, count * C], U32, name=f"codes_{a}_{first}", align_bytes=64)
             scales = keep.tile([P, count * C], U8, name=f"scales_{a}_{first}", align_bytes=64)
-            nc.vector.quantize_mx(out=codes[:].bitcast(FP8X4), scales=scales[:], in_=woven[:, slots(PACK * first, PACK * count)])
+            nc.vector.quantize_mx(out=codes[:].bitcast(FP8X4), scales=scales[:], in_=rounded)
             for j in range(count):
                 e = first + j
                 bank = BANK_OF[e]
@@ -187,42 +207,42 @@ def tile_moe_pre_lin_bias_kernel(tc, xT, w_words, w_scales, b, gate, offs, pos1,
                 ADD,
             )
 
+        fed = []
         for a in range(OWN_PASSES):
-            gather_own(a)
-            gather(a, 0, OWN_FIRST)
-            nc.vector.tensor_copy(by_slot(OWN_FIRST, OWN, RUN), by_plane(gated[a][:], RUN))
-            vector_weave(a, 0, OWN_FIRST)
-            quantise_and_multiply(a, 8, 2)
-            quantise_and_multiply(a, 0, 8)
-        for a in range(OWN_PASSES, LAST_PASS):
-            gather(a, POOL_FIRST, E - POOL_FIRST)
-            pool_weave(a, POOL_FIRST, E - POOL_FIRST)
-            for first, count in ((0, PER_BANK), (PER_BANK, POOL_FIRST - PER_BANK)):
-                gather(a, first, count)
-                vector_weave(a, first, count)
-            quantise_and_multiply(a, 0, 8)
-            quantise_and_multiply(a, 8, 2)
+            gather_own(a, range(1))
+            if a > 0:
+                quantise(a - 1, OWN_FIRST, OWN, woven[0][:])
+            gather_own(a, range(1, PACK))
+            fed.append(gather(a, 0, OWN_FIRST))
+            nc.vector.tensor_copy(by_slot(woven[0][:]), by_plane(gated[a % 2][:].rearrange("p (t s) -> p t s", t=PACK)))
+        quantise(OWN_PASSES - 1, OWN_FIRST, OWN, woven[0][:])
+
+        pool_weave(OWN_FIRST, OWN, gather(POOL_PASS, OWN_FIRST, OWN), woven[0][:])
+        for a in range(OWN_PASSES):
+            vector_weave(0, OWN_FIRST, fed[a], woven[a + 1][:])
+        for a in range(OWN_PASSES):
+            quantise(a, 0, OWN_FIRST, woven[a + 1][:])
+        quantise(POOL_PASS, OWN_FIRST, OWN, woven[0][:])
+
+        rest = OWN_FIRST - POOL_SECOND
+        values = gather(POOL_PASS, 0, OWN_FIRST)
+        pool_weave(rest, POOL_SECOND, values[:, :, slots(rest, POOL_SECOND)], room(woven[0], rest, POOL_SECOND))
+        vector_weave(0, rest, values[:, :, slots(0, rest)], room(woven[1], 0, rest))
         a = LAST_PASS
-        gather(a, 0, 4, gated[0][:, slots(0, 16)])
-        gather(a, 8, 2, gated[0][:, slots(16, 8)])
-        gather(a, 4, 2, gated[1][:, slots(0, 8)])
-        gather(a, 6, 1, gated[1][:, slots(8, 4)])
-        gather(a, 7, 1, gated[1][:, slots(12, 4)])
-        pool_weave(a, 8, 2)
-        vector_weave(a, 0, 4)
-        vector_weave(a, 4, 2)
-        quantise_and_multiply(a, 0, 4)
+        vector_weave(0, 4, gather(a, 0, 4, room(gated[1], 0, 4)), room(woven[2], 0, 4))
+        vector_weave(4, 4, gather(a, 4, 4, room(gated[0], 0, 4)), room(woven[3], 0, 4))
+        quantise(POOL_PASS, 0, rest, woven[1][:])
+        quantise(POOL_PASS, rest, POOL_SECOND, room(woven[0], rest, POOL_SECOND))
+        quantise(a, 0, 4, woven[2][:])
         add_bias_on_scalar(0, 4)
-        quantise_and_multiply(a, 8, 2)
-        add_bias_on_scalar(8, 2)
-        vector_weave(a, 6, 1)
-        quantise_and_multiply(a, 4, 2)
-        vector_weave(a, 7, 1)
-        quantise_and_multiply(a, 6, 1)
-        add_bias_on_scalar(6, 1)
-        quantise_and_multiply(a, 7, 1)
-        add_bias_on_vector(4, 2)
-        add_bias_on_vector(7, 1)
+        vector_weave(8, 1, gather(a, 8, 1, room(gated[1], 4, 1)), room(woven[1], 0, 1))
+        quantise(a, 4, 4, woven[3][:])
+        add_bias_on_scalar(4, 4)
+        vector_weave(9, 1, gather(a, 9, 1, room(gated[0], 4, 1)), room(woven[1], 1, 1))
+        quantise(a, 8, 1, room(woven[1], 0, 1))
+        add_bias_on_scalar(8, 1)
+        quantise(a, 9, 1, room(woven[1], 1, 1))
+        add_bias_on_vector(9, 1)
 
         picked = keep.tile([P, T], F32, name="picked")
         total = keep.tile([P, T], F32, name="total")

@@ -23,32 +23,24 @@ COPY = mybir.ActivationFunctionType.Copy
 P = 128
 PACK = 4
 PASSES = K // (P * PACK)
-PLANES = PASSES * PACK
 LAST_PASS = PASSES - 1
 PER_COLUMN = 16
 QUADRANT = 32
 RUN = 2
-
-OWN_PASSES = 3
-OWN_FIRST = 5
-OWN = E - OWN_FIRST
-POOL_PASS = OWN_PASSES
-POOL_SECOND = 3
+SPARE = 8
 PER_BANK = 4
+
+SHARED = 3
+FED = 5
+OWN = E - FED
+POOL_PASS = SHARED
+POOL_FIRST = 6
+POOL_SECOND = 3
+POOL_LEFT = E - POOL_FIRST - POOL_SECOND
 GATE_BANKS = 2
-GATE_PIECES = ((OWN_FIRST, 2), (OWN_FIRST + 2, OWN - 2), (0, OWN_FIRST))
-WINDOW_COLUMNS = T + 8
-TOKEN_RUN = 160
+GATE_PIECES = ((FED, 2), (FED + 2, OWN - 2), (0, FED))
 BANK_OF = (0, 0, 0, 0, 1, 1, 2, 2, 3, 4)
-
-
-def quantise_runs(count):
-    runs, first = [], 0
-    while first < count:
-        size = max(m for m in (8, 4, 3, 2, 1) if m <= count - first)
-        runs.append((first, size))
-        first = first + size
-    return runs
+TOKEN_RUN = 160
 
 
 def slots(first, count):
@@ -57,6 +49,10 @@ def slots(first, count):
 
 def list_columns(first_entry, count):
     return slice(first_entry // PER_COLUMN, (first_entry + count) // PER_COLUMN)
+
+
+def units(a, first, count):
+    return [(a, e) for e in range(first, first + count)]
 
 
 def tile_moe_pre_lin_bias_kernel(tc, xT, w_words, w_scales, b, gate, offs, pos1, pos2, out):
@@ -69,7 +65,10 @@ def tile_moe_pre_lin_bias_kernel(tc, xT, w_words, w_scales, b, gate, offs, pos1,
         pos1_sb = keep.tile([P, T // PER_COLUMN], U16, name="pos1_sb")
         pos2_sb = keep.tile([P, T // PER_COLUMN], U16, name="pos2_sb")
         w_scale_sb = keep.tile([P, E * PASSES * N], U8, name="w_scale_sb", align_bytes=64)
-        windows = [keep.tile([P, WINDOW_COLUMNS], F32, name=f"window_{i}") for i in range(PLANES)]
+        windows = [
+            keep.tile([P, (POOL_FIRST if i // PACK == POOL_PASS else OWN) * C + SPARE], F32, name=f"window_{i}")
+            for i in range(PASSES * PACK)
+        ]
         nc.gpsimd.memset(w_scale_sb[:].bitcast(I32), 0)
 
         warm = keep.tile([P, 2], F32, name="warm")
@@ -89,8 +88,9 @@ def tile_moe_pre_lin_bias_kernel(tc, xT, w_words, w_scales, b, gate, offs, pos1,
         load_plane(0)
         load_gate(*GATE_PIECES[0])
         load_gate(*GATE_PIECES[1])
-        for i in range(1, PLANES):
-            load_plane(i)
+        for a in (0, 1, POOL_PASS, SHARED - 1, LAST_PASS):
+            for i in range(max(1, a * PACK), (a + 1) * PACK):
+                load_plane(i)
         load_gate(*GATE_PIECES[2])
         gate_columns = keep.tile([P, GATE_BANKS * PER_BANK], F32, name="gate_columns")
         with nc.allow_non_contiguous_dma(reason="one gate value a partition"):
@@ -115,34 +115,36 @@ def tile_moe_pre_lin_bias_kernel(tc, xT, w_words, w_scales, b, gate, offs, pos1,
         y = keep.tile([P, S], F32, name="y")
         banks = [psum.tile([P, BANK_OF.count(i) * C], F32, name=f"bank_{i}") for i in range(max(BANK_OF) + 1)]
         gated = [keep.tile([P, PACK * OWN * C], F32, name=f"gated_{i}", align_bytes=64) for i in range(2)]
-        woven = [keep.tile([P, PACK * OWN * C], BF16, name=f"woven_{i}", align_bytes=64) for i in range(OWN_PASSES + 1)]
+        pool_place = SHARED * FED
+        woven = keep.tile([P, PACK * (pool_place + POOL_FIRST) * C], BF16, name="woven", align_bytes=64)
 
         identity = keep.tile([P, P], F32, name="identity")
         make_identity(nc, identity[:])
         gate_ps = []
         for i in range(GATE_BANKS):
-            spread = psum.tile([P, PER_BANK * C], F32, name=f"gate_ps_{i}")
+            gate_bank = psum.tile([P, PER_BANK * C], F32, name=f"gate_ps_{i}")
             for j in range(PER_BANK):
                 e = i * PER_BANK + j
-                nc.tensor.transpose(spread[:, slots(j, 1)], gate_columns[:, e : e + 1].to_broadcast([P, P]), identity[:])
-            gate_ps.append(spread)
+                nc.tensor.transpose(gate_bank[:, slots(j, 1)], gate_columns[:, e : e + 1].to_broadcast([P, P]), identity[:])
+            gate_ps.append(gate_bank)
 
         def window(a, t, first, count):
             return windows[a * PACK + t][:].indirect(offs_sb[:, list_columns(first * C, count * C)])
 
+        def room(tile, place, count):
+            return tile[:, slots(PACK * place, PACK * count)]
+
         def by_plane(values):
             return values.rearrange("p t (c i) -> p c t i", i=RUN)
 
-        def by_slot(rounded):
-            return rounded.rearrange("p (c i t) -> p c t i", t=PACK, i=RUN)
+        def by_slot(place, count):
+            return room(woven, place, count).rearrange("p (c i t) -> p c t i", t=PACK, i=RUN)
 
-        def room(tile, first, count):
-            return tile[:, slots(PACK * first, PACK * count)]
-
-        def gather_own(a, planes):
+        def gather_times_gate(a, planes):
             for t in planes:
-                for first, count in GATE_PIECES[:2] if a == 0 and t == 0 else ((OWN_FIRST, OWN),):
-                    nc.vector.tensor_tensor(gated[a % 2][:, slots(t * OWN + first - OWN_FIRST, count)], window(a, t, first, count), gate_sb[:, slots(first, count)], MULT)
+                for first, count in GATE_PIECES[:2] if a == 0 and t == 0 else ((FED, OWN),):
+                    values = gated[a % 2][:, slots(t * OWN + first - FED, count)]
+                    nc.vector.tensor_tensor(values, window(a, t, first, count), gate_sb[:, slots(first, count)], MULT)
 
         def gather(a, first, count, values=None):
             if values is None:
@@ -151,105 +153,107 @@ def tile_moe_pre_lin_bias_kernel(tc, xT, w_words, w_scales, b, gate, offs, pos1,
                 nc.scalar.activation(values[:, slots(t * count, count)], window(a, t, first, count), COPY)
             return values.rearrange("p (t s) -> p t s", t=PACK)
 
-        def weave(engine, values, weight, rounded):
-            count = weight.shape[1]
-            spread = weight.rearrange("p (c i) -> p c i", i=RUN).unsqueeze(2).to_broadcast([P, count // RUN, PACK, RUN])
-            engine.tensor_tensor(by_slot(rounded), by_plane(values), spread, MULT)
+        def pool_weave(first, count, values, place):
+            nc.gpsimd.tensor_tensor(
+                room(woven, place, count).rearrange("p (s t) -> p s t", t=PACK),
+                values.rearrange("p t s -> p s t"),
+                gate_sb[:, slots(first, count)].unsqueeze(2).to_broadcast([P, count * C, PACK]),
+                MULT,
+            )
 
-        def pool_weave(first, count, values, rounded):
-            weave(nc.gpsimd, values, gate_sb[:, slots(first, count)], rounded)
-
-        def vector_weave(first, count, values, rounded):
-            if first >= GATE_BANKS * PER_BANK:
-                weave(nc.vector, values, gate_sb[:, slots(first, count)], rounded)
-                return
+        def vector_weave(first, count, values, place):
             for lo in range(first, first + count):
                 if lo == first or lo % PER_BANK == 0:
                     size = min(first + count, (lo // PER_BANK + 1) * PER_BANK) - lo
-                    weave(nc.vector, values[:, :, slots(lo - first, size)], gate_ps[lo // PER_BANK][:, slots(lo % PER_BANK, size)], room(rounded, lo - first, size))
+                    if lo < GATE_BANKS * PER_BANK:
+                        weight = gate_ps[lo // PER_BANK][:, slots(lo % PER_BANK, size)]
+                    else:
+                        weight = gate_sb[:, slots(lo, size)]
+                    weight = weight.rearrange("p (c i) -> p c i", i=RUN).unsqueeze(2).to_broadcast([P, size * C // RUN, PACK, RUN])
+                    nc.vector.tensor_tensor(by_slot(place + lo - first, size), by_plane(values[:, :, slots(lo - first, size)]), weight, MULT)
 
         passes_left = [PASSES * BANK_OF.count(i) for i in range(len(banks))]
 
-        def quantise(a, first, count, rounded):
-            for place, size in quantise_runs(count):
-                quantise_and_multiply(a, first + place, size, room(rounded, place, size))
-
-        def quantise_and_multiply(a, first, count, rounded):
-            codes = keep.tile([P, count * C], U32, name=f"codes_{a}_{first}", align_bytes=64)
-            scales = keep.tile([P, count * C], U8, name=f"scales_{a}_{first}", align_bytes=64)
-            nc.vector.quantize_mx(out=codes[:].bitcast(FP8X4), scales=scales[:], in_=rounded)
-            for j in range(count):
-                e = first + j
-                bank = BANK_OF[e]
-                opens = passes_left[bank] == PASSES * BANK_OF.count(bank)
-                passes_left[bank] = passes_left[bank] - 1
-                scale_column = (e * PASSES + a) * N
-                nc.tensor.matmul_mx(
-                    out=banks[bank][:, slots(e - BANK_OF.index(bank), 1)],
-                    lhsT=w_codes[a][:, e, :].bitcast(FP8X4),
-                    lhsT_scale=w_scale_sb[:, scale_column : scale_column + N],
-                    rhs=codes[:, slots(j, 1)].bitcast(FP8X4),
-                    rhs_scale=scales[:, slots(j, 1)],
-                    start=opens,
-                    stop=(passes_left[bank] == 0),
-                )
-
-        def add_bias_on_scalar(first, count):
-            for e in range(first, first + count):
-                sums = banks[BANK_OF[e]][:, slots(e - BANK_OF.index(BANK_OF[e]), 1)]
-                nc.scalar.activation(y[:, slots(e, 1)], sums, IDENTITY, bias=bias[:, e : e + 1])
-
-        def add_bias_on_vector(first, count):
-            nc.vector.tensor_tensor(
-                y[:, slots(first, count)].rearrange("p (e c) -> p e c", c=C),
-                banks[BANK_OF[first]][:].rearrange("p (e c) -> p e c", c=C),
-                bias[:, first : first + count].unsqueeze(2).to_broadcast([P, count, C]),
-                ADD,
+        def multiply(a, e, codes, scales):
+            bank = BANK_OF[e]
+            opens = passes_left[bank] == PASSES * BANK_OF.count(bank)
+            passes_left[bank] = passes_left[bank] - 1
+            scale_column = (e * PASSES + a) * N
+            nc.tensor.matmul_mx(
+                out=banks[bank][:, slots(e - BANK_OF.index(bank), 1)],
+                lhsT=w_codes[a][:, e, :].bitcast(FP8X4),
+                lhsT_scale=w_scale_sb[:, scale_column : scale_column + N],
+                rhs=codes.bitcast(FP8X4),
+                rhs_scale=scales,
+                start=opens,
+                stop=(passes_left[bank] == 0),
             )
 
+        def quantise_and_multiply(place, todo):
+            while todo:
+                size = max(m for m in (8, 4, 3, 2, 1) if m <= len(todo))
+                name = f"{todo[0][0]}_{todo[0][1]}"
+                codes = keep.tile([P, size * C], U32, name=f"codes_{name}", align_bytes=64)
+                scales = keep.tile([P, size * C], U8, name=f"scales_{name}", align_bytes=64)
+                nc.vector.quantize_mx(out=codes[:].bitcast(FP8X4), scales=scales[:], in_=room(woven, place, size))
+                for j, (a, e) in enumerate(todo[:size]):
+                    multiply(a, e, codes[:, slots(j, 1)], scales[:, slots(j, 1)])
+                place, todo = place + size, todo[size:]
+
+        def sums_of(e):
+            return banks[BANK_OF[e]][:, slots(e - BANK_OF.index(BANK_OF[e]), 1)]
+
+        def add_bias(first, count):
+            for e in range(first, first + count):
+                nc.scalar.activation(y[:, slots(e, 1)], sums_of(e), IDENTITY, bias=bias[:, e : e + 1])
+
         fed = []
-        for a in range(OWN_PASSES):
-            gather_own(a, range(1))
+        for a in range(SHARED):
+            gather_times_gate(a, range(1))
             if a > 0:
-                quantise(a - 1, OWN_FIRST, OWN, woven[0][:])
-            gather_own(a, range(1, PACK))
-            fed.append(gather(a, 0, OWN_FIRST))
-            nc.vector.tensor_copy(by_slot(woven[0][:]), by_plane(gated[a % 2][:].rearrange("p (t s) -> p t s", t=PACK)))
-        quantise(OWN_PASSES - 1, OWN_FIRST, OWN, woven[0][:])
+                quantise_and_multiply(pool_place, units(a - 1, FED, OWN))
+            gather_times_gate(a, range(1, PACK))
+            if a == SHARED - 1:
+                first_share = gather(POOL_PASS, E - POOL_FIRST, POOL_FIRST)
+            fed.append(gather(a, 0, FED))
+            nc.vector.tensor_copy(by_slot(pool_place, OWN), by_plane(gated[a % 2][:].rearrange("p (t s) -> p t s", t=PACK)))
+        quantise_and_multiply(pool_place, units(SHARED - 1, FED, OWN))
 
-        pool_weave(OWN_FIRST, OWN, gather(POOL_PASS, OWN_FIRST, OWN), woven[0][:])
-        for a in range(OWN_PASSES):
-            vector_weave(0, OWN_FIRST, fed[a], woven[a + 1][:])
-        for a in range(OWN_PASSES):
-            quantise(a, 0, OWN_FIRST, woven[a + 1][:])
-        quantise(POOL_PASS, OWN_FIRST, OWN, woven[0][:])
+        pool_weave(E - POOL_FIRST, POOL_FIRST, first_share, pool_place)
+        todo = []
+        for a in range(SHARED):
+            vector_weave(0, FED, fed[a], a * FED)
+            todo = todo + units(a, 0, FED)
+        todo = todo + units(POOL_PASS, E - POOL_FIRST, POOL_FIRST)
+        second_place = len(todo) - POOL_SECOND
+        quantise_and_multiply(0, todo[:second_place])
+        quantise_and_multiply(second_place, todo[second_place:])
 
-        rest = OWN_FIRST - POOL_SECOND
-        values = gather(POOL_PASS, 0, OWN_FIRST)
-        pool_weave(rest, POOL_SECOND, values[:, :, slots(rest, POOL_SECOND)], room(woven[0], rest, POOL_SECOND))
-        vector_weave(0, rest, values[:, :, slots(0, rest)], room(woven[1], 0, rest))
-        a = LAST_PASS
-        vector_weave(0, 4, gather(a, 0, 4, room(gated[1], 0, 4)), room(woven[2], 0, 4))
-        vector_weave(4, 4, gather(a, 4, 4, room(gated[0], 0, 4)), room(woven[3], 0, 4))
-        quantise(POOL_PASS, 0, rest, woven[1][:])
-        quantise(POOL_PASS, rest, POOL_SECOND, room(woven[0], rest, POOL_SECOND))
-        quantise(a, 0, 4, woven[2][:])
-        add_bias_on_scalar(0, 4)
-        vector_weave(8, 1, gather(a, 8, 1, room(gated[1], 4, 1)), room(woven[1], 0, 1))
-        quantise(a, 4, 4, woven[3][:])
-        add_bias_on_scalar(4, 4)
-        vector_weave(9, 1, gather(a, 9, 1, room(gated[0], 4, 1)), room(woven[1], 1, 1))
-        quantise(a, 8, 1, room(woven[1], 0, 1))
-        add_bias_on_scalar(8, 1)
-        quantise(a, 9, 1, room(woven[1], 1, 1))
-        add_bias_on_vector(9, 1)
+        values = gather(POOL_PASS, 0, POOL_LEFT + POOL_SECOND)
+        pool_weave(POOL_LEFT, POOL_SECOND, values[:, :, slots(POOL_LEFT, POOL_SECOND)], second_place)
+        vector_weave(0, POOL_LEFT, values[:, :, slots(0, POOL_LEFT)], second_place - POOL_LEFT)
+        first_place = second_place - POOL_LEFT - PER_BANK
+        vector_weave(0, 4, gather(LAST_PASS, 0, 4, room(gated[1], 0, 4)), first_place)
+        vector_weave(4, 2, gather(LAST_PASS, 4, 2, room(gated[0], 0, 2)), 4)
+        vector_weave(6, 2, gather(LAST_PASS, 6, 2, room(gated[0], 2, 2)), 6)
+        quantise_and_multiply(first_place, units(LAST_PASS, 0, 4) + units(POOL_PASS, 0, POOL_LEFT + POOL_SECOND))
+        add_bias(0, 4)
+        vector_weave(8, 1, gather(LAST_PASS, 8, 1, room(gated[1], 4, 1)), 8)
+        quantise_and_multiply(4, units(LAST_PASS, 4, 4))
+        add_bias(4, 4)
+        vector_weave(9, 1, gather(LAST_PASS, 9, 1, room(gated[0], 4, 1)), 9)
+        quantise_and_multiply(8, units(LAST_PASS, 8, 1))
+        add_bias(8, 1)
+        quantise_and_multiply(9, units(LAST_PASS, 9, 1))
+        nc.vector.tensor_scalar_add(y[:, slots(E - 1, 1)], sums_of(E - 1), bias[:, E - 1 : E])
 
         picked = keep.tile([P, T], F32, name="picked")
         total = keep.tile([P, T], F32, name="total")
+        last_run = T - TOKEN_RUN
         for t0 in range(0, T, TOKEN_RUN):
             run = slice(t0, t0 + TOKEN_RUN)
             nc.scalar.activation(picked[:, run], y[:].indirect(pos1_sb[:, list_columns(t0, TOKEN_RUN)]), COPY)
             nc.vector.tensor_tensor(total[:, run], y[:].indirect(pos2_sb[:, list_columns(t0, TOKEN_RUN)]), picked[:, run], ADD)
-            if t0 == 2 * TOKEN_RUN:
-                nc.sync.dma_start(out[:, : 3 * TOKEN_RUN], total[:, : 3 * TOKEN_RUN])
-        nc.sync.dma_start(out[:, 3 * TOKEN_RUN :], total[:, 3 * TOKEN_RUN :])
+            if t0 + TOKEN_RUN == last_run:
+                nc.sync.dma_start(out[:, :last_run], total[:, :last_run])
+        nc.sync.dma_start(out[:, last_run:], total[:, last_run:])

@@ -31,14 +31,14 @@ SPARE = 8
 PER_BANK = 4
 
 SHARED = 3
-FED = 5
-OWN = E - FED
+FED = (5, 5, 4)
+OWN = tuple(E - count for count in FED)
 POOL_PASS = SHARED
-POOL_FIRST = 6
+POOL_FIRST = 5
 POOL_SECOND = 3
 POOL_LEFT = E - POOL_FIRST - POOL_SECOND
-GATE_BANKS = 2
-GATE_PIECES = ((FED, 2), (FED + 2, OWN - 2), (0, FED))
+GATE_BANKS = 3
+GATE_PIECES = ((FED[0], 2), (FED[0] + 2, OWN[0] - 2), (0, FED[0]))
 BANK_OF = (0, 0, 0, 0, 1, 1, 2, 2, 3, 4)
 TOKEN_RUN = 160
 
@@ -66,7 +66,7 @@ def tile_moe_pre_lin_bias_kernel(tc, xT, w_words, w_scales, b, gate, offs, pos1,
         pos2_sb = keep.tile([P, T // PER_COLUMN], U16, name="pos2_sb")
         w_scale_sb = keep.tile([P, E * PASSES * N], U8, name="w_scale_sb", align_bytes=64)
         windows = [
-            keep.tile([P, (POOL_FIRST if i // PACK == POOL_PASS else OWN) * C + SPARE], F32, name=f"window_{i}")
+            keep.tile([P, max(T, max(FED[i // PACK], OWN[i // PACK]) * C if i // PACK < SHARED else max(POOL_FIRST, E - POOL_FIRST) * C) + SPARE], F32, name=f"window_{i}")
             for i in range(PASSES * PACK)
         ]
         nc.gpsimd.memset(w_scale_sb[:].bitcast(I32), 0)
@@ -88,13 +88,11 @@ def tile_moe_pre_lin_bias_kernel(tc, xT, w_words, w_scales, b, gate, offs, pos1,
         load_plane(0)
         load_gate(*GATE_PIECES[0])
         load_gate(*GATE_PIECES[1])
-        for a in (0, 1, POOL_PASS, SHARED - 1, LAST_PASS):
+        for a in range(PASSES):
             for i in range(max(1, a * PACK), (a + 1) * PACK):
                 load_plane(i)
-        load_gate(*GATE_PIECES[2])
-        gate_columns = keep.tile([P, GATE_BANKS * PER_BANK], F32, name="gate_columns")
-        with nc.allow_non_contiguous_dma(reason="one gate value a partition"):
-            nc.sync.dma_start(gate_columns[:], gate[0, slots(0, GATE_BANKS * PER_BANK)].rearrange("(e s) -> s e", s=C))
+            if a == 0:
+                load_gate(*GATE_PIECES[2])
 
         bias = keep.tile([P, E], F32, name="bias")
         rows = w_scales.rearrange("e a q n -> q (e a) n").bitcast(I32)
@@ -114,18 +112,21 @@ def tile_moe_pre_lin_bias_kernel(tc, xT, w_words, w_scales, b, gate, offs, pos1,
 
         y = keep.tile([P, S], F32, name="y")
         banks = [psum.tile([P, BANK_OF.count(i) * C], F32, name=f"bank_{i}") for i in range(max(BANK_OF) + 1)]
-        gated = [keep.tile([P, PACK * OWN * C], F32, name=f"gated_{i}", align_bytes=64) for i in range(2)]
-        pool_place = SHARED * FED
-        woven = keep.tile([P, PACK * (pool_place + POOL_FIRST) * C], BF16, name="woven", align_bytes=64)
+        gated = [keep.tile([P, PACK * max(OWN) * C], F32, name=f"gated_{i}", align_bytes=64) for i in range(2)]
+        woven = keep.tile([P, PACK * (SHARED * E - OWN[0] + POOL_LEFT + POOL_FIRST) * C], BF16, name="woven", align_bytes=64)
 
         identity = keep.tile([P, P], F32, name="identity")
         make_identity(nc, identity[:])
+        gate_columns = keep.tile([P, E], F32, name="gate_columns")
         gate_ps = []
-        for i in range(GATE_BANKS):
-            gate_bank = psum.tile([P, PER_BANK * C], F32, name=f"gate_ps_{i}")
-            for j in range(PER_BANK):
-                e = i * PER_BANK + j
-                nc.tensor.transpose(gate_bank[:, slots(j, 1)], gate_columns[:, e : e + 1].to_broadcast([P, P]), identity[:])
+        for first in range(0, E, PER_BANK):
+            count = min(PER_BANK, E - first)
+            gate_bank = psum.tile([P, count * C], F32, name=f"gate_ps_{first}")
+            for j in range(count):
+                nc.tensor.transpose(gate_bank[:, slots(j, 1)], gate_sb[:, slots(first + j, 1)], identity[:])
+            nc.vector.tensor_copy(gate_columns[:, first : first + count], gate_bank[:, 0 : count * C : C])
+            for j in range(count):
+                nc.tensor.transpose(gate_bank[:, slots(j, 1)], gate_columns[:, first + j : first + j + 1].to_broadcast([P, P]), identity[:])
             gate_ps.append(gate_bank)
 
         def window(a, t, first, count):
@@ -140,11 +141,18 @@ def tile_moe_pre_lin_bias_kernel(tc, xT, w_words, w_scales, b, gate, offs, pos1,
         def by_slot(place, count):
             return room(woven, place, count).rearrange("p (c i t) -> p c t i", t=PACK, i=RUN)
 
-        def gather_times_gate(a, planes):
+        def gather_times_gate():
+            for t in range(PACK):
+                for first, count in GATE_PIECES[:2] if t == 0 else ((FED[0], OWN[0]),):
+                    values = gated[0][:, slots(t * OWN[0] + first - FED[0], count)]
+                    nc.vector.tensor_tensor(values, window(0, t, first, count), gate_sb[:, slots(first, count)], MULT)
+
+        def gather_own(a, planes):
             for t in planes:
-                for first, count in GATE_PIECES[:2] if a == 0 and t == 0 else ((FED, OWN),):
-                    values = gated[a % 2][:, slots(t * OWN + first - FED, count)]
-                    nc.vector.tensor_tensor(values, window(a, t, first, count), gate_sb[:, slots(first, count)], MULT)
+                nc.vector.tensor_copy(gated[a % 2][:, slots(t * OWN[a], OWN[a])], window(a, t, FED[a], OWN[a]))
+
+        def own_values(a):
+            return room(gated[a % 2], 0, OWN[a]).rearrange("p (t s) -> p t s", t=PACK)
 
         def gather(a, first, count, values=None):
             if values is None:
@@ -165,10 +173,7 @@ def tile_moe_pre_lin_bias_kernel(tc, xT, w_words, w_scales, b, gate, offs, pos1,
             for lo in range(first, first + count):
                 if lo == first or lo % PER_BANK == 0:
                     size = min(first + count, (lo // PER_BANK + 1) * PER_BANK) - lo
-                    if lo < GATE_BANKS * PER_BANK:
-                        weight = gate_ps[lo // PER_BANK][:, slots(lo % PER_BANK, size)]
-                    else:
-                        weight = gate_sb[:, slots(lo, size)]
+                    weight = gate_ps[lo // PER_BANK][:, slots(lo % PER_BANK, size)]
                     weight = weight.rearrange("p (c i) -> p c i", i=RUN).unsqueeze(2).to_broadcast([P, size * C // RUN, PACK, RUN])
                     nc.vector.tensor_tensor(by_slot(place + lo - first, size), by_plane(values[:, :, slots(lo - first, size)]), weight, MULT)
 
@@ -207,38 +212,44 @@ def tile_moe_pre_lin_bias_kernel(tc, xT, w_words, w_scales, b, gate, offs, pos1,
             for e in range(first, first + count):
                 nc.scalar.activation(y[:, slots(e, 1)], sums_of(e), IDENTITY, bias=bias[:, e : e + 1])
 
-        fed = []
-        for a in range(SHARED):
-            gather_times_gate(a, range(1))
-            if a > 0:
-                quantise_and_multiply(pool_place, units(a - 1, FED, OWN))
-            gather_times_gate(a, range(1, PACK))
-            if a == SHARED - 1:
-                first_share = gather(POOL_PASS, E - POOL_FIRST, POOL_FIRST)
-            fed.append(gather(a, 0, FED))
-            nc.vector.tensor_copy(by_slot(pool_place, OWN), by_plane(gated[a % 2][:].rearrange("p (t s) -> p t s", t=PACK)))
-        quantise_and_multiply(pool_place, units(SHARED - 1, FED, OWN))
+        gather_times_gate()
+        fed = [gather(a, 0, FED[a]) for a in range(SHARED)]
+        first_share = gather(POOL_PASS, E - POOL_FIRST, POOL_FIRST)
+        nc.vector.tensor_copy(by_slot(1, OWN[0]), by_plane(own_values(0)))
+        gather_own(1, range(1))
+        quantise_and_multiply(1, units(0, FED[0], 3))
+        quantise_and_multiply(4, units(0, FED[0] + 3, OWN[0] - 3))
 
-        pool_weave(E - POOL_FIRST, POOL_FIRST, first_share, pool_place)
         todo = []
-        for a in range(SHARED):
-            vector_weave(0, FED, fed[a], a * FED)
-            todo = todo + units(a, 0, FED)
+        for a in range(2):
+            pool_weave(0, FED[a], fed[a], len(todo))
+            todo = todo + units(a, 0, FED[a])
+        gather_own(1, range(1, PACK))
+        gather_own(2, range(1))
+        vector_weave(FED[1], OWN[1], own_values(1), len(todo))
+        todo = todo + units(1, FED[1], OWN[1])
+        gather_own(2, range(1, PACK))
+        vector_weave(0, FED[2], fed[2], len(todo))
+        vector_weave(FED[2], OWN[2], own_values(2), len(todo) + FED[2])
+        todo = todo + units(2, 0, E)
+        left = gather(POOL_PASS, 0, POOL_LEFT)
+        values = gather(POOL_PASS, POOL_LEFT, POOL_SECOND)
+        vector_weave(0, POOL_LEFT, left, len(todo))
+        todo = todo + units(POOL_PASS, 0, POOL_LEFT)
+        pool_weave(E - POOL_FIRST, POOL_FIRST, first_share, len(todo))
         todo = todo + units(POOL_PASS, E - POOL_FIRST, POOL_FIRST)
         second_place = len(todo) - POOL_SECOND
         quantise_and_multiply(0, todo[:second_place])
         quantise_and_multiply(second_place, todo[second_place:])
 
-        values = gather(POOL_PASS, 0, POOL_LEFT + POOL_SECOND)
-        pool_weave(POOL_LEFT, POOL_SECOND, values[:, :, slots(POOL_LEFT, POOL_SECOND)], second_place)
-        vector_weave(0, POOL_LEFT, values[:, :, slots(0, POOL_LEFT)], second_place - POOL_LEFT)
-        first_place = second_place - POOL_LEFT - PER_BANK
+        pool_weave(POOL_LEFT, POOL_SECOND, values, second_place)
+        first_place = second_place - PER_BANK
         vector_weave(0, 4, gather(LAST_PASS, 0, 4, room(gated[1], 0, 4)), first_place)
         vector_weave(4, 2, gather(LAST_PASS, 4, 2, room(gated[0], 0, 2)), 4)
         vector_weave(6, 2, gather(LAST_PASS, 6, 2, room(gated[0], 2, 2)), 6)
-        quantise_and_multiply(first_place, units(LAST_PASS, 0, 4) + units(POOL_PASS, 0, POOL_LEFT + POOL_SECOND))
+        quantise_and_multiply(first_place, units(LAST_PASS, 0, 4) + units(POOL_PASS, POOL_LEFT, POOL_SECOND))
         add_bias(0, 4)
-        vector_weave(8, 1, gather(LAST_PASS, 8, 1, room(gated[1], 4, 1)), 8)
+        vector_weave(8, 1, gather(LAST_PASS, 8, 1, room(gated[0], 5, 1)), 8)
         quantise_and_multiply(4, units(LAST_PASS, 4, 4))
         add_bias(4, 4)
         vector_weave(9, 1, gather(LAST_PASS, 9, 1, room(gated[0], 4, 1)), 9)

@@ -23,23 +23,18 @@ COPY = mybir.ActivationFunctionType.Copy
 P = 128
 PACK = 4
 PASSES = K // (P * PACK)
-LAST_PASS = PASSES - 1
 PER_COLUMN = 16
 QUADRANT = 32
 RUN = 2
-SPARE = 8
 PER_BANK = 4
+CALL = 8
 
-SHARED = 3
-FED = (5, 5, 4)
-OWN = tuple(E - count for count in FED)
-POOL_PASS = SHARED
-POOL_FIRST = 5
-POOL_SECOND = 3
-POOL_LEFT = E - POOL_FIRST - POOL_SECOND
-GATE_BANKS = 3
-GATE_PIECES = ((FED[0], 2), (FED[0] + 2, OWN[0] - 2), (0, FED[0]))
-BANK_OF = (0, 0, 0, 0, 1, 1, 2, 2, 3, 4)
+OWN = (3, 3, 4, 2, 4)
+FED = tuple(E - count for count in OWN)
+POOL_FIRST = 2
+EARLY = 4
+WINDOW = (904, 904, 904, 648, 704)
+BANK_OF = (1, 1, 1, 2, 3, 4, 0, 0, 0, 0)
 TOKEN_RUN = 160
 
 
@@ -65,10 +60,7 @@ def tile_moe_pre_lin_bias_kernel(tc, xT, w_words, w_scales, b, gate, offs, pos1,
         pos1_sb = keep.tile([P, T // PER_COLUMN], U16, name="pos1_sb")
         pos2_sb = keep.tile([P, T // PER_COLUMN], U16, name="pos2_sb")
         w_scale_sb = keep.tile([P, E * PASSES * N], U8, name="w_scale_sb", align_bytes=64)
-        windows = [
-            keep.tile([P, max(T, max(FED[i // PACK], OWN[i // PACK]) * C if i // PACK < SHARED else max(POOL_FIRST, E - POOL_FIRST) * C) + SPARE], F32, name=f"window_{i}")
-            for i in range(PASSES * PACK)
-        ]
+        windows = [keep.tile([P, WINDOW[i // PACK]], F32, name=f"window_{i}", tag=f"window_{i}", align_bytes=64) for i in range(PASSES * PACK)]
         nc.gpsimd.memset(w_scale_sb[:].bitcast(I32), 0)
 
         warm = keep.tile([P, 2], F32, name="warm")
@@ -77,22 +69,20 @@ def tile_moe_pre_lin_bias_kernel(tc, xT, w_words, w_scales, b, gate, offs, pos1,
 
         x_planes = xT.rearrange("(a p t) c -> a t p c", p=P, t=PACK)
         gate_sb = keep.tile([P, S], F32, name="gate_sb")
-
-        def load_plane(i):
-            nc.sync.dma_start(windows[i][:, :T], x_planes[i // PACK, i % PACK])
+        gate_columns = keep.tile([P, max(FED)], F32, name="gate_columns")
 
         def load_gate(first, count):
             nc.sync.dma_start(gate_sb[:, slots(first, count)], gate[0:P, slots(first, count)])
 
         nc.sync.dma_start(offs_sb[:], offs)
-        load_plane(0)
-        load_gate(*GATE_PIECES[0])
-        load_gate(*GATE_PIECES[1])
-        for a in range(PASSES):
-            for i in range(max(1, a * PACK), (a + 1) * PACK):
-                load_plane(i)
-            if a == 0:
-                load_gate(*GATE_PIECES[2])
+        for i in range(PASSES * PACK):
+            nc.sync.dma_start(windows[i][:, :T], x_planes[i // PACK, i % PACK])
+            if i == PACK - 1:
+                load_gate(FED[0], OWN[0])
+            if i == 2 * PACK - 1:
+                load_gate(POOL_FIRST, FED[0] - POOL_FIRST)
+        with nc.allow_non_contiguous_dma(reason="one gate value a partition"):
+            nc.sync.dma_start(gate_columns[:], gate[0:1, slots(0, max(FED))].rearrange("o (e c) -> c (o e)", c=C))
 
         bias = keep.tile([P, E], F32, name="bias")
         rows = w_scales.rearrange("e a q n -> q (e a) n").bitcast(I32)
@@ -112,54 +102,48 @@ def tile_moe_pre_lin_bias_kernel(tc, xT, w_words, w_scales, b, gate, offs, pos1,
 
         y = keep.tile([P, S], F32, name="y")
         banks = [psum.tile([P, BANK_OF.count(i) * C], F32, name=f"bank_{i}") for i in range(max(BANK_OF) + 1)]
-        gated = [keep.tile([P, PACK * max(OWN) * C], F32, name=f"gated_{i}", align_bytes=64) for i in range(2)]
-        woven = keep.tile([P, PACK * (SHARED * E - OWN[0] + POOL_LEFT + POOL_FIRST) * C], BF16, name="woven", align_bytes=64)
+        block = sum(OWN) + sum(FED[:3]) + EARLY
+        woven = keep.tile([P, PACK * block * C], BF16, name="woven", align_bytes=64)
 
         identity = keep.tile([P, P], F32, name="identity")
         make_identity(nc, identity[:])
-        gate_columns = keep.tile([P, E], F32, name="gate_columns")
         gate_ps = []
-        for first in range(0, E, PER_BANK):
-            count = min(PER_BANK, E - first)
+        for first in range(0, max(FED), PER_BANK):
+            count = min(PER_BANK, max(FED) - first)
             gate_bank = psum.tile([P, count * C], F32, name=f"gate_ps_{first}")
-            for j in range(count):
-                nc.tensor.transpose(gate_bank[:, slots(j, 1)], gate_sb[:, slots(first + j, 1)], identity[:])
-            nc.vector.tensor_copy(gate_columns[:, first : first + count], gate_bank[:, 0 : count * C : C])
             for j in range(count):
                 nc.tensor.transpose(gate_bank[:, slots(j, 1)], gate_columns[:, first + j : first + j + 1].to_broadcast([P, P]), identity[:])
             gate_ps.append(gate_bank)
 
-        def window(a, t, first, count):
-            return windows[a * PACK + t][:].indirect(offs_sb[:, list_columns(first * C, count * C)])
+        def offsets(first, count):
+            return offs_sb[:, list_columns(first * C, count * C)]
 
         def room(tile, place, count):
             return tile[:, slots(PACK * place, PACK * count)]
 
-        def by_plane(values):
-            return values.rearrange("p t (c i) -> p c t i", i=RUN)
-
-        def by_slot(place, count):
-            return room(woven, place, count).rearrange("p (c i t) -> p c t i", t=PACK, i=RUN)
-
-        def gather_times_gate():
+        def gather_own(a):
+            values = keep.tile([P, PACK * OWN[a] * C], F32, name=f"own_{a}", tag=f"own_{a}", align_bytes=64)
+            by_plane = values[:].bitcast(U32).rearrange("p (c t i) -> p t c i", t=PACK, i=RUN)
             for t in range(PACK):
-                for first, count in GATE_PIECES[:2] if t == 0 else ((FED[0], OWN[0]),):
-                    values = gated[0][:, slots(t * OWN[0] + first - FED[0], count)]
-                    nc.vector.tensor_tensor(values, window(0, t, first, count), gate_sb[:, slots(first, count)], MULT)
+                nc.vector.tensor_copy(by_plane[:, t], windows[a * PACK + t][:].bitcast(U32).indirect(offsets(FED[a], OWN[a])))
+            return values[:].rearrange("p (c t i) -> p c i t", t=PACK, i=RUN)
 
-        def gather_own(a, planes):
-            for t in planes:
-                nc.vector.tensor_copy(gated[a % 2][:, slots(t * OWN[a], OWN[a])], window(a, t, FED[a], OWN[a]))
-
-        def own_values(a):
-            return room(gated[a % 2], 0, OWN[a]).rearrange("p (t s) -> p t s", t=PACK)
-
-        def gather(a, first, count, values=None):
-            if values is None:
-                values = keep.tile([P, PACK * count * C], F32, name=f"raw_{a}_{first}", align_bytes=64)[:]
+        def gather(a, first, count, values):
             for t in range(PACK):
-                nc.scalar.activation(values[:, slots(t * count, count)], window(a, t, first, count), COPY)
+                nc.scalar.activation(values[:, slots(t * count, count)], windows[a * PACK + t][:].indirect(offsets(first, count)), COPY)
             return values.rearrange("p (t s) -> p t s", t=PACK)
+
+        def raw(i, count, name):
+            return keep.tile([P, PACK * count * C], F32, name=name, tag=f"raw_{i}", align_bytes=64)
+
+        def pool_weave_own(a, values, place):
+            weight = gate_sb[:, slots(FED[a], OWN[a])].rearrange("p (c i) -> p c i", i=RUN).unsqueeze(3)
+            nc.gpsimd.tensor_tensor(
+                room(woven, place, OWN[a]).rearrange("p (c i t) -> p c i t", t=PACK, i=RUN),
+                values,
+                weight.to_broadcast([P, OWN[a] * C // RUN, RUN, PACK]),
+                MULT,
+            )
 
         def pool_weave(first, count, values, place):
             nc.gpsimd.tensor_tensor(
@@ -175,7 +159,12 @@ def tile_moe_pre_lin_bias_kernel(tc, xT, w_words, w_scales, b, gate, offs, pos1,
                     size = min(first + count, (lo // PER_BANK + 1) * PER_BANK) - lo
                     weight = gate_ps[lo // PER_BANK][:, slots(lo % PER_BANK, size)]
                     weight = weight.rearrange("p (c i) -> p c i", i=RUN).unsqueeze(2).to_broadcast([P, size * C // RUN, PACK, RUN])
-                    nc.vector.tensor_tensor(by_slot(place + lo - first, size), by_plane(values[:, :, slots(lo - first, size)]), weight, MULT)
+                    nc.vector.tensor_tensor(
+                        room(woven, place + lo - first, size).rearrange("p (c i t) -> p c t i", t=PACK, i=RUN),
+                        values[:, :, slots(lo - first, size)].rearrange("p t (c i) -> p c t i", i=RUN),
+                        weight,
+                        MULT,
+                    )
 
         passes_left = [PASSES * BANK_OF.count(i) for i in range(len(banks))]
 
@@ -185,7 +174,7 @@ def tile_moe_pre_lin_bias_kernel(tc, xT, w_words, w_scales, b, gate, offs, pos1,
             passes_left[bank] = passes_left[bank] - 1
             scale_column = (e * PASSES + a) * N
             nc.tensor.matmul_mx(
-                out=banks[bank][:, slots(e - BANK_OF.index(bank), 1)],
+                out=sums_of(e),
                 lhsT=w_codes[a][:, e, :].bitcast(FP8X4),
                 lhsT_scale=w_scale_sb[:, scale_column : scale_column + N],
                 rhs=codes.bitcast(FP8X4),
@@ -194,69 +183,62 @@ def tile_moe_pre_lin_bias_kernel(tc, xT, w_words, w_scales, b, gate, offs, pos1,
                 stop=(passes_left[bank] == 0),
             )
 
-        def quantise_and_multiply(place, todo):
-            while todo:
-                size = max(m for m in (8, 4, 3, 2, 1) if m <= len(todo))
-                name = f"{todo[0][0]}_{todo[0][1]}"
-                codes = keep.tile([P, size * C], U32, name=f"codes_{name}", align_bytes=64)
-                scales = keep.tile([P, size * C], U8, name=f"scales_{name}", align_bytes=64)
-                nc.vector.quantize_mx(out=codes[:].bitcast(FP8X4), scales=scales[:], in_=room(woven, place, size))
-                for j, (a, e) in enumerate(todo[:size]):
-                    multiply(a, e, codes[:, slots(j, 1)], scales[:, slots(j, 1)])
-                place, todo = place + size, todo[size:]
-
         def sums_of(e):
             return banks[BANK_OF[e]][:, slots(e - BANK_OF.index(BANK_OF[e]), 1)]
+
+        def quantise_and_multiply(place, todo, scales, call):
+            codes = keep.tile([P, len(todo) * C], U32, name=f"codes_{call}", tag=f"window_{call}", align_bytes=64)
+            nc.vector.quantize_mx(out=codes[:].bitcast(FP8X4), scales=scales, in_=room(woven, place, len(todo)))
+            for j, (a, e) in enumerate(todo):
+                multiply(a, e, codes[:, slots(j, 1)], scales[:, slots(j, 1)])
 
         def add_bias(first, count):
             for e in range(first, first + count):
                 nc.scalar.activation(y[:, slots(e, 1)], sums_of(e), IDENTITY, bias=bias[:, e : e + 1])
 
-        gather_times_gate()
-        fed = [gather(a, 0, FED[a]) for a in range(SHARED)]
-        first_share = gather(POOL_PASS, E - POOL_FIRST, POOL_FIRST)
-        nc.vector.tensor_copy(by_slot(1, OWN[0]), by_plane(own_values(0)))
-        gather_own(1, range(1))
-        quantise_and_multiply(1, units(0, FED[0], 3))
-        quantise_and_multiply(4, units(0, FED[0] + 3, OWN[0] - 3))
-
+        fed = [gather(a, 0, FED[a], raw(a, FED[a], f"fed_{a}")[:]) for a in range(3)]
         todo = []
-        for a in range(2):
-            pool_weave(0, FED[a], fed[a], len(todo))
+        for a in range(PASSES):
+            pool_weave_own(a, gather_own(a), len(todo))
+            todo = todo + units(a, FED[a], OWN[a])
+            if a == 1:
+                pool_weave(POOL_FIRST, FED[0] - POOL_FIRST, fed[0][:, :, slots(POOL_FIRST, FED[0] - POOL_FIRST)], len(todo))
+                todo = todo + units(0, POOL_FIRST, FED[0] - POOL_FIRST)
+        vector_weave(0, POOL_FIRST, fed[0][:, :, slots(0, POOL_FIRST)], len(todo))
+        todo = todo + units(0, 0, POOL_FIRST)
+        for a in (1, 2):
+            vector_weave(0, FED[a], fed[a], len(todo))
             todo = todo + units(a, 0, FED[a])
-        gather_own(1, range(1, PACK))
-        gather_own(2, range(1))
-        vector_weave(FED[1], OWN[1], own_values(1), len(todo))
-        todo = todo + units(1, FED[1], OWN[1])
-        gather_own(2, range(1, PACK))
-        vector_weave(0, FED[2], fed[2], len(todo))
-        vector_weave(FED[2], OWN[2], own_values(2), len(todo) + FED[2])
-        todo = todo + units(2, 0, E)
-        left = gather(POOL_PASS, 0, POOL_LEFT)
-        values = gather(POOL_PASS, POOL_LEFT, POOL_SECOND)
-        vector_weave(0, POOL_LEFT, left, len(todo))
-        todo = todo + units(POOL_PASS, 0, POOL_LEFT)
-        pool_weave(E - POOL_FIRST, POOL_FIRST, first_share, len(todo))
-        todo = todo + units(POOL_PASS, E - POOL_FIRST, POOL_FIRST)
-        second_place = len(todo) - POOL_SECOND
-        quantise_and_multiply(0, todo[:second_place])
-        quantise_and_multiply(second_place, todo[second_place:])
+        fed_3 = raw(0, FED[3], "fed_3")
+        late = FED[3] - EARLY
+        for first in (late + EARLY // 2, late):
+            vector_weave(first, EARLY // 2, gather(3, first, EARLY // 2, room(fed_3, first, EARLY // 2)), len(todo))
+            todo = todo + units(3, first, EARLY // 2)
+        rest = gather(3, 0, late, room(fed_3, 0, late))
 
-        pool_weave(POOL_LEFT, POOL_SECOND, values, second_place)
-        first_place = second_place - PER_BANK
-        vector_weave(0, 4, gather(LAST_PASS, 0, 4, room(gated[1], 0, 4)), first_place)
-        vector_weave(4, 2, gather(LAST_PASS, 4, 2, room(gated[0], 0, 2)), 4)
-        vector_weave(6, 2, gather(LAST_PASS, 6, 2, room(gated[0], 2, 2)), 6)
-        quantise_and_multiply(first_place, units(LAST_PASS, 0, 4) + units(POOL_PASS, POOL_LEFT, POOL_SECOND))
-        add_bias(0, 4)
-        vector_weave(8, 1, gather(LAST_PASS, 8, 1, room(gated[0], 5, 1)), 8)
-        quantise_and_multiply(4, units(LAST_PASS, 4, 4))
-        add_bias(4, 4)
-        vector_weave(9, 1, gather(LAST_PASS, 9, 1, room(gated[0], 4, 1)), 9)
-        quantise_and_multiply(8, units(LAST_PASS, 8, 1))
-        add_bias(8, 1)
-        quantise_and_multiply(9, units(LAST_PASS, 9, 1))
-        nc.vector.tensor_scalar_add(y[:, slots(E - 1, 1)], sums_of(E - 1), bias[:, E - 1 : E])
+        scales = keep.tile([P, block * C], U8, name="scales", tag="own_4", align_bytes=64)
+        for call in range(block // CALL):
+            quantise_and_multiply(call * CALL, todo[call * CALL : (call + 1) * CALL], scales[:, slots(call * CALL, CALL)], call)
+
+        second = block - CALL
+        pool_weave(POOL_FIRST, late - POOL_FIRST, rest[:, :, slots(POOL_FIRST, late - POOL_FIRST)], second)
+        place = second - POOL_FIRST
+        vector_weave(0, POOL_FIRST, rest[:, :, slots(0, POOL_FIRST)], place)
+        fed_4 = raw(2, FED[4], "fed_4")
+        half = FED[4] // 2
+        vector_weave(0, half, gather(4, 0, half, room(fed_4, 0, half)), 0)
+        last = gather(4, half, half, room(fed_4, half, half))
+        add_bias(FED[4], OWN[4])
+        last_scales = keep.tile([P, (late + FED[4]) * C], U8, name="last_scales", tag="raw_0", align_bytes=64)
+        call = block // CALL
+        quantise_and_multiply(place, units(3, 0, late), last_scales[:, slots(0, late)], call)
+        quantise_and_multiply(0, units(4, 0, half), last_scales[:, slots(late, half)], call + 1)
+        add_bias(0, half)
+        vector_weave(half, half, last, place)
+        quantise_and_multiply(place, units(4, half, 1), last_scales[:, slots(late + half, 1)], call + 2)
+        quantise_and_multiply(place + 1, units(4, half + 1, half - 1), last_scales[:, slots(late + half + 1, half - 1)], call + 3)
+        add_bias(half, half - 1)
+        nc.vector.tensor_scalar_add(y[:, slots(FED[4] - 1, 1)], sums_of(FED[4] - 1), bias[:, FED[4] - 1 : FED[4]])
 
         picked = keep.tile([P, T], F32, name="picked")
         total = keep.tile([P, T], F32, name="total")

@@ -123,10 +123,9 @@ def tile_moe_pre_lin_bias_kernel(tc, xT, w_words, w_scales, b, gate, offs, pos1,
 
         def gather_own(a):
             values = keep.tile([P, PACK * OWN[a] * C], F32, name=f"own_{a}", tag=f"own_{a}", align_bytes=64)
-            by_plane = values[:].bitcast(U32).rearrange("p (c t i) -> p t c i", t=PACK, i=RUN)
             for t in range(PACK):
-                nc.vector.tensor_copy(by_plane[:, t], windows[a * PACK + t][:].bitcast(U32).indirect(offsets(FED[a], OWN[a])))
-            return values[:].rearrange("p (c t i) -> p c i t", t=PACK, i=RUN)
+                nc.vector.tensor_copy(values[:, slots(t * OWN[a], OWN[a])], windows[a * PACK + t][:].indirect(offsets(FED[a], OWN[a])))
+            return values[:].rearrange("p (t s) -> p t s", t=PACK)
 
         def gather(a, first, count, values):
             for t in range(PACK):
@@ -135,15 +134,6 @@ def tile_moe_pre_lin_bias_kernel(tc, xT, w_words, w_scales, b, gate, offs, pos1,
 
         def raw(i, count, name):
             return keep.tile([P, PACK * count * C], F32, name=name, tag=f"raw_{i}", align_bytes=64)
-
-        def pool_weave_own(a, values, place):
-            weight = gate_sb[:, slots(FED[a], OWN[a])].rearrange("p (c i) -> p c i", i=RUN).unsqueeze(3)
-            nc.gpsimd.tensor_tensor(
-                room(woven, place, OWN[a]).rearrange("p (c i t) -> p c i t", t=PACK, i=RUN),
-                values,
-                weight.to_broadcast([P, OWN[a] * C // RUN, RUN, PACK]),
-                MULT,
-            )
 
         def pool_weave(first, count, values, place):
             nc.gpsimd.tensor_tensor(
@@ -199,7 +189,7 @@ def tile_moe_pre_lin_bias_kernel(tc, xT, w_words, w_scales, b, gate, offs, pos1,
         fed = [gather(a, 0, FED[a], raw(a, FED[a], f"fed_{a}")[:]) for a in range(3)]
         todo = []
         for a in range(PASSES):
-            pool_weave_own(a, gather_own(a), len(todo))
+            pool_weave(FED[a], OWN[a], gather_own(a), len(todo))
             todo = todo + units(a, FED[a], OWN[a])
             if a == 1:
                 pool_weave(POOL_FIRST, FED[0] - POOL_FIRST, fed[0][:, :, slots(POOL_FIRST, FED[0] - POOL_FIRST)], len(todo))

@@ -26,6 +26,7 @@ PASSES = K // (P * PACK)
 PER_COLUMN = 16
 QUADRANT = 32
 RUN = 2
+LINE = 4
 PER_BANK = 4
 CALL = 8
 
@@ -137,9 +138,9 @@ def tile_moe_pre_lin_bias_kernel(tc, xT, w_words, w_scales, b, gate, offs, pos1,
 
         def pool_weave(first, count, values, place):
             nc.gpsimd.tensor_tensor(
-                room(woven, place, count).rearrange("p (s t) -> p s t", t=PACK),
-                values.rearrange("p t s -> p s t"),
-                gate_sb[:, slots(first, count)].unsqueeze(2).to_broadcast([P, count * C, PACK]),
+                room(woven, place, count).rearrange("p (c i t) -> p c t i", t=PACK, i=LINE),
+                values.rearrange("p t (c i) -> p c t i", i=LINE),
+                gate_sb[:, slots(first, count)].rearrange("p (c i) -> p c i", i=LINE).unsqueeze(2).to_broadcast([P, count * C // LINE, PACK, LINE]),
                 MULT,
             )
 

@@ -30,10 +30,10 @@ LINE = 4
 PER_BANK = 4
 CALL = 8
 
-OWN = (3, 3, 4, 2, 4)
+OWN = (3, 3, 4, 3, 4)
 FED = tuple(E - count for count in OWN)
-POOL_FIRST = 2
-EARLY = 4
+POOL_SECOND = 2
+EARLY = 3
 WINDOW = (904, 904, 904, 648, 704)
 BANK_OF = (1, 1, 1, 2, 3, 4, 0, 0, 0, 0)
 TOKEN_RUN = 160
@@ -81,9 +81,10 @@ def tile_moe_pre_lin_bias_kernel(tc, xT, w_words, w_scales, b, gate, offs, pos1,
             if i == PACK - 1:
                 load_gate(FED[0], OWN[0])
             if i == 2 * PACK - 1:
-                load_gate(POOL_FIRST, FED[0] - POOL_FIRST)
-        with nc.allow_non_contiguous_dma(reason="one gate value a partition"):
-            nc.sync.dma_start(gate_columns[:], gate[0:1, slots(0, max(FED))].rearrange("o (e c) -> c (o e)", c=C))
+                load_gate(0, FED[0])
+            if i == 4 * PACK - 1:
+                with nc.allow_non_contiguous_dma(reason="one gate value a partition"):
+                    nc.sync.dma_start(gate_columns[:], gate[0:1, slots(0, max(FED))].rearrange("o (e c) -> c (o e)", c=C))
 
         bias = keep.tile([P, E], F32, name="bias")
         rows = w_scales.rearrange("e a q n -> q (e a) n").bitcast(I32)
@@ -193,18 +194,15 @@ def tile_moe_pre_lin_bias_kernel(tc, xT, w_words, w_scales, b, gate, offs, pos1,
             pool_weave(FED[a], OWN[a], gather_own(a), len(todo))
             todo = todo + units(a, FED[a], OWN[a])
             if a == 1:
-                pool_weave(POOL_FIRST, FED[0] - POOL_FIRST, fed[0][:, :, slots(POOL_FIRST, FED[0] - POOL_FIRST)], len(todo))
-                todo = todo + units(0, POOL_FIRST, FED[0] - POOL_FIRST)
-        vector_weave(0, POOL_FIRST, fed[0][:, :, slots(0, POOL_FIRST)], len(todo))
-        todo = todo + units(0, 0, POOL_FIRST)
+                pool_weave(0, FED[0], fed[0], len(todo))
+                todo = todo + units(0, 0, FED[0])
         for a in (1, 2):
             vector_weave(0, FED[a], fed[a], len(todo))
             todo = todo + units(a, 0, FED[a])
         fed_3 = raw(0, FED[3], "fed_3")
         late = FED[3] - EARLY
-        for first in (late + EARLY // 2, late):
-            vector_weave(first, EARLY // 2, gather(3, first, EARLY // 2, room(fed_3, first, EARLY // 2)), len(todo))
-            todo = todo + units(3, first, EARLY // 2)
+        vector_weave(late, EARLY, gather(3, late, EARLY, room(fed_3, late, EARLY)), len(todo))
+        todo = todo + units(3, late, EARLY)
         rest = gather(3, 0, late, room(fed_3, 0, late))
 
         scales = keep.tile([P, block * C], U8, name="scales", tag="own_4", align_bytes=64)
@@ -212,9 +210,10 @@ def tile_moe_pre_lin_bias_kernel(tc, xT, w_words, w_scales, b, gate, offs, pos1,
             quantise_and_multiply(call * CALL, todo[call * CALL : (call + 1) * CALL], scales[:, slots(call * CALL, CALL)], call)
 
         second = block - CALL
-        pool_weave(POOL_FIRST, late - POOL_FIRST, rest[:, :, slots(POOL_FIRST, late - POOL_FIRST)], second)
-        place = second - POOL_FIRST
-        vector_weave(0, POOL_FIRST, rest[:, :, slots(0, POOL_FIRST)], place)
+        left = late - POOL_SECOND
+        pool_weave(left, POOL_SECOND, rest[:, :, slots(left, POOL_SECOND)], second)
+        place = second - left
+        vector_weave(0, left, rest[:, :, slots(0, left)], place)
         fed_4 = raw(2, FED[4], "fed_4")
         half = FED[4] // 2
         vector_weave(0, half, gather(4, 0, half, room(fed_4, 0, half)), 0)

@@ -32,11 +32,14 @@ CALL = 8
 
 OWN = (3, 3, 4, 3, 4)
 FED = tuple(E - count for count in OWN)
-POOL_SECOND = 2
-EARLY = 3
-WINDOW = (904, 904, 904, 648, 704)
-BANK_OF = (1, 1, 1, 2, 3, 4, 0, 0, 0, 0)
-TOKEN_RUN = 160
+VECTOR_FIRST = 320
+POOL_SECOND = 3
+LAST_CHUNKS = (2, 2, 1, 1)
+WINDOW = (904, 904, 776, 904, 704)
+BANK_OF = (1, 1, 2, 2, 3, 4, 0, 0, 0, 0)
+FIRST_RUN = (0, 96)
+VECTOR_RUN = (96, 160)
+LATER_RUNS = ((256, 224), (480, 160))
 
 
 def slots(first, count):
@@ -72,19 +75,18 @@ def tile_moe_pre_lin_bias_kernel(tc, xT, w_words, w_scales, b, gate, offs, pos1,
         gate_sb = keep.tile([P, S], F32, name="gate_sb")
         gate_columns = keep.tile([P, max(FED)], F32, name="gate_columns")
 
-        def load_gate(first, count):
-            nc.sync.dma_start(gate_sb[:, slots(first, count)], gate[0:P, slots(first, count)])
+        def load_gate(first_slot, end_slot):
+            nc.sync.dma_start(gate_sb[:, first_slot:end_slot], gate[0:P, first_slot:end_slot])
 
         nc.sync.dma_start(offs_sb[:], offs)
         for i in range(PASSES * PACK):
             nc.sync.dma_start(windows[i][:, :T], x_planes[i // PACK, i % PACK])
             if i == PACK - 1:
-                load_gate(FED[0], OWN[0])
+                load_gate(FED[0] * C, S)
             if i == 2 * PACK - 1:
-                load_gate(0, FED[0])
-            if i == 4 * PACK - 1:
-                with nc.allow_non_contiguous_dma(reason="one gate value a partition"):
-                    nc.sync.dma_start(gate_columns[:], gate[0:1, slots(0, max(FED))].rearrange("o (e c) -> c (o e)", c=C))
+                load_gate(VECTOR_FIRST, FED[0] * C)
+        with nc.allow_non_contiguous_dma(reason="one gate value a partition"):
+            nc.sync.dma_start(gate_columns[:], gate[0:1, slots(0, max(FED))].rearrange("o (e c) -> c (o e)", c=C))
 
         bias = keep.tile([P, E], F32, name="bias")
         rows = w_scales.rearrange("e a q n -> q (e a) n").bitcast(I32)
@@ -104,7 +106,7 @@ def tile_moe_pre_lin_bias_kernel(tc, xT, w_words, w_scales, b, gate, offs, pos1,
 
         y = keep.tile([P, S], F32, name="y")
         banks = [psum.tile([P, BANK_OF.count(i) * C], F32, name=f"bank_{i}") for i in range(max(BANK_OF) + 1)]
-        block = sum(OWN) + sum(FED[:3]) + EARLY
+        block = sum(OWN) + sum(FED[:3])
         woven = keep.tile([P, PACK * block * C], BF16, name="woven", align_bytes=64)
 
         identity = keep.tile([P, P], F32, name="identity")
@@ -137,26 +139,31 @@ def tile_moe_pre_lin_bias_kernel(tc, xT, w_words, w_scales, b, gate, offs, pos1,
         def raw(i, count, name):
             return keep.tile([P, PACK * count * C], F32, name=name, tag=f"raw_{i}", align_bytes=64)
 
-        def pool_weave(first, count, values, place):
+        def words(first_slot, count):
+            return woven[:, PACK * first_slot : PACK * (first_slot + count)]
+
+        def pool_weave(first_slot, count, values, place):
+            weight = gate_sb[:, first_slot : first_slot + count].rearrange("p (c i) -> p c i", i=LINE)
             nc.gpsimd.tensor_tensor(
-                room(woven, place, count).rearrange("p (c i t) -> p c t i", t=PACK, i=LINE),
+                words(place, count).rearrange("p (c i t) -> p c t i", t=PACK, i=LINE),
                 values.rearrange("p t (c i) -> p c t i", i=LINE),
-                gate_sb[:, slots(first, count)].rearrange("p (c i) -> p c i", i=LINE).unsqueeze(2).to_broadcast([P, count * C // LINE, PACK, LINE]),
+                weight.unsqueeze(2).to_broadcast([P, count // LINE, PACK, LINE]),
                 MULT,
             )
 
-        def vector_weave(first, count, values, place):
-            for lo in range(first, first + count):
-                if lo == first or lo % PER_BANK == 0:
-                    size = min(first + count, (lo // PER_BANK + 1) * PER_BANK) - lo
-                    weight = gate_ps[lo // PER_BANK][:, slots(lo % PER_BANK, size)]
-                    weight = weight.rearrange("p (c i) -> p c i", i=RUN).unsqueeze(2).to_broadcast([P, size * C // RUN, PACK, RUN])
-                    nc.vector.tensor_tensor(
-                        room(woven, place + lo - first, size).rearrange("p (c i t) -> p c t i", t=PACK, i=RUN),
-                        values[:, :, slots(lo - first, size)].rearrange("p t (c i) -> p c t i", i=RUN),
-                        weight,
-                        MULT,
-                    )
+        def vector_weave(first_slot, count, values, place):
+            bank_slots = PER_BANK * C
+            for bank in range(first_slot // bank_slots, (first_slot + count - 1) // bank_slots + 1):
+                lo = max(first_slot, bank * bank_slots)
+                size = min(first_slot + count, (bank + 1) * bank_slots) - lo
+                weight = gate_ps[bank][:, lo - bank * bank_slots : lo - bank * bank_slots + size]
+                weight = weight.rearrange("p (c i) -> p c i", i=RUN).unsqueeze(2).to_broadcast([P, size // RUN, PACK, RUN])
+                nc.vector.tensor_tensor(
+                    words(place + lo - first_slot, size).rearrange("p (c i t) -> p c t i", t=PACK, i=RUN),
+                    values[:, :, lo - first_slot : lo - first_slot + size].rearrange("p t (c i) -> p c t i", i=RUN),
+                    weight,
+                    MULT,
+                )
 
         passes_left = [PASSES * BANK_OF.count(i) for i in range(len(banks))]
 
@@ -191,52 +198,78 @@ def tile_moe_pre_lin_bias_kernel(tc, xT, w_words, w_scales, b, gate, offs, pos1,
         fed = [gather(a, 0, FED[a], raw(a, FED[a], f"fed_{a}")[:]) for a in range(3)]
         todo = []
         for a in range(PASSES):
-            pool_weave(FED[a], OWN[a], gather_own(a), len(todo))
+            pool_weave(FED[a] * C, OWN[a] * C, gather_own(a), len(todo) * C)
             todo = todo + units(a, FED[a], OWN[a])
             if a == 1:
-                pool_weave(0, FED[0], fed[0], len(todo))
+                shared = len(todo) * C
+                pool_weave(VECTOR_FIRST, FED[0] * C - VECTOR_FIRST, fed[0][:, :, VECTOR_FIRST:], shared + VECTOR_FIRST)
                 todo = todo + units(0, 0, FED[0])
+        vector_weave(0, VECTOR_FIRST, fed[0][:, :, :VECTOR_FIRST], shared)
         for a in (1, 2):
-            vector_weave(0, FED[a], fed[a], len(todo))
+            vector_weave(0, FED[a] * C, fed[a], len(todo) * C)
             todo = todo + units(a, 0, FED[a])
-        fed_3 = raw(0, FED[3], "fed_3")
-        late = FED[3] - EARLY
-        vector_weave(late, EARLY, gather(3, late, EARLY, room(fed_3, late, EARLY)), len(todo))
-        todo = todo + units(3, late, EARLY)
-        rest = gather(3, 0, late, room(fed_3, 0, late))
+        fed_3 = gather(3, 0, FED[3], raw(0, FED[3], "fed_3")[:])
+        fed_4 = raw(2, FED[4], "fed_4")
+        chunks = []
+        first = 0
+        for count in LAST_CHUNKS:
+            chunks.append((first, count, gather(4, first, count, room(fed_4, first, count))))
+            first = first + count
+
+        def quantise_run(place, todo, widths, scales, call):
+            done = 0
+            for j, width in enumerate(widths):
+                quantise_and_multiply(place + done, todo[done : done + width], scales[:, slots(done, width)], call + j)
+                done = done + width
 
         scales = keep.tile([P, block * C], U8, name="scales", tag="own_4", align_bytes=64)
-        for call in range(block // CALL):
-            quantise_and_multiply(call * CALL, todo[call * CALL : (call + 1) * CALL], scales[:, slots(call * CALL, CALL)], call)
+        widths = (CALL, CALL, CALL, CALL, 1, 4)
+        quantise_run(0, todo, widths, scales, 0)
+        call = len(widths)
 
-        second = block - CALL
-        left = late - POOL_SECOND
-        pool_weave(left, POOL_SECOND, rest[:, :, slots(left, POOL_SECOND)], second)
-        place = second - left
-        vector_weave(0, left, rest[:, :, slots(0, left)], place)
-        fed_4 = raw(2, FED[4], "fed_4")
-        half = FED[4] // 2
-        vector_weave(0, half, gather(4, 0, half, room(fed_4, 0, half)), 0)
-        last = gather(4, half, half, room(fed_4, half, half))
+        left = FED[3] - POOL_SECOND
+        second = block - widths[-1]
+        pool_weave(left * C, POOL_SECOND * C, fed_3[:, :, left * C :], second * C)
+        vector_weave(0, left * C, fed_3[:, :, : left * C], (second - left) * C)
+        first, count, values = chunks[0]
+        place = second - left - count
+        vector_weave(first * C, count * C, values, place * C)
+        todo = units(4, first, count) + units(3, 0, FED[3])
+        last_scales = keep.tile([P, (FED[3] + FED[4]) * C], U8, name="last_scales", tag="raw_0", align_bytes=64)
+        extra = len(todo) - CALL
+        quantise_and_multiply(place + extra, todo[extra:], last_scales[:, slots(extra, CALL)], call)
+        quantise_and_multiply(place, todo[:extra], last_scales[:, slots(0, extra)], call + 1)
         add_bias(FED[4], OWN[4])
-        last_scales = keep.tile([P, (late + FED[4]) * C], U8, name="last_scales", tag="raw_0", align_bytes=64)
-        call = block // CALL
-        quantise_and_multiply(place, units(3, 0, late), last_scales[:, slots(0, late)], call)
-        quantise_and_multiply(0, units(4, 0, half), last_scales[:, slots(late, half)], call + 1)
-        add_bias(0, half)
-        vector_weave(half, half, last, place)
-        quantise_and_multiply(place, units(4, half, 1), last_scales[:, slots(late + half, 1)], call + 2)
-        quantise_and_multiply(place + 1, units(4, half + 1, half - 1), last_scales[:, slots(late + half + 1, half - 1)], call + 3)
-        add_bias(half, half - 1)
-        nc.vector.tensor_scalar_add(y[:, slots(FED[4] - 1, 1)], sums_of(FED[4] - 1), bias[:, FED[4] - 1 : FED[4]])
+        add_bias(first, count)
+
+        place = place + extra
+        for first, count, values in chunks[1:3]:
+            vector_weave(first * C, count * C, values, (place + first) * C)
+        first, count, values = chunks[1]
+        quantise_and_multiply(place + first, units(4, first, count), last_scales[:, slots(FED[3] + first, count)], call + 2)
+        add_bias(first, count)
+        final, count, values = chunks[3]
+        vector_weave(final * C, count * C, values, (place + final) * C)
+        quantise_and_multiply(place + final - 1, units(4, final - 1, 2), last_scales[:, slots(FED[3] + final - 1, 2)], call + 3)
+        add_bias(final - 1, 1)
+        nc.vector.tensor_scalar_add(y[:, slots(final, 1)], sums_of(final), bias[:, final : final + 1])
 
         picked = keep.tile([P, T], F32, name="picked")
         total = keep.tile([P, T], F32, name="total")
-        last_run = T - TOKEN_RUN
-        for t0 in range(0, T, TOKEN_RUN):
-            run = slice(t0, t0 + TOKEN_RUN)
-            nc.scalar.activation(picked[:, run], y[:].indirect(pos1_sb[:, list_columns(t0, TOKEN_RUN)]), COPY)
-            nc.vector.tensor_tensor(total[:, run], y[:].indirect(pos2_sb[:, list_columns(t0, TOKEN_RUN)]), picked[:, run], ADD)
-            if t0 + TOKEN_RUN == last_run:
-                nc.sync.dma_start(out[:, :last_run], total[:, :last_run])
+
+        def first_results(t0, count):
+            return y[:].indirect(pos1_sb[:, list_columns(t0, count)])
+
+        def add_second(t0, count):
+            nc.vector.tensor_tensor(total[:, t0 : t0 + count], y[:].indirect(pos2_sb[:, list_columns(t0, count)]), picked[:, t0 : t0 + count], ADD)
+
+        for t0, count in (FIRST_RUN,) + LATER_RUNS:
+            nc.scalar.activation(picked[:, t0 : t0 + count], first_results(t0, count), COPY)
+        t0, count = VECTOR_RUN
+        nc.vector.tensor_copy(picked[:, t0 : t0 + count], first_results(t0, count))
+        for t0, count in (FIRST_RUN, VECTOR_RUN, LATER_RUNS[0]):
+            add_second(t0, count)
+        last_run, count = LATER_RUNS[1]
+        nc.sync.dma_start(out[:, :last_run], total[:, :last_run])
+        add_second(last_run, count)
         nc.sync.dma_start(out[:, last_run:], total[:, last_run:])

@@ -33,10 +33,10 @@ CALL = 8
 OWN = (3, 3, 4, 3, 4)
 FED = tuple(E - count for count in OWN)
 VECTOR_FIRST = 320
-POOL_SECOND = 3
-LAST_CHUNKS = (2, 2, 1, 1)
+POOL_SECOND = 352
+LAST_CHUNKS = (3, 2, 1)
 WINDOW = (904, 904, 776, 904, 704)
-BANK_OF = (1, 1, 2, 2, 3, 4, 0, 0, 0, 0)
+BANK_OF = (2, 2, 2, 3, 3, 4, 1, 0, 0, 0)
 FIRST_RUN = (0, 96)
 VECTOR_RUN = (96, 160)
 LATER_RUNS = ((256, 224), (480, 160))
@@ -65,11 +65,11 @@ def tile_moe_pre_lin_bias_kernel(tc, xT, w_words, w_scales, b, gate, offs, pos1,
         pos2_sb = keep.tile([P, T // PER_COLUMN], U16, name="pos2_sb")
         w_scale_sb = keep.tile([P, E * PASSES * N], U8, name="w_scale_sb", align_bytes=64)
         windows = [keep.tile([P, WINDOW[i // PACK]], F32, name=f"window_{i}", tag=f"window_{i}", align_bytes=64) for i in range(PASSES * PACK)]
-        nc.gpsimd.memset(w_scale_sb[:].bitcast(I32), 0)
 
         warm = keep.tile([P, 2], F32, name="warm")
         nc.vector.memset(warm[:, 0:1], 0.0)
         nc.scalar.activation(warm[:, 1:2], warm[:, 0:1], COPY)
+        nc.vector.memset(w_scale_sb[:].bitcast(I32), 0)
 
         x_planes = xT.rearrange("(a p t) c -> a t p c", p=P, t=PACK)
         gate_sb = keep.tile([P, S], F32, name="gate_sb")
@@ -83,7 +83,7 @@ def tile_moe_pre_lin_bias_kernel(tc, xT, w_words, w_scales, b, gate, offs, pos1,
             nc.sync.dma_start(windows[i][:, :T], x_planes[i // PACK, i % PACK])
             if i == PACK - 1:
                 load_gate(FED[0] * C, S)
-            if i == 2 * PACK - 1:
+            if i == 3 * PACK - 2:
                 load_gate(VECTOR_FIRST, FED[0] * C)
         with nc.allow_non_contiguous_dma(reason="one gate value a partition"):
             nc.sync.dma_start(gate_columns[:], gate[0:1, slots(0, max(FED))].rearrange("o (e c) -> c (o e)", c=C))
@@ -227,31 +227,29 @@ def tile_moe_pre_lin_bias_kernel(tc, xT, w_words, w_scales, b, gate, offs, pos1,
         quantise_run(0, todo, widths, scales, 0)
         call = len(widths)
 
-        left = FED[3] - POOL_SECOND
-        second = block - widths[-1]
-        pool_weave(left * C, POOL_SECOND * C, fed_3[:, :, left * C :], second * C)
-        vector_weave(0, left * C, fed_3[:, :, : left * C], (second - left) * C)
+        add_bias(FED[3], OWN[3])
+
+        left = FED[3] * C - POOL_SECOND
+        place_3 = block - 1 - FED[3]
+        pool_weave(left, POOL_SECOND, fed_3[:, :, left:], place_3 * C + left)
+        vector_weave(0, left, fed_3[:, :, :left], place_3 * C)
         first, count, values = chunks[0]
-        place = second - left - count
+        place = place_3 - count
         vector_weave(first * C, count * C, values, place * C)
         todo = units(4, first, count) + units(3, 0, FED[3])
         last_scales = keep.tile([P, (FED[3] + FED[4]) * C], U8, name="last_scales", tag="raw_0", align_bytes=64)
         extra = len(todo) - CALL
         quantise_and_multiply(place + extra, todo[extra:], last_scales[:, slots(extra, CALL)], call)
         quantise_and_multiply(place, todo[:extra], last_scales[:, slots(0, extra)], call + 1)
-        add_bias(FED[4], OWN[4])
+        add_bias(FED[4], FED[3] - FED[4])
         add_bias(first, count)
 
-        place = place + extra
-        for first, count, values in chunks[1:3]:
+        for first, count, values in chunks[1:]:
             vector_weave(first * C, count * C, values, (place + first) * C)
-        first, count, values = chunks[1]
-        quantise_and_multiply(place + first, units(4, first, count), last_scales[:, slots(FED[3] + first, count)], call + 2)
-        add_bias(first, count)
-        final, count, values = chunks[3]
-        vector_weave(final * C, count * C, values, (place + final) * C)
-        quantise_and_multiply(place + final - 1, units(4, final - 1, 2), last_scales[:, slots(FED[3] + final - 1, 2)], call + 3)
-        add_bias(final - 1, 1)
+        for j, (first, count, values) in enumerate(chunks[1:]):
+            quantise_and_multiply(place + first, units(4, first, count), last_scales[:, slots(FED[3] + first, count)], call + 2 + j)
+        add_bias(chunks[1][0], chunks[1][1])
+        final = FED[4] - 1
         nc.vector.tensor_scalar_add(y[:, slots(final, 1)], sums_of(final), bias[:, final : final + 1])
 
         picked = keep.tile([P, T], F32, name="picked")

@@ -30,13 +30,14 @@ LINE = 4
 PER_BANK = 4
 CALL = 8
 
-OWN = (3, 3, 4, 3, 4)
-FED = tuple(E - count for count in OWN)
-VECTOR_FIRST = 320
-POOL_SECOND = 352
+OWN = (384, 384, 544, 384, 512)
+FED = tuple(S - count for count in OWN)
+VECTOR_FIRST = 288
+SECOND_SHARE = 3
 LAST_CHUNKS = (3, 2, 1)
+BLOCK_CALLS = ((0, 8), (8, 8), (16, 8), (36, 1), (32, 4), (24, 8))
 WINDOW = (904, 904, 776, 904, 704)
-BANK_OF = (2, 2, 2, 3, 3, 4, 1, 0, 0, 0)
+BANK_OF = (2, 2, 2, 5, 3, 4, 1, 0, 0, 0)
 FIRST_RUN = (0, 96)
 VECTOR_RUN = (96, 160)
 LATER_RUNS = ((256, 224), (480, 160))
@@ -73,7 +74,7 @@ def tile_moe_pre_lin_bias_kernel(tc, xT, w_words, w_scales, b, gate, offs, pos1,
 
         x_planes = xT.rearrange("(a p t) c -> a t p c", p=P, t=PACK)
         gate_sb = keep.tile([P, S], F32, name="gate_sb")
-        gate_columns = keep.tile([P, max(FED)], F32, name="gate_columns")
+        gate_columns = keep.tile([P, max(FED) // C], F32, name="gate_columns")
 
         def load_gate(first_slot, end_slot):
             nc.sync.dma_start(gate_sb[:, first_slot:end_slot], gate[0:P, first_slot:end_slot])
@@ -82,11 +83,11 @@ def tile_moe_pre_lin_bias_kernel(tc, xT, w_words, w_scales, b, gate, offs, pos1,
         for i in range(PASSES * PACK):
             nc.sync.dma_start(windows[i][:, :T], x_planes[i // PACK, i % PACK])
             if i == PACK - 1:
-                load_gate(FED[0] * C, S)
+                load_gate(FED[0], S)
             if i == 3 * PACK - 2:
-                load_gate(VECTOR_FIRST, FED[0] * C)
+                load_gate(VECTOR_FIRST, FED[0])
         with nc.allow_non_contiguous_dma(reason="one gate value a partition"):
-            nc.sync.dma_start(gate_columns[:], gate[0:1, slots(0, max(FED))].rearrange("o (e c) -> c (o e)", c=C))
+            nc.sync.dma_start(gate_columns[:], gate[0:1, : max(FED)].rearrange("o (e c) -> c (o e)", c=C))
 
         bias = keep.tile([P, E], F32, name="bias")
         rows = w_scales.rearrange("e a q n -> q (e a) n").bitcast(I32)
@@ -106,38 +107,35 @@ def tile_moe_pre_lin_bias_kernel(tc, xT, w_words, w_scales, b, gate, offs, pos1,
 
         y = keep.tile([P, S], F32, name="y")
         banks = [psum.tile([P, BANK_OF.count(i) * C], F32, name=f"bank_{i}") for i in range(max(BANK_OF) + 1)]
-        block = sum(OWN) + sum(FED[:3])
+        block = 3 * E + (OWN[3] + OWN[4]) // C
         woven = keep.tile([P, PACK * block * C], BF16, name="woven", align_bytes=64)
 
         identity = keep.tile([P, P], F32, name="identity")
         make_identity(nc, identity[:])
         gate_ps = []
-        for first in range(0, max(FED), PER_BANK):
-            count = min(PER_BANK, max(FED) - first)
+        for first in range(0, max(FED) // C, PER_BANK):
+            count = min(PER_BANK, max(FED) // C - first)
             gate_bank = psum.tile([P, count * C], F32, name=f"gate_ps_{first}")
             for j in range(count):
                 nc.tensor.transpose(gate_bank[:, slots(j, 1)], gate_columns[:, first + j : first + j + 1].to_broadcast([P, P]), identity[:])
             gate_ps.append(gate_bank)
 
-        def offsets(first, count):
-            return offs_sb[:, list_columns(first * C, count * C)]
-
-        def room(tile, place, count):
-            return tile[:, slots(PACK * place, PACK * count)]
+        def offsets(first_slot, count):
+            return offs_sb[:, list_columns(first_slot, count)]
 
         def gather_own(a):
-            values = keep.tile([P, PACK * OWN[a] * C], F32, name=f"own_{a}", tag=f"own_{a}", align_bytes=64)
+            values = keep.tile([P, PACK * OWN[a]], F32, name=f"own_{a}", tag=f"own_{a}", align_bytes=64)
             for t in range(PACK):
-                nc.vector.tensor_copy(values[:, slots(t * OWN[a], OWN[a])], windows[a * PACK + t][:].indirect(offsets(FED[a], OWN[a])))
+                nc.vector.tensor_copy(values[:, t * OWN[a] : (t + 1) * OWN[a]], windows[a * PACK + t][:].indirect(offsets(FED[a], OWN[a])))
             return values[:].rearrange("p (t s) -> p t s", t=PACK)
 
-        def gather(a, first, count, values):
+        def gather(a, first_slot, count, values):
             for t in range(PACK):
-                nc.scalar.activation(values[:, slots(t * count, count)], windows[a * PACK + t][:].indirect(offsets(first, count)), COPY)
+                nc.scalar.activation(values[:, t * count : (t + 1) * count], windows[a * PACK + t][:].indirect(offsets(first_slot, count)), COPY)
             return values.rearrange("p (t s) -> p t s", t=PACK)
 
         def raw(i, count, name):
-            return keep.tile([P, PACK * count * C], F32, name=name, tag=f"raw_{i}", align_bytes=64)
+            return keep.tile([P, PACK * count], F32, name=name, tag=f"raw_{i}", align_bytes=64)
 
         def words(first_slot, count):
             return woven[:, PACK * first_slot : PACK * (first_slot + count)]
@@ -187,7 +185,7 @@ def tile_moe_pre_lin_bias_kernel(tc, xT, w_words, w_scales, b, gate, offs, pos1,
 
         def quantise_and_multiply(place, todo, scales, call):
             codes = keep.tile([P, len(todo) * C], U32, name=f"codes_{call}", tag=f"window_{call}", align_bytes=64)
-            nc.vector.quantize_mx(out=codes[:].bitcast(FP8X4), scales=scales, in_=room(woven, place, len(todo)))
+            nc.vector.quantize_mx(out=codes[:].bitcast(FP8X4), scales=scales, in_=words(place * C, len(todo) * C))
             for j, (a, e) in enumerate(todo):
                 multiply(a, e, codes[:, slots(j, 1)], scales[:, slots(j, 1)])
 
@@ -196,61 +194,55 @@ def tile_moe_pre_lin_bias_kernel(tc, xT, w_words, w_scales, b, gate, offs, pos1,
                 nc.scalar.activation(y[:, slots(e, 1)], sums_of(e), IDENTITY, bias=bias[:, e : e + 1])
 
         fed = [gather(a, 0, FED[a], raw(a, FED[a], f"fed_{a}")[:]) for a in range(3)]
-        todo = []
+        own_place = [FED[0], S + FED[1], 2 * S + FED[2], 3 * S, 3 * S + OWN[3]]
         for a in range(PASSES):
-            pool_weave(FED[a] * C, OWN[a] * C, gather_own(a), len(todo) * C)
-            todo = todo + units(a, FED[a], OWN[a])
+            pool_weave(FED[a], OWN[a], gather_own(a), own_place[a])
             if a == 1:
-                shared = len(todo) * C
-                pool_weave(VECTOR_FIRST, FED[0] * C - VECTOR_FIRST, fed[0][:, :, VECTOR_FIRST:], shared + VECTOR_FIRST)
-                todo = todo + units(0, 0, FED[0])
-        vector_weave(0, VECTOR_FIRST, fed[0][:, :, :VECTOR_FIRST], shared)
+                pool_weave(VECTOR_FIRST, FED[0] - VECTOR_FIRST, fed[0][:, :, VECTOR_FIRST:], VECTOR_FIRST)
+        vector_weave(0, VECTOR_FIRST, fed[0][:, :, :VECTOR_FIRST], 0)
         for a in (1, 2):
-            vector_weave(0, FED[a] * C, fed[a], len(todo) * C)
-            todo = todo + units(a, 0, FED[a])
+            vector_weave(0, FED[a], fed[a], a * S)
         fed_3 = gather(3, 0, FED[3], raw(0, FED[3], "fed_3")[:])
         fed_4 = raw(2, FED[4], "fed_4")
         chunks = []
         first = 0
         for count in LAST_CHUNKS:
-            chunks.append((first, count, gather(4, first, count, room(fed_4, first, count))))
+            chunks.append(gather(4, first * C, count * C, fed_4[:, slots(PACK * first, PACK * count)]))
             first = first + count
 
-        def quantise_run(place, todo, widths, scales, call):
-            done = 0
-            for j, width in enumerate(widths):
-                quantise_and_multiply(place + done, todo[done : done + width], scales[:, slots(done, width)], call + j)
-                done = done + width
-
+        todo = units(0, 0, E) + units(1, 0, E) + units(2, 0, E)
+        for a in (3, 4):
+            todo = todo + units(a, FED[a] // C, OWN[a] // C)
+        first_scales = keep.tile([P, CALL * C], U8, name="first_scales", tag="own_3", align_bytes=64)
         scales = keep.tile([P, block * C], U8, name="scales", tag="own_4", align_bytes=64)
-        widths = (CALL, CALL, CALL, CALL, 1, 4)
-        quantise_run(0, todo, widths, scales, 0)
-        call = len(widths)
+        for call, (place, count) in enumerate(BLOCK_CALLS):
+            plane = first_scales if call == 0 else scales
+            quantise_and_multiply(place, todo[place : place + count], plane[:, slots(place, count)], call)
+        call = len(BLOCK_CALLS)
+        add_bias(FED[3] // C, OWN[3] // C)
 
-        add_bias(FED[3], OWN[3])
+        pool_place = BLOCK_CALLS[-2][0]
+        free_place = BLOCK_CALLS[2][0]
+        left = FED[3] // C - SECOND_SHARE
+        early = LAST_CHUNKS[0]
+        pool_weave(left * C, SECOND_SHARE * C, fed_3[:, :, left * C :], pool_place * C)
+        vector_weave(0, left * C, fed_3[:, :, : left * C], (free_place + early) * C)
+        vector_weave(0, early * C, chunks[0], free_place * C)
+        free_scales = keep.tile([P, left * C], U8, name="free_scales", align_bytes=64)
+        last_scales = keep.tile([P, (SECOND_SHARE + FED[4] // C) * C], U8, name="last_scales", tag="raw_0", align_bytes=64)
+        quantise_and_multiply(free_place + early, units(3, 0, left), free_scales[:], call)
+        quantise_and_multiply(pool_place, units(3, left, SECOND_SHARE), last_scales[:, slots(0, SECOND_SHARE)], call + 1)
+        quantise_and_multiply(free_place, units(4, 0, early), last_scales[:, slots(SECOND_SHARE, early)], call + 2)
+        add_bias(FED[4] // C, (FED[3] - FED[4]) // C)
+        add_bias(0, early)
 
-        left = FED[3] * C - POOL_SECOND
-        place_3 = block - 1 - FED[3]
-        pool_weave(left, POOL_SECOND, fed_3[:, :, left:], place_3 * C + left)
-        vector_weave(0, left, fed_3[:, :, :left], place_3 * C)
-        first, count, values = chunks[0]
-        place = place_3 - count
-        vector_weave(first * C, count * C, values, place * C)
-        todo = units(4, first, count) + units(3, 0, FED[3])
-        last_scales = keep.tile([P, (FED[3] + FED[4]) * C], U8, name="last_scales", tag="raw_0", align_bytes=64)
-        extra = len(todo) - CALL
-        quantise_and_multiply(place + extra, todo[extra:], last_scales[:, slots(extra, CALL)], call)
-        quantise_and_multiply(place, todo[:extra], last_scales[:, slots(0, extra)], call + 1)
-        add_bias(FED[4], FED[3] - FED[4])
-        add_bias(first, count)
-
-        for first, count, values in chunks[1:]:
-            vector_weave(first * C, count * C, values, (place + first) * C)
-        for j, (first, count, values) in enumerate(chunks[1:]):
-            quantise_and_multiply(place + first, units(4, first, count), last_scales[:, slots(FED[3] + first, count)], call + 2 + j)
-        add_bias(chunks[1][0], chunks[1][1])
-        final = FED[4] - 1
-        nc.vector.tensor_scalar_add(y[:, slots(final, 1)], sums_of(final), bias[:, final : final + 1])
+        pool_weave(early * C, C, chunks[1][:, :, :C], pool_place * C)
+        vector_weave((early + 1) * C, C, chunks[1][:, :, C:], (pool_place + 1) * C)
+        vector_weave((early + 2) * C, C, chunks[2], (pool_place + 2) * C)
+        for j in (1, 2, 0):
+            quantise_and_multiply(pool_place + j, units(4, early + j, 1), last_scales[:, slots(SECOND_SHARE + early + j, 1)], call + 3 + j)
+        add_bias(early + 1, 2)
+        nc.vector.tensor_scalar_add(y[:, slots(early, 1)], sums_of(early), bias[:, early : early + 1])
 
         picked = keep.tile([P, T], F32, name="picked")
         total = keep.tile([P, T], F32, name="total")

@@ -38,8 +38,8 @@ LAST_CHUNKS = (3, 2, 1)
 BLOCK_CALLS = ((0, 8), (8, 8), (16, 8), (36, 1), (32, 4), (24, 8))
 WINDOW = (904, 904, 776, 904, 704)
 BANK_OF = (2, 2, 2, 5, 3, 4, 1, 0, 0, 0)
-FIRST_RUN = (0, 96)
-VECTOR_RUN = (96, 160)
+FIRST_RUN = (0, 64)
+VECTOR_RUN = (64, 192)
 LATER_RUNS = ((256, 224), (480, 160))
 
 
@@ -81,7 +81,8 @@ def tile_moe_pre_lin_bias_kernel(tc, xT, w_words, w_scales, b, gate, offs, pos1,
 
         nc.sync.dma_start(offs_sb[:], offs)
         for i in range(PASSES * PACK):
-            nc.sync.dma_start(windows[i][:, :T], x_planes[i // PACK, i % PACK])
+            queue = nc.scalar if i == 0 else nc.sync
+            queue.dma_start(windows[i][:, :T], x_planes[i // PACK, i % PACK])
             if i == PACK - 1:
                 load_gate(FED[0], S)
             if i == 3 * PACK - 2:
@@ -257,9 +258,9 @@ def tile_moe_pre_lin_bias_kernel(tc, xT, w_words, w_scales, b, gate, offs, pos1,
             nc.scalar.activation(picked[:, t0 : t0 + count], first_results(t0, count), COPY)
         t0, count = VECTOR_RUN
         nc.vector.tensor_copy(picked[:, t0 : t0 + count], first_results(t0, count))
-        for t0, count in (FIRST_RUN, VECTOR_RUN, LATER_RUNS[0]):
+        for t0, count in (FIRST_RUN, VECTOR_RUN):
             add_second(t0, count)
-        last_run, count = LATER_RUNS[1]
-        nc.sync.dma_start(out[:, :last_run], total[:, :last_run])
-        add_second(last_run, count)
-        nc.sync.dma_start(out[:, last_run:], total[:, last_run:])
+        nc.sync.dma_start(out[:, : t0 + count], total[:, : t0 + count])
+        for t0, count in LATER_RUNS:
+            add_second(t0, count)
+            nc.sync.dma_start(out[:, t0 : t0 + count], total[:, t0 : t0 + count])

@@ -33,11 +33,11 @@ CALL = 8
 OWN = (384, 384, 544, 384, 512)
 FED = tuple(S - count for count in OWN)
 VECTOR_FIRST = 288
-SECOND_SHARE = 3
-LAST_CHUNKS = (3, 2, 1)
+SECOND_SHARE = 352
+LAST_CHUNKS = (320, 320, 128)
 BLOCK_CALLS = ((0, 8), (8, 8), (16, 8), (36, 1), (32, 4), (24, 8))
 WINDOW = (904, 904, 776, 904, 704)
-BANK_OF = (2, 2, 2, 5, 3, 4, 1, 0, 0, 0)
+BANK_OF = (2, 2, 3, 3, 4, 5, 1, 0, 0, 0)
 FIRST_RUN = (0, 64)
 VECTOR_RUN = (64, 192)
 LATER_RUNS = ((256, 224), (480, 160))
@@ -208,7 +208,7 @@ def tile_moe_pre_lin_bias_kernel(tc, xT, w_words, w_scales, b, gate, offs, pos1,
         chunks = []
         first = 0
         for count in LAST_CHUNKS:
-            chunks.append(gather(4, first * C, count * C, fed_4[:, slots(PACK * first, PACK * count)]))
+            chunks.append((first, count, gather(4, first, count, fed_4[:, PACK * first : PACK * (first + count)])))
             first = first + count
 
         todo = units(0, 0, E) + units(1, 0, E) + units(2, 0, E)
@@ -224,26 +224,32 @@ def tile_moe_pre_lin_bias_kernel(tc, xT, w_words, w_scales, b, gate, offs, pos1,
 
         pool_place = BLOCK_CALLS[-2][0]
         free_place = BLOCK_CALLS[2][0]
-        left = FED[3] // C - SECOND_SHARE
-        early = LAST_CHUNKS[0]
-        pool_weave(left * C, SECOND_SHARE * C, fed_3[:, :, left * C :], pool_place * C)
-        vector_weave(0, left * C, fed_3[:, :, : left * C], (free_place + early) * C)
-        vector_weave(0, early * C, chunks[0], free_place * C)
-        free_scales = keep.tile([P, left * C], U8, name="free_scales", align_bytes=64)
-        last_scales = keep.tile([P, (SECOND_SHARE + FED[4] // C) * C], U8, name="last_scales", tag="raw_0", align_bytes=64)
-        quantise_and_multiply(free_place + early, units(3, 0, left), free_scales[:], call)
-        quantise_and_multiply(pool_place, units(3, left, SECOND_SHARE), last_scales[:, slots(0, SECOND_SHARE)], call + 1)
-        quantise_and_multiply(free_place, units(4, 0, early), last_scales[:, slots(SECOND_SHARE, early)], call + 2)
+        free = PER_BANK
+        held = FED[3] // C - free
+        left = FED[3] - SECOND_SHARE
+        place_4 = pool_place - 3
+        early = LAST_CHUNKS[0] // C
+        pool_weave(left, SECOND_SHARE, fed_3[:, :, left:], pool_place * C + left - free * C)
+        vector_weave(0, free * C, fed_3[:, :, : free * C], free_place * C)
+        vector_weave(free * C, left - free * C, fed_3[:, :, free * C : left], pool_place * C)
+        first, count, values = chunks[0]
+        vector_weave(first, count, values, place_4 * C)
+        free_scales = keep.tile([P, free * C], U8, name="free_scales", align_bytes=64)
+        last_scales = keep.tile([P, (held + FED[4] // C) * C], U8, name="last_scales", tag="raw_0", align_bytes=64)
+        quantise_and_multiply(free_place, units(3, 0, free), free_scales[:], call)
+        quantise_and_multiply(pool_place, units(3, free, held), last_scales[:, slots(0, held)], call + 1)
+        quantise_and_multiply(place_4, units(4, 0, early), last_scales[:, slots(held, early)], call + 2)
         add_bias(FED[4] // C, (FED[3] - FED[4]) // C)
         add_bias(0, early)
 
-        pool_weave(early * C, C, chunks[1][:, :, :C], pool_place * C)
-        vector_weave((early + 1) * C, C, chunks[1][:, :, C:], (pool_place + 1) * C)
-        vector_weave((early + 2) * C, C, chunks[2], (pool_place + 2) * C)
-        for j in (1, 2, 0):
-            quantise_and_multiply(pool_place + j, units(4, early + j, 1), last_scales[:, slots(SECOND_SHARE + early + j, 1)], call + 3 + j)
-        add_bias(early + 1, 2)
-        nc.vector.tensor_scalar_add(y[:, slots(early, 1)], sums_of(early), bias[:, early : early + 1])
+        for first, count, values in chunks[1:]:
+            vector_weave(first, count, values, place_4 * C + first)
+        final = FED[4] // C - 1
+        quantise_and_multiply(place_4 + early, units(4, early, final - early), last_scales[:, slots(held + early, final - early)], call + 3)
+        quantise_and_multiply(place_4 + final, units(4, final, 1), last_scales[:, slots(held + final, 1)], call + 4)
+        add_bias(early, 2)
+        for e in (final - 1, final):
+            nc.vector.tensor_scalar_add(y[:, slots(e, 1)], sums_of(e), bias[:, e : e + 1])
 
         picked = keep.tile([P, T], F32, name="picked")
         total = keep.tile([P, T], F32, name="total")

@@ -27,20 +27,27 @@ PER_COLUMN = 16
 QUADRANT = 32
 RUN = 2
 LINE = 4
-PER_BANK = 4
-CALL = 8
+BANK_SLOTS = 512
 
-OWN = (384, 384, 544, 384, 512)
-FED = tuple(S - count for count in OWN)
-VECTOR_FIRST = 288
-SECOND_SHARE = 352
-LAST_CHUNKS = (320, 320, 128)
-BLOCK_CALLS = ((0, 8), (8, 8), (16, 8), (36, 1), (32, 4), (24, 8))
-WINDOW = (904, 904, 776, 904, 704)
-BANK_OF = (2, 2, 3, 3, 4, 5, 1, 0, 0, 0)
+FIRST_OWN = 448
+LAST_OWN = 480
+POOL_SHARE = {1: 512, 2: 320, 3: 512}
+TAIL_CHUNKS = (352, 320, 128)
+WIDE_WINDOW = 1712
 FIRST_RUN = (0, 64)
 VECTOR_RUN = (64, 192)
 LATER_RUNS = ((256, 224), (480, 160))
+
+PLACE = {
+    0: tuple(range(18, 28)),
+    1: tuple(range(0, 4)) + tuple(range(28, 34)),
+    2: tuple(range(4, 8)) + tuple(range(12, 18)),
+    3: tuple(range(23, 33)),
+    4: tuple(range(30, 34)) + tuple(range(6, 12)),
+}
+PLACES = 34
+BLOCK_CALLS = ((17, 8), (0, 8), (33, 1), (25, 8), (9, 8))
+BANK_OF = (0, 1, 2, 3, 4, 4, 4, 5, 5, 5)
 
 
 def slots(first, count):
@@ -49,10 +56,6 @@ def slots(first, count):
 
 def list_columns(first_entry, count):
     return slice(first_entry // PER_COLUMN, (first_entry + count) // PER_COLUMN)
-
-
-def units(a, first, count):
-    return [(a, e) for e in range(first, first + count)]
 
 
 def tile_moe_pre_lin_bias_kernel(tc, xT, w_words, w_scales, b, gate, offs, pos1, pos2, out):
@@ -65,7 +68,20 @@ def tile_moe_pre_lin_bias_kernel(tc, xT, w_words, w_scales, b, gate, offs, pos1,
         pos1_sb = keep.tile([P, T // PER_COLUMN], U16, name="pos1_sb")
         pos2_sb = keep.tile([P, T // PER_COLUMN], U16, name="pos2_sb")
         w_scale_sb = keep.tile([P, E * PASSES * N], U8, name="w_scale_sb", align_bytes=64)
-        windows = [keep.tile([P, WINDOW[i // PACK]], F32, name=f"window_{i}", tag=f"window_{i}", align_bytes=64) for i in range(PASSES * PACK)]
+
+        width = {0: S - FIRST_OWN + PER_COLUMN, 2: S + PER_COLUMN, 3: S + PER_COLUMN, 4: T}
+        planes = {}
+        windows = {}
+        for a in width:
+            for t in range(PACK):
+                tile = keep.tile([P, width[a]], F32, name=f"window_{a}_{t}", tag=f"window_{a}_{t}", align_bytes=64)
+                planes[a, t] = tile[:, :T]
+                windows[a, t] = tile[:]
+        shared = keep.tile([P, (PACK - 1) * T + WIDE_WINDOW], F32, name="window_1", tag="window_1", align_bytes=64)
+        for t in range(PACK):
+            first = (PACK - 1 - t) * T
+            planes[1, t] = shared[:, first : first + T]
+            windows[1, t] = shared[:, first : first + WIDE_WINDOW]
 
         warm = keep.tile([P, 2], F32, name="warm")
         nc.vector.memset(warm[:, 0:1], 0.0)
@@ -74,21 +90,31 @@ def tile_moe_pre_lin_bias_kernel(tc, xT, w_words, w_scales, b, gate, offs, pos1,
 
         x_planes = xT.rearrange("(a p t) c -> a t p c", p=P, t=PACK)
         gate_sb = keep.tile([P, S], F32, name="gate_sb")
-        gate_columns = keep.tile([P, max(FED) // C], F32, name="gate_columns")
+        gate_experts = 2 * BANK_SLOTS // C
+        gate_columns = keep.tile([P, gate_experts], F32, name="gate_columns")
+
+        def load_plane(a, t):
+            queue = nc.scalar if (a, t) == (0, 0) else nc.sync
+            queue.dma_start(planes[a, t], x_planes[a, t])
 
         def load_gate(first_slot, end_slot):
             nc.sync.dma_start(gate_sb[:, first_slot:end_slot], gate[0:P, first_slot:end_slot])
 
         nc.sync.dma_start(offs_sb[:], offs)
-        for i in range(PASSES * PACK):
-            queue = nc.scalar if i == 0 else nc.sync
-            queue.dma_start(windows[i][:, :T], x_planes[i // PACK, i % PACK])
-            if i == PACK - 1:
-                load_gate(FED[0], S)
-            if i == 3 * PACK - 2:
-                load_gate(VECTOR_FIRST, FED[0])
+        for t in range(PACK):
+            load_plane(0, t)
+        load_gate(S - FIRST_OWN, S)
+        for t in range(PACK):
+            load_plane(1, t)
+            if t == 0:
+                load_gate(0, S - FIRST_OWN)
+            load_plane(2, t)
+        for t in range(PACK):
+            load_plane(4, t)
         with nc.allow_non_contiguous_dma(reason="one gate value a partition"):
-            nc.sync.dma_start(gate_columns[:], gate[0:1, : max(FED)].rearrange("o (e c) -> c (o e)", c=C))
+            nc.sync.dma_start(gate_columns[:], gate[0:1, : gate_experts * C].rearrange("o (e c) -> c (o e)", c=C))
+        for t in range(PACK):
+            load_plane(3, t)
 
         bias = keep.tile([P, E], F32, name="bias")
         rows = w_scales.rearrange("e a q n -> q (e a) n").bitcast(I32)
@@ -108,151 +134,141 @@ def tile_moe_pre_lin_bias_kernel(tc, xT, w_words, w_scales, b, gate, offs, pos1,
 
         y = keep.tile([P, S], F32, name="y")
         banks = [psum.tile([P, BANK_OF.count(i) * C], F32, name=f"bank_{i}") for i in range(max(BANK_OF) + 1)]
-        block = 3 * E + (OWN[3] + OWN[4]) // C
-        woven = keep.tile([P, PACK * block * C], BF16, name="woven", align_bytes=64)
+        woven = keep.tile([P, PACK * PLACES * C], BF16, name="woven", align_bytes=64)
 
         identity = keep.tile([P, P], F32, name="identity")
         make_identity(nc, identity[:])
         gate_ps = []
-        for first in range(0, max(FED) // C, PER_BANK):
-            count = min(PER_BANK, max(FED) // C - first)
-            gate_bank = psum.tile([P, count * C], F32, name=f"gate_ps_{first}")
-            for j in range(count):
-                nc.tensor.transpose(gate_bank[:, slots(j, 1)], gate_columns[:, first + j : first + j + 1].to_broadcast([P, P]), identity[:])
+        for bank in range(gate_experts * C // BANK_SLOTS):
+            gate_bank = psum.tile([P, BANK_SLOTS], F32, name=f"gate_ps_{bank}")
+            for j in range(BANK_SLOTS // C):
+                e = bank * BANK_SLOTS // C + j
+                nc.tensor.transpose(gate_bank[:, slots(j, 1)], gate_columns[:, e : e + 1].to_broadcast([P, P]), identity[:])
             gate_ps.append(gate_bank)
 
-        def offsets(first_slot, count):
-            return offs_sb[:, list_columns(first_slot, count)]
+        def raw(tag, count, name):
+            return keep.tile([P, PACK * count], F32, name=name, tag=tag, align_bytes=64)
 
-        def gather_own(a):
-            values = keep.tile([P, PACK * OWN[a]], F32, name=f"own_{a}", tag=f"own_{a}", align_bytes=64)
+        def gather(engine, a, first_slot, count, values):
+            offsets = offs_sb[:, list_columns(first_slot, count)]
             for t in range(PACK):
-                nc.vector.tensor_copy(values[:, t * OWN[a] : (t + 1) * OWN[a]], windows[a * PACK + t][:].indirect(offsets(FED[a], OWN[a])))
-            return values[:].rearrange("p (t s) -> p t s", t=PACK)
+                target = values[:, t * count : (t + 1) * count]
+                if engine == "vector":
+                    nc.vector.tensor_copy(target, windows[a, t].indirect(offsets))
+                else:
+                    nc.scalar.activation(target, windows[a, t].indirect(offsets), COPY)
+            return first_slot, values.rearrange("p (t s) -> p t s", t=PACK)
 
-        def gather(a, first_slot, count, values):
-            for t in range(PACK):
-                nc.scalar.activation(values[:, t * count : (t + 1) * count], windows[a * PACK + t][:].indirect(offsets(first_slot, count)), COPY)
-            return values.rearrange("p (t s) -> p t s", t=PACK)
+        def words(a, first_slot, count):
+            first = PLACE[a][first_slot // C] * C + first_slot % C
+            return woven[:, PACK * first : PACK * (first + count)]
 
-        def raw(i, count, name):
-            return keep.tile([P, PACK * count], F32, name=name, tag=f"raw_{i}", align_bytes=64)
-
-        def words(first_slot, count):
-            return woven[:, PACK * first_slot : PACK * (first_slot + count)]
-
-        def pool_weave(first_slot, count, values, place):
+        def pool_weave(a, first_slot, count, chunk):
+            start, values = chunk
             weight = gate_sb[:, first_slot : first_slot + count].rearrange("p (c i) -> p c i", i=LINE)
             nc.gpsimd.tensor_tensor(
-                words(place, count).rearrange("p (c i t) -> p c t i", t=PACK, i=LINE),
-                values.rearrange("p t (c i) -> p c t i", i=LINE),
+                words(a, first_slot, count).rearrange("p (c i t) -> p c t i", t=PACK, i=LINE),
+                values[:, :, first_slot - start : first_slot - start + count].rearrange("p t (c i) -> p c t i", i=LINE),
                 weight.unsqueeze(2).to_broadcast([P, count // LINE, PACK, LINE]),
                 MULT,
             )
 
-        def vector_weave(first_slot, count, values, place):
-            bank_slots = PER_BANK * C
-            for bank in range(first_slot // bank_slots, (first_slot + count - 1) // bank_slots + 1):
-                lo = max(first_slot, bank * bank_slots)
-                size = min(first_slot + count, (bank + 1) * bank_slots) - lo
-                weight = gate_ps[bank][:, lo - bank * bank_slots : lo - bank * bank_slots + size]
+        def vector_weave(a, first_slot, count, chunk):
+            start, values = chunk
+            for bank in range(first_slot // BANK_SLOTS, (first_slot + count - 1) // BANK_SLOTS + 1):
+                lo = max(first_slot, bank * BANK_SLOTS)
+                size = min(first_slot + count, (bank + 1) * BANK_SLOTS) - lo
+                weight = gate_ps[bank][:, lo - bank * BANK_SLOTS : lo - bank * BANK_SLOTS + size]
                 weight = weight.rearrange("p (c i) -> p c i", i=RUN).unsqueeze(2).to_broadcast([P, size // RUN, PACK, RUN])
                 nc.vector.tensor_tensor(
-                    words(place + lo - first_slot, size).rearrange("p (c i t) -> p c t i", t=PACK, i=RUN),
-                    values[:, :, lo - first_slot : lo - first_slot + size].rearrange("p t (c i) -> p c t i", i=RUN),
+                    words(a, lo, size).rearrange("p (c i t) -> p c t i", t=PACK, i=RUN),
+                    values[:, :, lo - start : lo - start + size].rearrange("p t (c i) -> p c t i", i=RUN),
                     weight,
                     MULT,
                 )
 
         passes_left = [PASSES * BANK_OF.count(i) for i in range(len(banks))]
 
-        def multiply(a, e, codes, scales):
-            bank = BANK_OF[e]
-            opens = passes_left[bank] == PASSES * BANK_OF.count(bank)
-            passes_left[bank] = passes_left[bank] - 1
-            scale_column = (e * PASSES + a) * N
-            nc.tensor.matmul_mx(
-                out=sums_of(e),
-                lhsT=w_codes[a][:, e, :].bitcast(FP8X4),
-                lhsT_scale=w_scale_sb[:, scale_column : scale_column + N],
-                rhs=codes.bitcast(FP8X4),
-                rhs_scale=scales,
-                start=opens,
-                stop=(passes_left[bank] == 0),
-            )
-
         def sums_of(e):
             return banks[BANK_OF[e]][:, slots(e - BANK_OF.index(BANK_OF[e]), 1)]
 
-        def quantise_and_multiply(place, todo, scales, call):
-            codes = keep.tile([P, len(todo) * C], U32, name=f"codes_{call}", tag=f"window_{call}", align_bytes=64)
-            nc.vector.quantize_mx(out=codes[:].bitcast(FP8X4), scales=scales, in_=words(place * C, len(todo) * C))
-            for j, (a, e) in enumerate(todo):
-                multiply(a, e, codes[:, slots(j, 1)], scales[:, slots(j, 1)])
+        def quantise_and_multiply(passes, place, count, scales, tag):
+            codes = keep.tile([P, count * C], U32, name=f"codes_{tag}", tag=tag, align_bytes=64)
+            nc.vector.quantize_mx(out=codes[:].bitcast(FP8X4), scales=scales, in_=woven[:, PACK * place * C : PACK * (place + count) * C])
+            for j in range(count):
+                a = [a for a in passes if place + j in PLACE[a]][0]
+                e = PLACE[a].index(place + j)
+                bank = BANK_OF[e]
+                opens = passes_left[bank] == PASSES * BANK_OF.count(bank)
+                passes_left[bank] = passes_left[bank] - 1
+                scale_column = (e * PASSES + a) * N
+                nc.tensor.matmul_mx(
+                    out=sums_of(e),
+                    lhsT=w_codes[a][:, e, :].bitcast(FP8X4),
+                    lhsT_scale=w_scale_sb[:, scale_column : scale_column + N],
+                    rhs=codes[:, slots(j, 1)].bitcast(FP8X4),
+                    rhs_scale=scales[:, slots(j, 1)],
+                    start=opens,
+                    stop=(passes_left[bank] == 0),
+                )
 
-        def add_bias(first, count):
-            for e in range(first, first + count):
-                nc.scalar.activation(y[:, slots(e, 1)], sums_of(e), IDENTITY, bias=bias[:, e : e + 1])
+        def add_bias(e):
+            nc.scalar.activation(y[:, slots(e, 1)], sums_of(e), IDENTITY, bias=bias[:, e : e + 1])
 
-        fed = [gather(a, 0, FED[a], raw(a, FED[a], f"fed_{a}")[:]) for a in range(3)]
-        own_place = [FED[0], S + FED[1], 2 * S + FED[2], 3 * S, 3 * S + OWN[3]]
-        for a in range(PASSES):
-            pool_weave(FED[a], OWN[a], gather_own(a), own_place[a])
-            if a == 1:
-                pool_weave(VECTOR_FIRST, FED[0] - VECTOR_FIRST, fed[0][:, :, VECTOR_FIRST:], VECTOR_FIRST)
-        vector_weave(0, VECTOR_FIRST, fed[0][:, :, :VECTOR_FIRST], 0)
-        for a in (1, 2):
-            vector_weave(0, FED[a], fed[a], a * S)
-        fed_3 = gather(3, 0, FED[3], raw(0, FED[3], "fed_3")[:])
-        fed_4 = raw(2, FED[4], "fed_4")
-        chunks = []
-        first = 0
-        for count in LAST_CHUNKS:
-            chunks.append((first, count, gather(4, first, count, fed_4[:, PACK * first : PACK * (first + count)])))
-            first = first + count
+        raw_0 = raw("raw_a", S, "raw_0")
+        fed_0 = gather("scalar", 0, 0, S - FIRST_OWN, raw_0[:, : PACK * (S - FIRST_OWN)])
+        own_0 = gather("vector", 0, S - FIRST_OWN, FIRST_OWN, raw_0[:, PACK * (S - FIRST_OWN) :])
+        pass_1 = gather("vector", 1, 0, S, raw("raw_b", S, "raw_1")[:])
+        pass_2 = gather("scalar", 2, 0, S, raw("raw_c", S, "raw_2")[:])
+        own_4 = gather("vector", 4, S - LAST_OWN, LAST_OWN, raw("raw_d", LAST_OWN, "own_4")[:])
 
-        todo = units(0, 0, E) + units(1, 0, E) + units(2, 0, E)
-        for a in (3, 4):
-            todo = todo + units(a, FED[a] // C, OWN[a] // C)
-        first_scales = keep.tile([P, CALL * C], U8, name="first_scales", tag="own_3", align_bytes=64)
-        scales = keep.tile([P, block * C], U8, name="scales", tag="own_4", align_bytes=64)
+        pool_weave(0, S - FIRST_OWN, FIRST_OWN, own_0)
+        pool_weave(0, 0, S - FIRST_OWN, fed_0)
+        pool_weave(1, S - POOL_SHARE[1], POOL_SHARE[1], pass_1)
+        pool_weave(2, S - POOL_SHARE[2], POOL_SHARE[2], pass_2)
+        pool_weave(4, S - LAST_OWN, LAST_OWN, own_4)
+        vector_weave(1, 0, S - POOL_SHARE[1], pass_1)
+        vector_weave(2, 0, S - POOL_SHARE[2], pass_2)
+
+        pass_3 = gather("scalar", 3, 0, S, raw("raw_a", S, "raw_3")[:])
+        raw_4 = raw("raw_b", S - LAST_OWN, "raw_4")
+        tail = []
+        end = S - LAST_OWN
+        for count in TAIL_CHUNKS:
+            first = end - count
+            tail.append((first, count, gather("scalar", 4, first, count, raw_4[:, PACK * first : PACK * end])))
+            end = first
+
+        first_scales = keep.tile([P, BLOCK_CALLS[0][1] * C], U8, name="first_scales", align_bytes=64)
+        scales = keep.tile([P, PLACES * C], U8, name="scales", tag="raw_d", align_bytes=64)
+        block_tags = ("window_2_0", "window_2_1", "window_0_0", "window_2_2", "window_2_3")
         for call, (place, count) in enumerate(BLOCK_CALLS):
-            plane = first_scales if call == 0 else scales
-            quantise_and_multiply(place, todo[place : place + count], plane[:, slots(place, count)], call)
-        call = len(BLOCK_CALLS)
-        add_bias(FED[3] // C, OWN[3] // C)
+            plane = first_scales[:] if call == 0 else scales[:, slots(place, count)]
+            quantise_and_multiply((0, 1, 2, 4), place, count, plane, block_tags[call])
 
-        pool_place = BLOCK_CALLS[-2][0]
-        free_place = BLOCK_CALLS[2][0]
-        free = PER_BANK
-        held = FED[3] // C - free
-        left = FED[3] - SECOND_SHARE
-        place_4 = pool_place - 3
-        early = LAST_CHUNKS[0] // C
-        pool_weave(left, SECOND_SHARE, fed_3[:, :, left:], pool_place * C + left - free * C)
-        vector_weave(0, free * C, fed_3[:, :, : free * C], free_place * C)
-        vector_weave(free * C, left - free * C, fed_3[:, :, free * C : left], pool_place * C)
-        first, count, values = chunks[0]
-        vector_weave(first, count, values, place_4 * C)
-        free_scales = keep.tile([P, free * C], U8, name="free_scales", align_bytes=64)
-        last_scales = keep.tile([P, (held + FED[4] // C) * C], U8, name="last_scales", tag="raw_0", align_bytes=64)
-        quantise_and_multiply(free_place, units(3, 0, free), free_scales[:], call)
-        quantise_and_multiply(pool_place, units(3, free, held), last_scales[:, slots(0, held)], call + 1)
-        quantise_and_multiply(place_4, units(4, 0, early), last_scales[:, slots(held, early)], call + 2)
-        add_bias(FED[4] // C, (FED[3] - FED[4]) // C)
-        add_bias(0, early)
+        pool_weave(3, S - POOL_SHARE[3], POOL_SHARE[3], pass_3)
+        vector_weave(3, 0, S - POOL_SHARE[3], pass_3)
+        first, count, chunk = tail[0]
+        vector_weave(4, first, count, chunk)
+        free_scales = keep.tile([P, 2 * C], U8, name="free_scales", align_bytes=64)
+        last_scales = keep.tile([P, 15 * C], U8, name="last_scales", tag="raw_a", align_bytes=64)
+        quantise_and_multiply((3,), PLACE[3][0], 2, free_scales[:], "window_0_1")
+        quantise_and_multiply((3,), PLACE[3][2], 8, last_scales[:, slots(0, 8)], "window_3_0")
+        quantise_and_multiply((4,), PLACE[4][4], 3, last_scales[:, slots(8, 3)], "window_0_2")
+        for e in (7, 8, 9, 4, 5, 6):
+            add_bias(e)
 
-        for first, count, values in chunks[1:]:
-            vector_weave(first, count, values, place_4 * C + first)
-        final = FED[4] // C - 1
-        quantise_and_multiply(place_4 + early, units(4, early, final - early), last_scales[:, slots(held + early, final - early)], call + 3)
-        quantise_and_multiply(place_4 + final, units(4, final, 1), last_scales[:, slots(held + final, 1)], call + 4)
-        add_bias(early, 2)
-        for e in (final - 1, final):
+        for first, count, chunk in tail[1:]:
+            vector_weave(4, first, count, chunk)
+        quantise_and_multiply((4,), PLACE[4][1], 3, last_scales[:, slots(11, 3)], "window_0_3")
+        quantise_and_multiply((4,), PLACE[4][0], 1, last_scales[:, slots(14, 1)], "window_3_1")
+        for e in (1, 2):
+            add_bias(e)
+        for e in (3, 0):
             nc.vector.tensor_scalar_add(y[:, slots(e, 1)], sums_of(e), bias[:, e : e + 1])
 
-        picked = keep.tile([P, T], F32, name="picked")
-        total = keep.tile([P, T], F32, name="total")
+        picked = keep.tile([P, T], F32, name="picked", tag="raw_c", align_bytes=64)
+        total = keep.tile([P, T], F32, name="total", tag="raw_b", align_bytes=64)
 
         def first_results(t0, count):
             return y[:].indirect(pos1_sb[:, list_columns(t0, count)])

@@ -91,7 +91,7 @@ def tile_moe_pre_lin_bias_kernel(tc, xT, w_words, w_scales, b, gate, offs, pos1,
         x_planes = xT.rearrange("(a p t) c -> a t p c", p=P, t=PACK)
         gate_sb = keep.tile([P, S], F32, name="gate_sb")
         gate_experts = 2 * BANK_SLOTS // C
-        gate_columns = keep.tile([P, gate_experts], F32, name="gate_columns")
+        gate_columns = keep.tile([P, gate_experts], F32, name="gate_columns", tag="gate_columns", align_bytes=64)
 
         def load_plane(a, t):
             queue = nc.scalar if (a, t) == (0, 0) else nc.sync
@@ -101,6 +101,8 @@ def tile_moe_pre_lin_bias_kernel(tc, xT, w_words, w_scales, b, gate, offs, pos1,
             nc.sync.dma_start(gate_sb[:, first_slot:end_slot], gate[0:P, first_slot:end_slot])
 
         nc.sync.dma_start(offs_sb[:], offs)
+        nc.sync.dma_start(pos1_sb[:], pos1)
+        nc.sync.dma_start(pos2_sb[:], pos2)
         for t in range(PACK):
             load_plane(0, t)
         load_gate(S - FIRST_OWN, S)
@@ -124,8 +126,6 @@ def tile_moe_pre_lin_bias_kernel(tc, xT, w_words, w_scales, b, gate, offs, pos1,
                 rows[4 * quadrant : 4 * quadrant + 4],
             )
         nc.sync.dma_start(bias[:], b)
-        nc.sync.dma_start(pos1_sb[:], pos1)
-        nc.sync.dma_start(pos2_sb[:], pos2)
         w_codes = []
         for a in range(PASSES):
             w_a = keep.tile([P, E, N * PACK], U8, name=f"w_{a}", align_bytes=64)
@@ -239,7 +239,7 @@ def tile_moe_pre_lin_bias_kernel(tc, xT, w_words, w_scales, b, gate, offs, pos1,
             tail.append((first, count, gather("scalar", 4, first, count, raw_4[:, PACK * first : PACK * end])))
             end = first
 
-        first_scales = keep.tile([P, BLOCK_CALLS[0][1] * C], U8, name="first_scales", align_bytes=64)
+        first_scales = keep.tile([P, BLOCK_CALLS[0][1] * C], U8, name="first_scales", tag="gate_columns", align_bytes=64)
         scales = keep.tile([P, PLACES * C], U8, name="scales", tag="raw_d", align_bytes=64)
         block_tags = ("window_2_0", "window_2_1", "window_0_0", "window_2_2", "window_2_3")
         for call, (place, count) in enumerate(BLOCK_CALLS):

@@ -30,9 +30,9 @@ LINE = 4
 BANK_SLOTS = 512
 
 FIRST_OWN = 448
-LAST_OWN = 480
+LAST_OWN = 416
 POOL_SHARE = {1: 512, 2: 320, 3: 512}
-TAIL_CHUNKS = (352, 320, 128)
+TAIL_CHUNKS = (384, 352, 128)
 WIDE_WINDOW = 1712
 FIRST_RUN = (0, 64)
 VECTOR_RUN = (64, 192)

@@ -30,9 +30,9 @@ LINE = 4
 BANK_SLOTS = 512
 
 FIRST_OWN = 448
-LAST_OWN = 416
-POOL_SHARE = {1: 512, 2: 320, 3: 512}
-TAIL_CHUNKS = (384, 352, 128)
+LAST_OWN = 448
+POOL_SHARE = {1: 576, 2: 256, 3: 512}
+TAIL_CHUNKS = (384, 320, 128)
 WIDE_WINDOW = 1712
 FIRST_RUN = (0, 64)
 VECTOR_RUN = (64, 192)

@@ -28,6 +28,7 @@ QUADRANT = 32
 RUN = 2
 LINE = 4
 BANK_SLOTS = 512
+PAD = 16
 
 FIRST_OWN = 448
 LAST_OWN = 448
@@ -146,13 +147,15 @@ def tile_moe_pre_lin_bias_kernel(tc, xT, w_words, w_scales, b, gate, offs, pos1,
                 nc.tensor.transpose(gate_bank[:, slots(j, 1)], gate_columns[:, e : e + 1].to_broadcast([P, P]), identity[:])
             gate_ps.append(gate_bank)
 
-        def raw(tag, count, name):
-            return keep.tile([P, PACK * count], F32, name=name, tag=tag, align_bytes=64)
+        def raw(tag, counts, name):
+            tile = keep.tile([P, PACK * sum(count + PAD for count in counts)], F32, name=name, tag=tag, align_bytes=64)
+            ends = [PACK * sum(count + PAD for count in counts[: i + 1]) for i in range(len(counts))]
+            return [tile[:, end - PACK * (count + PAD) : end] for count, end in zip(counts, ends)]
 
         def gather(engine, a, first_slot, count, values):
             offsets = offs_sb[:, list_columns(first_slot, count)]
             for t in range(PACK):
-                target = values[:, t * count : (t + 1) * count]
+                target = values[:, t * (count + PAD) : t * (count + PAD) + count]
                 if engine == "vector":
                     nc.vector.tensor_copy(target, windows[a, t].indirect(offsets))
                 else:
@@ -215,12 +218,12 @@ def tile_moe_pre_lin_bias_kernel(tc, xT, w_words, w_scales, b, gate, offs, pos1,
         def add_bias(e):
             nc.scalar.activation(y[:, slots(e, 1)], sums_of(e), IDENTITY, bias=bias[:, e : e + 1])
 
-        raw_0 = raw("raw_a", S, "raw_0")
-        fed_0 = gather("scalar", 0, 0, S - FIRST_OWN, raw_0[:, : PACK * (S - FIRST_OWN)])
-        own_0 = gather("vector", 0, S - FIRST_OWN, FIRST_OWN, raw_0[:, PACK * (S - FIRST_OWN) :])
-        pass_1 = gather("vector", 1, 0, S, raw("raw_b", S, "raw_1")[:])
-        pass_2 = gather("scalar", 2, 0, S, raw("raw_c", S, "raw_2")[:])
-        own_4 = gather("vector", 4, S - LAST_OWN, LAST_OWN, raw("raw_d", LAST_OWN, "own_4")[:])
+        raw_fed, raw_own = raw("raw_a", (S - FIRST_OWN, FIRST_OWN), "raw_0")
+        fed_0 = gather("scalar", 0, 0, S - FIRST_OWN, raw_fed)
+        own_0 = gather("vector", 0, S - FIRST_OWN, FIRST_OWN, raw_own)
+        pass_1 = gather("vector", 1, 0, S, raw("raw_b", (S,), "raw_1")[0])
+        pass_2 = gather("scalar", 2, 0, S, raw("raw_c", (S,), "raw_2")[0])
+        own_4 = gather("vector", 4, S - LAST_OWN, LAST_OWN, raw("raw_d", (LAST_OWN,), "own_4")[0])
 
         pool_weave(0, S - FIRST_OWN, FIRST_OWN, own_0)
         pool_weave(0, 0, S - FIRST_OWN, fed_0)
@@ -230,13 +233,12 @@ def tile_moe_pre_lin_bias_kernel(tc, xT, w_words, w_scales, b, gate, offs, pos1,
         vector_weave(1, 0, S - POOL_SHARE[1], pass_1)
         vector_weave(2, 0, S - POOL_SHARE[2], pass_2)
 
-        pass_3 = gather("scalar", 3, 0, S, raw("raw_a", S, "raw_3")[:])
-        raw_4 = raw("raw_b", S - LAST_OWN, "raw_4")
+        pass_3 = gather("scalar", 3, 0, S, raw("raw_a", (S,), "raw_3")[0])
         tail = []
         end = S - LAST_OWN
-        for count in TAIL_CHUNKS:
+        for count, values in zip(TAIL_CHUNKS, raw("raw_b", TAIL_CHUNKS, "raw_4")):
             first = end - count
-            tail.append((first, count, gather("scalar", 4, first, count, raw_4[:, PACK * first : PACK * end])))
+            tail.append((first, count, gather("scalar", 4, first, count, values)))
             end = first
 
         first_scales = keep.tile([P, BLOCK_CALLS[0][1] * C], U8, name="first_scales", tag="gate_columns", align_bytes=64)

@@ -30,10 +30,10 @@ LINE = 4
 BANK_SLOTS = 512
 PAD = 16
 
-FIRST_OWN = 448
+FIRST_OWN = 480
 LAST_OWN = 448
-POOL_SHARE = {1: 576, 2: 256, 3: 512}
-TAIL_CHUNKS = (384, 320, 128)
+POOL_SHARE = {1: 448, 2: 544, 3: 512}
+TAIL_CHUNKS = (352, 352, 128)
 WIDE_WINDOW = 1712
 FIRST_RUN = (0, 64)
 VECTOR_RUN = (64, 192)
@@ -106,7 +106,8 @@ def tile_moe_pre_lin_bias_kernel(tc, xT, w_words, w_scales, b, gate, offs, pos1,
         nc.sync.dma_start(pos2_sb[:], pos2)
         for t in range(PACK):
             load_plane(0, t)
-        load_gate(S - FIRST_OWN, S)
+            if t == 1:
+                load_gate(S - FIRST_OWN, S)
         for t in range(PACK):
             load_plane(1, t)
             if t == 0:
@@ -166,13 +167,13 @@ def tile_moe_pre_lin_bias_kernel(tc, xT, w_words, w_scales, b, gate, offs, pos1,
             first = PLACE[a][first_slot // C] * C + first_slot % C
             return woven[:, PACK * first : PACK * (first + count)]
 
-        def pool_weave(a, first_slot, count, chunk):
+        def pool_weave(a, first_slot, count, chunk, first_plane=0, end_plane=PACK):
             start, values = chunk
             weight = gate_sb[:, first_slot : first_slot + count].rearrange("p (c i) -> p c i", i=LINE)
             nc.gpsimd.tensor_tensor(
-                words(a, first_slot, count).rearrange("p (c i t) -> p c t i", t=PACK, i=LINE),
-                values[:, :, first_slot - start : first_slot - start + count].rearrange("p t (c i) -> p c t i", i=LINE),
-                weight.unsqueeze(2).to_broadcast([P, count // LINE, PACK, LINE]),
+                words(a, first_slot, count).rearrange("p (c i t) -> p c t i", t=PACK, i=LINE)[:, :, first_plane:end_plane, :],
+                values[:, first_plane:end_plane, first_slot - start : first_slot - start + count].rearrange("p t (c i) -> p c t i", i=LINE),
+                weight.unsqueeze(2).to_broadcast([P, count // LINE, end_plane - first_plane, LINE]),
                 MULT,
             )
 
@@ -225,10 +226,12 @@ def tile_moe_pre_lin_bias_kernel(tc, xT, w_words, w_scales, b, gate, offs, pos1,
         pass_2 = gather("scalar", 2, 0, S, raw("raw_c", (S,), "raw_2")[0])
         own_4 = gather("vector", 4, S - LAST_OWN, LAST_OWN, raw("raw_d", (LAST_OWN,), "own_4")[0])
 
-        pool_weave(0, S - FIRST_OWN, FIRST_OWN, own_0)
-        pool_weave(0, 0, S - FIRST_OWN, fed_0)
+        for pair in ((0, 2), (2, 4)):
+            pool_weave(0, S - FIRST_OWN, FIRST_OWN, own_0, *pair)
+            pool_weave(0, 0, S - FIRST_OWN, fed_0, *pair)
+        pool_weave(2, S - POOL_SHARE[2], POOL_SHARE[2], pass_2, 0, 2)
         pool_weave(1, S - POOL_SHARE[1], POOL_SHARE[1], pass_1)
-        pool_weave(2, S - POOL_SHARE[2], POOL_SHARE[2], pass_2)
+        pool_weave(2, S - POOL_SHARE[2], POOL_SHARE[2], pass_2, 2, 4)
         pool_weave(4, S - LAST_OWN, LAST_OWN, own_4)
         vector_weave(1, 0, S - POOL_SHARE[1], pass_1)
         vector_weave(2, 0, S - POOL_SHARE[2], pass_2)

@@ -106,7 +106,7 @@ def tile_moe_pre_lin_bias_kernel(tc, xT, w_words, w_scales, b, gate, offs, pos1,
         nc.sync.dma_start(pos2_sb[:], pos2)
         for t in range(PACK):
             load_plane(0, t)
-            if t == 1:
+            if t == 2:
                 load_gate(S - FIRST_OWN, S)
         for t in range(PACK):
             load_plane(1, t)

@@ -30,10 +30,10 @@ LINE = 4
 BANK_SLOTS = 512
 PAD = 16
 
-FIRST_OWN = 480
-LAST_OWN = 448
-POOL_SHARE = {1: 448, 2: 544, 3: 512}
-TAIL_CHUNKS = (352, 352, 128)
+FIRST_OWN = 512
+LAST_OWN = 416
+POOL_SHARE = {1: 464, 2: 544, 3: 520}
+TAIL_CHUNKS = (384, 352, 128)
 WIDE_WINDOW = 1712
 FIRST_RUN = (0, 64)
 VECTOR_RUN = (64, 192)
@@ -228,7 +228,7 @@ def tile_moe_pre_lin_bias_kernel(tc, xT, w_words, w_scales, b, gate, offs, pos1,
 
         for pair in ((0, 2), (2, 4)):
             pool_weave(0, S - FIRST_OWN, FIRST_OWN, own_0, *pair)
-            pool_weave(0, 0, S - FIRST_OWN, fed_0, *pair)
+        pool_weave(0, 0, S - FIRST_OWN, fed_0)
         pool_weave(2, S - POOL_SHARE[2], POOL_SHARE[2], pass_2, 0, 2)
         pool_weave(1, S - POOL_SHARE[1], POOL_SHARE[1], pass_1)
         pool_weave(2, S - POOL_SHARE[2], POOL_SHARE[2], pass_2, 2, 4)

@@ -87,6 +87,8 @@ def tile_moe_pre_lin_bias_kernel(tc, xT, w_words, w_scales, b, gate, offs, pos1,
         warm = keep.tile([P, 2], F32, name="warm")
         nc.vector.memset(warm[:, 0:1], 0.0)
         nc.scalar.activation(warm[:, 1:2], warm[:, 0:1], COPY)
+        pool_warm = keep.tile([P, 1], BF16, name="pool_warm")
+        nc.gpsimd.tensor_tensor(pool_warm[:], warm[:, 0:1], warm[:, 0:1], MULT)
         nc.vector.memset(w_scale_sb[:].bitcast(I32), 0)
 
         x_planes = xT.rearrange("(a p t) c -> a t p c", p=P, t=PACK)

from contextlib import ExitStack

import concourse.mybir as mybir
from concourse.masks import make_identity

K, T, E, C, N = 2560, 640, 10, 128, 128
S = E * C
FLOPS = 2 * K * S * N
BYTES = K * T * 4 + E * K * N + E * (K // 32) * N + N * E * 4 + S * 4 + 128 * (S + 2 * T) // 8 + N * T * 4

F32 = mybir.dt.float32
BF16 = mybir.dt.bfloat16
I32 = mybir.dt.int32
U32 = mybir.dt.uint32
U16 = mybir.dt.uint16
U8 = mybir.dt.uint8
FP8X4 = mybir.dt.float8_e4m3fn_x4
MULT = mybir.AluOpType.mult
ADD = mybir.AluOpType.add
IDENTITY = mybir.ActivationFunctionType.Identity
COPY = mybir.ActivationFunctionType.Copy

P = 128
PACK = 4
PASSES = K // (P * PACK)
PER_COLUMN = 16
QUADRANT = 32
RUN = 2
LINE = 4
BANK_SLOTS = 512
PAD = 16

FIRST_OWN = 512
LAST_OWN = 416
POOL_SHARE = {1: 464, 2: 544, 3: 520}
TAIL_CHUNKS = (384, 352, 128)
WIDE_WINDOW = 1712
FIRST_RUN = (0, 64)
VECTOR_RUN = (64, 192)
LATER_RUNS = ((256, 224), (480, 160))

PLACE = {
    0: tuple(range(18, 28)),
    1: tuple(range(0, 4)) + tuple(range(28, 34)),
    2: tuple(range(4, 8)) + tuple(range(12, 18)),
    3: tuple(range(23, 33)),
    4: tuple(range(30, 34)) + tuple(range(6, 12)),
}
PLACES = 34
BLOCK_CALLS = ((17, 8), (0, 8), (33, 1), (25, 8), (9, 8))
BANK_OF = (0, 1, 2, 3, 4, 4, 4, 5, 5, 5)


def slots(first, count):
    return slice(first * C, (first + count) * C)


def list_columns(first_entry, count):
    return slice(first_entry // PER_COLUMN, (first_entry + count) // PER_COLUMN)


def tile_moe_pre_lin_bias_kernel(tc, xT, w_words, w_scales, b, gate, offs, pos1, pos2, out):
    nc = tc.nc
    with ExitStack() as ctx:
        keep = ctx.enter_context(tc.tile_pool(name="keep", bufs=1))
        psum = ctx.enter_context(tc.psum_pool(name="psum", bufs=1))

        offs_sb = keep.tile([P, S // PER_COLUMN], U16, name="offs_sb")
        pos1_sb = keep.tile([P, T // PER_COLUMN], U16, name="pos1_sb")
        pos2_sb = keep.tile([P, T // PER_COLUMN], U16, name="pos2_sb")
        w_scale_sb = keep.tile([P, E * PASSES * N], U8, name="w_scale_sb", align_bytes=64)

        width = {0: S - FIRST_OWN + PER_COLUMN, 2: S + PER_COLUMN, 3: S + PER_COLUMN, 4: T}
        planes = {}
        windows = {}
        for a in width:
            for t in range(PACK):
                tile = keep.tile([P, width[a]], F32, name=f"window_{a}_{t}", tag=f"window_{a}_{t}", align_bytes=64)
                planes[a, t] = tile[:, :T]
                windows[a, t] = tile[:]
        shared = keep.tile([P, (PACK - 1) * T + WIDE_WINDOW], F32, name="window_1", tag="window_1", align_bytes=64)
        for t in range(PACK):
            first = (PACK - 1 - t) * T
            planes[1, t] = shared[:, first : first + T]
            windows[1, t] = shared[:, first : first + WIDE_WINDOW]

        warm = keep.tile([P, 2], F32, name="warm")
        nc.vector.memset(warm[:, 0:1], 0.0)
        nc.scalar.activation(warm[:, 1:2], warm[:, 0:1], COPY)
        pool_warm = keep.tile([P, 1], BF16, name="pool_warm")
        nc.gpsimd.tensor_tensor(pool_warm[:], warm[:, 0:1], warm[:, 0:1], MULT)
        nc.vector.memset(w_scale_sb[:].bitcast(I32), 0)

        x_planes = xT.rearrange("(a p t) c -> a t p c", p=P, t=PACK)
        gate_sb = keep.tile([P, S], F32, name="gate_sb")
        gate_experts = 2 * BANK_SLOTS // C
        gate_columns = keep.tile([P, gate_experts], F32, name="gate_columns", tag="gate_columns", align_bytes=64)

        def load_plane(a, t):
            queue = nc.scalar if (a, t) == (0, 0) else nc.sync
            queue.dma_start(planes[a, t], x_planes[a, t])

        def load_gate(first_slot, end_slot):
            nc.sync.dma_start(gate_sb[:, first_slot:end_slot], gate[0:P, first_slot:end_slot])

        nc.sync.dma_start(offs_sb[:], offs)
        nc.sync.dma_start(pos1_sb[:], pos1)
        nc.sync.dma_start(pos2_sb[:], pos2)
        for t in range(PACK):
            load_plane(0, t)
            if t == 2:
                load_gate(S - FIRST_OWN, S)
        for t in range(PACK):
            load_plane(1, t)
            if t == 0:
                load_gate(0, S - FIRST_OWN)
            load_plane(2, t)
        for t in range(PACK):
            load_plane(4, t)
        with nc.allow_non_contiguous_dma(reason="one gate value a partition"):
            nc.sync.dma_start(gate_columns[:], gate[0:1, : gate_experts * C].rearrange("o (e c) -> c (o e)", c=C))
        for t in range(PACK):
            load_plane(3, t)

        bias = keep.tile([P, E], F32, name="bias")
        rows = w_scales.rearrange("e a q n -> q (e a) n").bitcast(I32)
        for quadrant in range(P // QUADRANT):
            nc.sync.dma_start(
                w_scale_sb[QUADRANT * quadrant : QUADRANT * quadrant + 4, :].bitcast(I32).rearrange("p (i n) -> p i n", n=N // 4),
                rows[4 * quadrant : 4 * quadrant + 4],
            )
        nc.sync.dma_start(bias[:], b)
        w_codes = []
        for a in range(PASSES):
            w_a = keep.tile([P, E, N * PACK], U8, name=f"w_{a}", align_bytes=64)
            nc.sync.dma_start(w_a[:].bitcast(I32), w_words[:, a].rearrange("e p n r -> p e (n r)").bitcast(I32))
            w_codes.append(w_a)

        y = keep.tile([P, S], F32, name="y")
        banks = [psum.tile([P, BANK_OF.count(i) * C], F32, name=f"bank_{i}") for i in range(max(BANK_OF) + 1)]
        woven = keep.tile([P, PACK * PLACES * C], BF16, name="woven", align_bytes=64)

        identity = keep.tile([P, P], F32, name="identity")
        make_identity(nc, identity[:])
        gate_ps = []
        for bank in range(gate_experts * C // BANK_SLOTS):
            gate_bank = psum.tile([P, BANK_SLOTS], F32, name=f"gate_ps_{bank}")
            for j in range(BANK_SLOTS // C):
                e = bank * BANK_SLOTS // C + j
                nc.tensor.transpose(gate_bank[:, slots(j, 1)], gate_columns[:, e : e + 1].to_broadcast([P, P]), identity[:])
            gate_ps.append(gate_bank)

        def raw(tag, counts, name):
            tile = keep.tile([P, PACK * sum(count + PAD for count in counts)], F32, name=name, tag=tag, align_bytes=64)
            ends = [PACK * sum(count + PAD for count in counts[: i + 1]) for i in range(len(counts))]
            return [tile[:, end - PACK * (count + PAD) : end] for count, end in zip(counts, ends)]

        def gather(engine, a, first_slot, count, values):
            offsets = offs_sb[:, list_columns(first_slot, count)]
            for t in range(PACK):
                target = values[:, t * (count + PAD) : t * (count + PAD) + count]
                if engine == "vector":
                    nc.vector.tensor_copy(target, windows[a, t].indirect(offsets))
                else:
                    nc.scalar.activation(target, windows[a, t].indirect(offsets), COPY)
            return first_slot, values.rearrange("p (t s) -> p t s", t=PACK)

        def words(a, first_slot, count):
            first = PLACE[a][first_slot // C] * C + first_slot % C
            return woven[:, PACK * first : PACK * (first + count)]

        def pool_weave(a, first_slot, count, chunk, first_plane=0, end_plane=PACK):
            start, values = chunk
            weight = gate_sb[:, first_slot : first_slot + count].rearrange("p (c i) -> p c i", i=LINE)
            nc.gpsimd.tensor_tensor(
                words(a, first_slot, count).rearrange("p (c i t) -> p c t i", t=PACK, i=LINE)[:, :, first_plane:end_plane, :],
                values[:, first_plane:end_plane, first_slot - start : first_slot - start + count].rearrange("p t (c i) -> p c t i", i=LINE),
                weight.unsqueeze(2).to_broadcast([P, count // LINE, end_plane - first_plane, LINE]),
                MULT,
            )

        def vector_weave(a, first_slot, count, chunk):
            start, values = chunk
            for bank in range(first_slot // BANK_SLOTS, (first_slot + count - 1) // BANK_SLOTS + 1):
                lo = max(first_slot, bank * BANK_SLOTS)
                size = min(first_slot + count, (bank + 1) * BANK_SLOTS) - lo
                weight = gate_ps[bank][:, lo - bank * BANK_SLOTS : lo - bank * BANK_SLOTS + size]
                weight = weight.rearrange("p (c i) -> p c i", i=RUN).unsqueeze(2).to_broadcast([P, size // RUN, PACK, RUN])
                nc.vector.tensor_tensor(
                    words(a, lo, size).rearrange("p (c i t) -> p c t i", t=PACK, i=RUN),
                    values[:, :, lo - start : lo - start + size].rearrange("p t (c i) -> p c t i", i=RUN),
                    weight,
                    MULT,
                )

        passes_left = [PASSES * BANK_OF.count(i) for i in range(len(banks))]

        def sums_of(e):
            return banks[BANK_OF[e]][:, slots(e - BANK_OF.index(BANK_OF[e]), 1)]

        def quantise_and_multiply(passes, place, count, scales, tag):
            codes = keep.tile([P, count * C], U32, name=f"codes_{tag}", tag=tag, align_bytes=64)
            nc.vector.quantize_mx(out=codes[:].bitcast(FP8X4), scales=scales, in_=woven[:, PACK * place * C : PACK * (place + count) * C])
            for j in range(count):
                a = [a for a in passes if place + j in PLACE[a]][0]
                e = PLACE[a].index(place + j)
                bank = BANK_OF[e]
                opens = passes_left[bank] == PASSES * BANK_OF.count(bank)
                passes_left[bank] = passes_left[bank] - 1
                scale_column = (e * PASSES + a) * N
                nc.tensor.matmul_mx(
                    out=sums_of(e),
                    lhsT=w_codes[a][:, e, :].bitcast(FP8X4),
                    lhsT_scale=w_scale_sb[:, scale_column : scale_column + N],
                    rhs=codes[:, slots(j, 1)].bitcast(FP8X4),
                    rhs_scale=scales[:, slots(j, 1)],
                    start=opens,
                    stop=(passes_left[bank] == 0),
                )

        def add_bias(e):
            nc.scalar.activation(y[:, slots(e, 1)], sums_of(e), IDENTITY, bias=bias[:, e : e + 1])

        raw_fed, raw_own = raw("raw_a", (S - FIRST_OWN, FIRST_OWN), "raw_0")
        fed_0 = gather("scalar", 0, 0, S - FIRST_OWN, raw_fed)
        own_0 = gather("vector", 0, S - FIRST_OWN, FIRST_OWN, raw_own)
        pass_1 = gather("vector", 1, 0, S, raw("raw_b", (S,), "raw_1")[0])
        pass_2 = gather("scalar", 2, 0, S, raw("raw_c", (S,), "raw_2")[0])
        own_4 = gather("vector", 4, S - LAST_OWN, LAST_OWN, raw("raw_d", (LAST_OWN,), "own_4")[0])

        for pair in ((0, 2), (2, 4)):
            pool_weave(0, S - FIRST_OWN, FIRST_OWN, own_0, *pair)
        pool_weave(0, 0, S - FIRST_OWN, fed_0)
        pool_weave(2, S - POOL_SHARE[2], POOL_SHARE[2], pass_2, 0, 2)
        pool_weave(1, S - POOL_SHARE[1], POOL_SHARE[1], pass_1)
        pool_weave(2, S - POOL_SHARE[2], POOL_SHARE[2], pass_2, 2, 4)
        pool_weave(4, S - LAST_OWN, LAST_OWN, own_4)
        vector_weave(1, 0, S - POOL_SHARE[1], pass_1)
        vector_weave(2, 0, S - POOL_SHARE[2], pass_2)

        pass_3 = gather("scalar", 3, 0, S, raw("raw_a", (S,), "raw_3")[0])
        tail = []
        end = S - LAST_OWN
        for count, values in zip(TAIL_CHUNKS, raw("raw_b", TAIL_CHUNKS, "raw_4")):
            first = end - count
            tail.append((first, count, gather("scalar", 4, first, count, values)))
            end = first

        first_scales = keep.tile([P, BLOCK_CALLS[0][1] * C], U8, name="first_scales", tag="gate_columns", align_bytes=64)
        scales = keep.tile([P, PLACES * C], U8, name="scales", tag="raw_d", align_bytes=64)
        block_tags = ("window_2_0", "window_2_1", "window_0_0", "window_2_2", "window_2_3")
        for call, (place, count) in enumerate(BLOCK_CALLS):
            plane = first_scales[:] if call == 0 else scales[:, slots(place, count)]
            quantise_and_multiply((0, 1, 2, 4), place, count, plane, block_tags[call])

        pool_weave(3, S - POOL_SHARE[3], POOL_SHARE[3], pass_3)
        vector_weave(3, 0, S - POOL_SHARE[3], pass_3)
        first, count, chunk = tail[0]
        vector_weave(4, first, count, chunk)
        free_scales = keep.tile([P, 2 * C], U8, name="free_scales", align_bytes=64)
        last_scales = keep.tile([P, 15 * C], U8, name="last_scales", tag="raw_a", align_bytes=64)
        quantise_and_multiply((3,), PLACE[3][0], 2, free_scales[:], "window_0_1")
        quantise_and_multiply((3,), PLACE[3][2], 8, last_scales[:, slots(0, 8)], "window_3_0")
        quantise_and_multiply((4,), PLACE[4][4], 3, last_scales[:, slots(8, 3)], "window_0_2")
        for e in (7, 8, 9, 4, 5, 6):
            add_bias(e)

        for first, count, chunk in tail[1:]:
            vector_weave(4, first, count, chunk)
        quantise_and_multiply((4,), PLACE[4][1], 3, last_scales[:, slots(11, 3)], "window_0_3")
        quantise_and_multiply((4,), PLACE[4][0], 1, last_scales[:, slots(14, 1)], "window_3_1")
        for e in (1, 2):
            add_bias(e)
        for e in (3, 0):
            nc.vector.tensor_scalar_add(y[:, slots(e, 1)], sums_of(e), bias[:, e : e + 1])

        picked = keep.tile([P, T], F32, name="picked", tag="raw_c", align_bytes=64)
        total = keep.tile([P, T], F32, name="total", tag="raw_b", align_bytes=64)

        def first_results(t0, count):
            return y[:].indirect(pos1_sb[:, list_columns(t0, count)])

        def add_second(t0, count):
            nc.vector.tensor_tensor(total[:, t0 : t0 + count], y[:].indirect(pos2_sb[:, list_columns(t0, count)]), picked[:, t0 : t0 + count], ADD)

        for t0, count in (FIRST_RUN,) + LATER_RUNS:
            nc.scalar.activation(picked[:, t0 : t0 + count], first_results(t0, count), COPY)
        t0, count = VECTOR_RUN
        nc.vector.tensor_copy(picked[:, t0 : t0 + count], first_results(t0, count))
        for t0, count in (FIRST_RUN, VECTOR_RUN):
            add_second(t0, count)
        nc.sync.dma_start(out[:, : t0 + count], total[:, : t0 + count])
        for t0, count in LATER_RUNS:
            add_second(t0, count)
            nc.sync.dma_start(out[:, t0 : t0 + count], total[:, t0 : t0 + count])
